import numpy as np, ml_dtypes
CORES = [8,136,40,168]
N = 4
BF = ml_dtypes.bfloat16
def f(rng, *shape):
    return (rng.standard_normal(shape, dtype=np.float32) * np.exp2(rng.integers(-2, 3, shape[:-1] + (1,)))).astype(BF)
def wide(rng, *shape):
    v = f(rng, *shape).astype(np.float32); k = shape[:-2] + (1, shape[-1])
    return (v * np.exp2(rng.integers(-6, 7, k)) * (rng.random(k) > 0.0625)).astype(BF)
S, U, HB, M, CAP, TH, RO = 2048, 2048, 512, 192, 32, 10, 3
def stand(rng):
    birth = np.arange(U)[None, :] // HB; pw = rng.choice(np.array([0.7, 1.0, 1.4]), (8, 1))
    any_ = np.minimum((N * rng.random((8, U)) ** pw).astype(np.int64), N - 1)
    w = np.where(rng.random((8, U)) < 0.4, (birth + rng.integers(0, N, (8, 1))) % N, any_)
    return np.where(rng.random((8, U)) < 0.04, -1, w)
def fair(rng):
    w = np.zeros((8, U), np.int64)
    for g in range(8):
        for e in range(2): w[g, e + 2 * rng.permutation(U // 2)] = np.arange(U // 2) // (HB // 2)
    return w
def lay(rng, w):
    b = np.full((N, 8, S), U, np.int64)
    for g in range(8):
        for r in range(N):
            u = np.flatnonzero(w[g] == r); b[r, g, rng.permutation(S)[:len(u)]] = u
    return b
def squares(b):
    at = np.full((8, U), -1, np.int64)
    for g in range(8):
        for r in range(N):
            s = np.flatnonzero(b[r, g] < U); at[g, b[r, g, s]] = s
    return at
def homes(rng):
    return np.array(np.argsort(rng.random((8, N, S)), axis=-1)[..., :HB]).reshape(8, U)
def trade(c, i, s):
    x, y = int(c[i]), int(c[s]); c[i] = y; c[s] = x
def put(c, u, s):
    trade(c, int(np.flatnonzero(c == u)[0]), s)
def rehome(hm, g, u, s):
    lo = u // HB * HB; i = np.flatnonzero(hm[g, lo:lo + HB] == s)
    if len(i): hm[g, lo + int(i[0])] = hm[g, u]
    hm[g, u] = s
def ranks(v):
    return np.array(np.broadcast_to(np.asarray(v).reshape(-1, 128, U), (N, 128, U)))
def pack(b, xs, ds, hm):
    h = np.asarray(hm).astype(np.int32)
    return {"board": b.astype(np.int32), "xs": ranks(xs).astype(BF), "ds": ranks(ds).astype(np.int32), "hm": np.stack([h] * N)}
def setup_inputs(rng):
    b = lay(rng, stand(rng))
    return pack(b, f(rng, N, 128, U), rng.integers(0, S, (N, 128, U)), homes(rng))
def setup_inputs_spread(rng):
    b = lay(rng, stand(rng)); v = np.minimum(np.exp2(np.log2(S) * rng.random((N, 128, U))).astype(np.int64), S - 1)
    return pack(b, wide(rng, N, 128, U), np.where(rng.random((N, 128, U)) < 0.5, v, S - v), homes(rng))
def setup_inputs_ends(rng):
    w = fair(rng); b = np.full((N, 8, S), U, np.int64); top = np.zeros(8, np.int64)
    ds = (S - 1) * rng.integers(0, 2, (8, 16, U)) * (rng.random((8, 1, U)) > 0.125); kind = rng.choice(np.array([0, 1, 2, 3]), (8, U), p=np.array([0.3, 0.35, 0.2, 0.15]))
    for g in range(8):
        for u, r in ((0, g % N), (U - 1, (N + g - 8) % N)):
            v = int(np.flatnonzero((w[g] == r) & (np.arange(U) % 2 == u % 2))[0]); w[g, v] = w[g, u]; w[g, u] = r
        for r in range(N):
            u = np.flatnonzero(w[g] == r); e = int(np.max(u[u % 2 == 0])); o = int(np.max(u[u % 2 == 1]))
            c = np.concatenate([np.array([0, S // 8 - 1]), 1 + rng.permutation(S // 8 - 2)[:HB // 6 - 1]])
            cells = (8 * c[:, None] + np.arange(8)[None, :]).reshape(-1); cells = cells[(cells > 0) & (cells < S - 2)]
            rest = rng.permutation(u[(u != e) & (u != o)])
            b[r, g, rng.permutation(cells)[:len(rest)]] = rest; b[r, g, 0] = e; b[r, g, S - 1] = o
            kind[g, e] = 0; kind[g, o] = 1
            if r == g % N: top[g] = e
            for v in (e, o): ds[g, :, v] = 0; ds[g, 15, v] = S - 1
    order = np.argsort(np.argsort(rng.random((8, 16, U)), axis=1), axis=1)
    xs = np.where(order < np.array([16, 0, TH, TH - 1])[kind][:, None, :], 2.0 ** 20, -2.0 ** 20)
    pool = np.concatenate([np.arange(HB // 2), S - HB // 2 + np.arange(HB // 2)])
    hm = np.stack([np.concatenate([rng.permutation(pool) for p in range(N)]) for g in range(8)])
    for g in range(8):
        e = int(top[g]); lo = e // HB * HB; i = lo + int(np.flatnonzero(hm[g, lo:lo + HB] == S - 1)[0])
        hm[g, i] = hm[g, e]; hm[g, e] = S - 1
    return pack(b, xs, ds, hm)
def setup_inputs_corners(rng):
    xs = f(rng, 128, U).astype(np.float32).reshape(8, 16, U); ds = rng.integers(0, S, (8, 16, U)); hm = homes(rng); w = fair(rng)
    ds = np.where(rng.random(ds.shape) < 0.1, rng.choice(np.array([0, 1, S - 1, S // 2]), ds.shape), ds)
    gp = rng.permutation(8); off = int(rng.integers(0, 6)); ev = 2 * np.arange(U // 2); K = M // N
    pats = ([0, M + 1, M - 1], [1, M, M + 1], [0, M, M - 1], [M + 1, 1, M])
    for i in range(8):
        g = int(gp[i]); w[g, ev] = -1
        if i < 4:
            for p in range(N):
                u = p * HB + 2 * rng.permutation(HB // 2); w[g, u[:N * K]] = np.repeat(np.arange(N), K)
        else:
            c = list(pats[i - 4]); c = c + [(U // 2 - sum(c)) // (N - 3)] * (N - 3)
            w[g, rng.permutation(ev)[:sum(c)]] = np.repeat(rng.permutation(N), c)
    b = lay(rng, w); at = squares(b)
    for i in range(8):
        g = int(gp[i])
        if i < 4:
            for r in range(N):
                vic = rng.permutation(np.flatnonzero((w[g] == r) & (np.arange(U) % 2 == 1))); used = 0
                e = ev[w[g, ev] == r]; xs[g][:, e] = -64.0
                for p in range(N):
                    n = (0, 1, CAP - 1, CAP, CAP + 1, K)[(r + 2 * p + i + off) % 6]
                    a = rng.permutation(e[e // HB == p])[:n]; v = vic[used:used + n]; used += n
                    xs[g][:, a] = 64.0; ds[g, 0, a] = (at[g, v] - at[g, a]) & (S - 1)
        else:
            for p in range(N):
                u = np.arange(p * HB, (p + 1) * HB); own = u[w[g, u] == p]; oth = u[w[g, u] != p]
                left = rng.permutation(np.setdiff1d(np.arange(S), at[g, own]))
                hm[g, own] = at[g, own]; hm[g, oth] = left[:len(oth)]
    return pack(b, xs, ds, hm)
def setup_inputs_crowd(rng):
    xs = f(rng, 128, U).astype(np.float32).reshape(8, 16, U); ds = rng.integers(0, S, (8, 16, U)); hm = homes(rng); w = fair(rng)
    gp = rng.permutation(8); off = int(rng.integers(0, 6)); ev = 2 * np.arange(U // 2); od = ev + 1; K = M // N
    ga, gb, gc = int(gp[0]), int(gp[1]), int(gp[2]); o = [int(v) for v in rng.permutation(N)]; r0, r1, rd = o[0], o[1], o[2]
    w[ga, ev] = -1
    for i in (0, 2):
        w[ga, ev[ev // HB == o[i + 1]]] = o[i]; w[ga, od[w[ga, od] == o[i + 1]]] = o[i]
    w[ga, U - 1] = o[0]
    w[gb, ev] = -1
    for p in range(N):
        u = p * HB + 2 * rng.permutation(HB // 2)[:N * K]; w[gb, u] = np.repeat(np.arange(N), K)
    w[gc, od[w[gc, od] == r0]] = r1; w[gc, ev[w[gc, ev] == r1]] = r0
    z = rd * HB + 1 + 2 * int(rng.integers(0, HB // 2)); w[gc, z] = rd; w[gc, 0] = rd
    b = lay(rng, w); put(b[rd, gc], z, 0); put(b[rd, gc], 0, S - 1)
    for i in range(3, 8):
        for r in range(N):
            c = b[r, int(gp[i])]; mode = (i + r + off) % 6; place = (0, S - 1, S - 1, 0, S - 1, 0)[mode]
            u = rng.permutation(c[c < U]); e = u[u % 2 == 0]; v = u[u % 2 == 1]
            if mode < 2: put(c, int(v[0]), place)
            else: trade(c, int(rng.choice(np.flatnonzero(c == U))), place)
            if place > 0: put(c, int(e[0]), 0); put(c, int(e[1]), 1)
    at = squares(b)
    for i in range(3, 8):
        g = int(gp[i])
        for r in range(N):
            c = b[r, g]; mode = (i + r + off) % 6; place = (0, S - 1, S - 1, 0, S - 1, 0)[mode]
            u = c[c < U]; e = u[u % 2 == 0]; vic = rng.permutation(u[u % 2 == 1]); emp = rng.permutation(np.flatnonzero(c == U))
            if mode < 2: vic = np.concatenate([c[place:place + 1], vic[vic != c[place]]])
            else: emp = np.concatenate([np.array([place]), emp[emp != place]])
            j = int(rng.integers(2, M))
            if mode < 2:
                xs[g][:, e] = 64.0; to = np.full(len(e), at[g, vic[0]])
                if mode == 1: to[j] = at[g, vic[1]]
            elif mode < 4:
                xs[g][:, e] = -64.0; to = np.full(len(e), emp[0])
                if mode == 3: to[j] = emp[1]
            else:
                xs[g][:, e] = 64.0; v = vic[:len(e)]; to = at[g, v]; back = np.full(len(e), emp[0])
                if mode == 5: back[j] = emp[1]
                ds[g, 0, v] = (back - to) & (S - 1)
            ds[g, 0, e] = (to - at[g, e]) & (S - 1)
    for i in (0, 2):
        c = b[o[i], ga]; u = c[c < U]; e = u[u % 2 == 0]; v = rng.permutation(u[u % 2 == 1])
        if i == 0: v = np.concatenate([np.array([U - 1]), v[v != U - 1]]); rehome(hm, ga, int(e[0]), S - 2)
        v = v[:len(e)]; xs[ga][:, e] = 64.0; ds[ga, 0, e] = (at[ga, v] - at[ga, e]) & (S - 1)
        if i == 2: xs[ga][:, int(e[int(rng.integers(0, M))])] = -64.0
    for r in range(N):
        c = b[r, gb]; s = np.flatnonzero((c < U) & (c % 2 == 0)); e = c[s]; v = rng.permutation(c[(c < U) & (c % 2 == 1)])[:len(e)]
        xs[gb][:, e] = 64.0; ds[gb, 0, e] = (at[gb, v] - s) & (S - 1)
        u = np.arange(r * HB, (r + 1) * HB); m = (u % 2 == 0) & (w[gb, u] >= 0)
        hm[gb, u[m]] = rng.permutation(s); hm[gb, u[~m]] = rng.permutation(np.setdiff1d(np.arange(S), s))[:HB - len(s)]
    c = b[r0, gc]; e = c[c < U]; xs[gc][:, ev] = -64.0
    ds[gc, 0, e] = (int(rng.choice(np.flatnonzero(c == U))) - at[gc, e]) & (S - 1)
    xs[gc][:, 0] = 64.0; xs[gc][:, z] = 128.0; ds[gc, :, 0] = 0; ds[gc, :, z] = S - 1; rehome(hm, gc, z, 0)
    return pack(b, xs, ds, hm)
def setup_inputs_heap(rng):
    w = np.tile(((np.arange(8) + int(rng.integers(0, N))) % N)[:, None], (1, U))
    xs = rng.integers(-2, 3, (N, 128, U)).astype(np.float32) * rng.choice(np.array([-1.0, 1.0], np.float32), (N, 128, U))
    return pack(lay(rng, w), xs, rng.integers(0, S, (N, 128, U)), homes(rng))
def check_inputs(d):
    bad = []
    for k, lo, hi in (("board", 0, U), ("ds", 0, S - 1), ("hm", 0, S - 1)):
        if np.min(d[k]) < lo or np.max(d[k]) > hi: bad.append("range of " + k)
    v = np.abs(np.asarray(d["xs"]).astype(np.float32))
    if not np.all((v == 0) | ((v >= 2.0 ** -100) & (v <= 2.0 ** 20))): bad.append("range of xs")
    b = np.asarray(d["board"]).astype(np.int64); h = np.asarray(d["hm"]).astype(np.int64)
    if not np.all(h == h[:1]): bad.append("ranks alike in hm")
    for g in range(8):
        v = b[:, g].reshape(-1); v = v[v != U]
        if len(np.unique(v)) != len(v): bad.append("units of board stand once (group " + str(g) + ")")
    for q in range(h.shape[0]):
        v = np.sort(h[q].reshape(8, N, HB), axis=-1)
        if np.any(v[..., 1:] == v[..., :-1]): bad.append("distinct homes in hm (rank " + str(q) + ")")
    return bad
def first_of(keys, ok):
    w = np.zeros(len(keys), bool); i = np.flatnonzero(ok); u, at = np.unique(keys[i], return_index=True); w[i[at]] = True
    return w
def reference(board, xs, ds, hm):
    bd = np.array(board).astype(np.int64)
    x = np.asarray(xs).astype(np.float32).reshape(N, 8, 16, U); d = np.asarray(ds).astype(np.int64).reshape(N, 8, 16, U); home = np.asarray(hm).astype(np.int64)
    for t in range(RO):
        new = np.array(bd); born = []
        for r in range(N):
            for g in range(8):
                c = bd[r, g]; X = x[r, g]; D = d[r, g]
                s = np.flatnonzero((c < U) & ((c & 1) == (t & 1)))[:M]; a = c[s]; n = len(a); j = np.arange(n)
                if n == 0: continue
                q = (s[None, :] + D[:, a]) & (S - 1)
                v = c[q]; more = np.add.reduce((X[:, a][:, None, :] > X[:, np.minimum(v, U - 1)]).astype(np.int64), axis=0)
                can = (v < U) & ((v & 1) != (t & 1)) & (more >= TH)
                claim = np.any(can, axis=0); sq = q[np.argmax(can, axis=0), j]
                won = first_of(sq, claim)
                at = np.where(won, sq, s); who = np.where(won, c[sq], a)
                w = (at[None, :] + D[:, np.minimum(who, U - 1)]) & (S - 1)
                free = c[w] == U; to = w[np.argmax(free, axis=0), j]
                go = first_of(to, np.any(free, axis=0) & (won | ~claim))
                new[r, g, s] = U; new[r, g, sq[won]] = U; new[r, g, np.where(go, to, at)] = a
                for p in range(N):
                    i = np.flatnonzero(won & (a // HB == p))[:CAP]
                    born.append((p, g, home[r, g, a[i]], c[sq[i]]))
        for p, g, h, b in born:
            e = new[p, g, h] == U; new[p, g, h[e]] = b[e]
        bd = new
    return {"y": bd.astype(np.float32)}

@@ -1,0 +1,619 @@
+from concourse.mybir import AluOpType as A, ActivationFunctionType as F
+
+TW, GW = 5184, 2496
+H0, BD0 = 2240, 4992
+BB = 16384.0
+SPLIT = True
+NB = 7
+TINY = 2.0 ** -110
+
+
+def _s(n, d):
+    return ("sbuf", [128, n], d)
+
+
+f32, bf, f16, i32, u16 = "float32", "bfloat16", "float16", "int32", "uint16"
+SCRATCH = {
+    "b16": _s(128, i32), "blk": _s(128, i32), "XS": _s(2080, bf), "DS": _s(2080, i32), "HM": _s(2080, i32),
+    "TB": _s(TW, bf), "XBe": _s(TW, f32), "XBo": _s(TW, f32), "WIN": _s(6912, f32), "MSG": _s(2880, f32), "RX": _s(384, f32),
+    "pI": _s(2, i32), "pJ": _s(2, i32), "col": _s(32, f32), "R": _s(16, f32), "colI": _s(192, bf), "J16": _s(208, bf),
+    "one": _s(128, bf), "BDt": _s(128, bf), "BD": _s(128, bf), "Tri": _s(128, bf), "Id": _s(128, bf), "Id16": _s(128, f16), "Idn": _s(128, bf),
+    "M1t": _s(128, bf), "M1": _s(128, bf), "BDn": _s(128, bf), "cm64": _s(128, bf), "c192": _s(128, bf),
+    "Z": _s(144 * 9, bf), "Zh": _s(144 * 3, f16), "BDv": _s(128 * 7, bf), "BDh": _s(384, f16), "H3": _s(128, f32), "TS": _s(2048, bf),
+    "HD1": _s(192, bf), "HD2": _s(192, bf), "HDa": _s(192, bf), "HDb": _s(192, bf), "PAT": _s(192, bf),
+    "jw": _s(12, f32), "K8": _s(8, f32), "K2": _s(12, f32), "K3": _s(12, f32), "PFi": _s(32, f32), "PF": _s(32, f32),
+    "ZR": _s(192, bf), "BIG": _s(192, f32), "sqw": _s(128, f32), "c65": _s(192, bf), "HOLD": _s(640, bf),
+    "x16": _s(128, i32), "fe16": _s(128, bf), "fo16": _s(128, bf), "o16": _s(128, f16), "IdK": _s(256, bf), "sq2": _s(128, f32), "mov": _s(128, bf), "offx": _s(256, u16),
+    "xb": _s(128, i32), "rows": _s(640, bf), "ti": _s(256, i32),
+    "Fw": _s(128, bf), "V0": _s(128, f32), "CE": _s(144, f32), "HS": _s(128, f32), "K16": _s(128, f16), "BDm": _s(128, bf),
+    "w8": _s(24, f32), "coff": _s(8, u16), "d0": _s(192, bf), "SB": _s(192, bf), "SH": _s(192, f32),
+    "swg": _s(12, u16), "swf": _s(12, f32), "swu": _s(36, u16), "srep": _s(192, f32), "acol": _s(192, bf), "acolA": _s(192, bf),
+    "arep": _s(192, u16), "aw": _s(12, u16), "qx": _s(192, i32), "q32": _s(192, i32), "qu": _s(192, u16), "q1": _s(192, f16),
+    "XA": _s(3072, bf), "XZ": _s(3072, bf), "CMP": _s(3072, bf), "sg": _s(192, bf), "sel": _s(192, f16), "fb": _s(192, f16),
+    "H": _s(200, f32), "keyr": _s(192, f16), "atr": _s(192, f32), "keyw": _s(12, f32), "atw": _s(12, u16),
+    "vcol": _s(192, bf), "vcf": _s(192, f32), "hcol": _s(192, f32), "whow": _s(12, u16),
+    "EQ": _s(192 * 13, bf), "AB": _s(640, bf), "EA": _s(640, bf), "G": _s(192, bf), "z": _s(192, f16), "posu": _s(12, u16),
+    "w12": _s(96, f32), "boff": _s(36, u16),
+    "H2": _s(192, f32), "endu": _s(36, u16), "RXh": _s(128, f16), "hwu": _s(8, u16), "hwh": _s(8, f16), "hg": _s(128, bf),
+    "roff": _s(24, u16), "vw": _s(8, u16), "xv": _s(128, f32), "yb": _s(128, f32),
+}
+for _k in range(8):
+    SCRATCH["P%d" % _k] = ("psum", [128, 512], f32)
+SEMAPHORES = ["v", "a", "p", "c", "b16", "blk", "xs", "ds", "hm", "tb", "pf", "out", "sent", "arr0", "arr1", "arr2"]
+
+
+def rank_program(g, core, T, topo):
+    rank = T.rank_of(core)
+    if rank is None:
+        return
+    Q = {"v": g.vector, "a": g.scalar, "p": g.tensor, "c": g, "s": g.sync}
+    cnt = {"v": 0, "a": 0, "p": 0, "c": 0}
+    seen, lastw, reads = {}, {}, {}
+    banks = ["P%d" % k for k in range(8)]
+
+    def wait(e, tok):
+        if seen.get((e, tok[0]), 0) < tok[1]:
+            seen[(e, tok[0])] = tok[1]
+            Q[e].wait_ge(T.sem[tok[0]], tok[1])
+
+    def deps(e, rd, wr, tok, free):
+        for k in rd + wr:
+            w = lastw.get(k)
+            if w and (w[0] != tok[0] or not free):
+                wait(e, w)
+            for r in reads.get(k, []):
+                if (k in wr and (r[0] != tok[0] or not free)) or (k in banks and r[0] != tok[0]):
+                    wait(e, r)
+        for k in wr:
+            lastw[k] = tok
+            reads[k] = []
+        for k in rd:
+            if k not in wr:
+                reads.setdefault(k, []).append(tok)
+
+    def op(e, fn, rd, wr, inc=True):
+        deps(e, rd, wr, (e, cnt[e] + 1), e == "p")
+        ins = fn()
+        if inc:
+            cnt[e] += 1
+            ins.then_inc(T.sem[e], 1)
+
+    def dma(e, out, in_, rd, wr, sem, total):
+        deps(e, rd, wr, (sem, total), True)
+        Q[e].dma_start(out, in_).then_inc(T.sem[sem], 16)
+
+    V, S = g.vector, g.scalar
+
+    def ts(out, in0, s1, s2, o0, o1, rd, wr):
+        if s2 is None:
+            op("v", lambda: V.tensor_scalar(out, in0, s1, None, o0), rd, wr)
+        else:
+            op("v", lambda: V.tensor_scalar(out, in0, s1, s2, o0, o1), rd, wr)
+
+    def tt(out, a, b, o, rd, wr):
+        op("v", lambda: V.tensor_tensor(out, a, b, o), rd, wr)
+
+    def cp(out, a, rd, wr):
+        op("v", lambda: V.tensor_copy(out, a), rd, wr)
+
+    def scan(out, a, b, ini, o0, o1, rd, wr):
+        op("v", lambda: V.tensor_tensor_scan(out, a, b, ini, o0, o1), rd, wr)
+
+    def ms(ap, c, wr):
+        op("v", lambda: V.memset(ap, c), [], wr)
+
+    def act(out, a, rd, wr, func=F.Identity, bias=0.0, scale=1.0):
+        op("a", lambda: S.activation(out, a, func, bias=bias, scale=scale), rd, wr)
+
+    def scaled(out, src, w, rd, wr):
+        act(out, src, rd, wr, F.Identity, 0.0, w)
+
+    def mm(out, l, r, start, stop, rd, wr, inc=None):
+        op("p", lambda: g.tensor.matmul(out, l, r, start, stop), rd, wr, stop if inc is None else inc)
+
+    def wrap(out, z, src, rd, wr, start=True, stop=True):
+        for i in range(16):
+            mm(out, z(i), src(i), start and i == 0, stop and i == 15, rd, wr, i == 15)
+
+    def iota(out, p, base, cm, wr, flag=True):
+        if flag:
+            op("c", lambda: g.iota(out, p, base, cm, allow_small_or_imprecise_dtypes=True), [], wr)
+        else:
+            op("c", lambda: g.iota(out, p, base, cm), [], wr)
+
+    def asel(out, a, p, o, fill, base, cm, rd, wr):
+        op("c", lambda: g.affine_select(out, a, p, o, fill, base, cm), rd, wr)
+
+    P = [T["P%d" % k] for k in range(8)]
+    pk = lambda k: "P%d" % k
+    col = lambda k: T.col[:, k:k + 1]
+    Rr = lambda k: T.R[:, k:k + 1]
+    (PM, C15, WU, WAE, WAO, WOCC, WY, WO2, WE0, WE1, WE2, MA, MV, OFF, OFF1, BSEL, I192, TMP, NOCC, OFFM, OFFA, OFS, OFS1, BS2) = range(24)
+    (Z1, ZU, ZOCC, ZFE, ZFO, ZY, ZE0, ZE1, ZE2) = range(9)
+    zt = lambda n: T.Z[:, 144 * n:144 * n + 144]
+    zw = lambda n: (lambda i: T.Z[:, 144 * n + 15 - i:144 * n + 143 - i])
+    zh = lambda n: (lambda i: T.Zh[:, 144 * n + 15 - i:144 * n + 143 - i])
+    bdv = lambda n: T.BDv[:, 128 * n:128 * n + 128]
+    XSk = ["XS", "XSa", "XSb"]
+
+    dma("s", T.blk[:], T.board[:], [], ["blk"], "blk", 16)
+    for k in range(8):
+        dma("s" if k < 4 else "a", T.b16[:, 16 * k:16 * k + 16], T.board[k, :], [], ["b16"], "b16", 128)
+    dma("a", T.XS[:, 0:2048], T.xs[:], [], ["XS"], "xs", 16)
+    dma("s", T.DS[0:64, 0:2048], T.ds[0:64, :], [], ["DS"], "ds", 32)
+
+    iota(T.pI[:, 0:1], [[0, 1]], 0, 1, ["pI"], False)
+    iota(T.colI[:], [[1, 192]], 0, 0, ["colI"])
+    ms(T.one[:], 1.0, ["one"])
+    asel(T.Id[:], T.one[:], [[-1, 128]], A.is_equal, 0.0, 0, 1, ["one"], ["Id"])
+    asel(T.BDt[:], T.one[:], [[-16, 8], [0, 16]], A.is_ge, 0.0, 0, 1, ["one"], ["BDt"])
+    asel(T.BD[:], T.BDt[:], [[16, 8], [0, 16]], A.is_ge, 0.0, 15, -1, ["BDt"], ["BD"])
+    iota(T.J16[:], [[0, 13], [1, 16]], 0, 0, ["J16"])
+    asel(T.Tri[:], T.BD[:], [[1, 128]], A.is_ge, 0.0, 0, -1, ["BD"], ["Tri"])
+    iota(T.jw[:], [[16, 12]], 2048, 0, ["jw"])
+    if SPLIT:
+        for k, (a, b) in enumerate(((32, 72), (104, 144), (160, 192))):
+            iota(T.XZ[:, 16 * a:16 * b], [[0, 16 * (b - a)]], 0, 0, ["XZ%d" % k])
+    ms(T.TB[:, 0:GW], 0.0, ["TB"])
+    scaled(T.cm64[:], T.colI[:, 0:128], -64.0, ["colI"], ["cm64"])
+    scaled(T.WIN[:, 0:192], T.colI[:], 0.0, ["colI"], ["WIN0"])
+    scaled(T.WIN[:, 2304:2496], T.colI[:], 0.0, ["colI"], ["WIN1"])
+    scaled(T.WIN[:, 4608:4800], T.colI[:], 0.0, ["colI"], ["WIN2"])
+    act(T.c192[:], T.colI[:, 0:128], ["colI"], ["c192"], F.Identity, 4096.0, 0.0)
+    scaled(T.ZR[:], T.colI[:], 0.0, ["colI"], ["ZR"])
+    for a, b, c in ((0, 32, 6.5), (32, 72, 0.0), (72, 104, 6.5), (104, 144, 0.0), (144, 160, 6.5), (160, 192, 0.0)):
+        act(T.c65[:, a:b], T.colI[:, a:b], ["colI"], ["c65%d" % a], F.Identity, c, 0.0)
+    act(T.Id16[:], T.Id[:], ["Id"], ["Id16"])
+    scaled(T.IdK[:, 0:128], T.Id[:], -4096.0, ["Id"], ["IdK0"])
+    scaled(T.IdK[:, 128:256], T.Id[:], 4096.0, ["Id"], ["IdK1"])
+    ts(T.pJ[:, 0:1], T.pI[:, 0:1], 15, None, A.bitwise_and, None, ["pI"], ["pJ0"])
+    ts(T.pJ[:, 1:2], T.pI[:, 0:1], 112, None, A.bitwise_and, None, ["pI"], ["pJ1"])
+    ms(T.CE[:, 0:16], 0.0, ["CE0"])
+    cp(col(PM), T.pJ[:, 0:1], ["pJ0"], ["PM"])
+    ts(col(C15), T.pJ[:, 1:2], 15.0, None, A.add, None, ["pJ1"], ["C15"])
+    ms(T.XS[:, 2048:2064], 1e9, ["XSa"])
+    ts(T.R[:], T.colI[:, 0:16], col(PM), None, A.is_equal, None, ["colI", "PM"], ["R"])
+    ts(zt(Z1), T.colI[:, 0:144], col(C15), None, A.is_equal, None, ["colI", "C15"], ["Z1"])
+    ms(T.XS[:, 2064:2080], -1e9, ["XSb"])
+    ts(col(TMP), Rr(0), 256.0, Rr(1), A.mult, A.add, ["R"], ["TMP"])
+    ts(col(WU), col(TMP), 2.0, Rr(8), A.mult, A.add, ["TMP", "R"], ["WU"])
+    ts(col(WAE), Rr(2), -2064.0, col(WU), A.mult, A.add, ["R", "WU"], ["WAE"])
+    ts(T.x16[:], T.b16[:], 2049, None, A.bitwise_and, None, ["b16"], ["x16"])
+    ts(T.xb[:], T.blk[:], 2049, None, A.bitwise_and, None, ["blk"], ["xb"])
+    ts(T.fe16[:], T.x16[:], 0.0, None, A.is_equal, None, ["x16"], ["fe16"])
+    mm(P[0][:, 0:128], T.fe16[:], T.Id[:], True, True, ["fe16", "Id"], ["P0"])
+    ts(T.rows[:, 256:384], T.xb[:], 0.0, None, A.is_equal, None, ["xb"], ["r2"])
+    ts(T.rows[:, 384:512], T.xb[:], 1.0, None, A.is_equal, None, ["xb"], ["r3"])
+    ts(T.HDa[:], T.J16[:, 0:192], col(PM), -4 * BB, A.is_equal, A.mult, ["J16", "PM"], ["HDa"])
+    ts(T.HDb[:], T.J16[:, 15:207], col(PM), BB, A.is_equal, A.mult, ["J16", "PM"], ["HDb"])
+    ts(T.ti[:, 0:128], T.blk[:], 9, 3, A.logical_shift_right, A.bitwise_and, ["blk"], ["ti0"])
+    ts(T.ti[:, 128:256], T.blk[:], 1, 255, A.logical_shift_right, A.bitwise_and, ["blk"], ["ti1"])
+    cp(T.o16[:], T.b16[:], ["b16"], ["o16"])
+    cp(T.rows[:, 0:256], T.ti[:], ["ti0", "ti1"], ["r01"])
+    for r, c0, k in ((2, 256, "r2"), (3, 384, "r3"), (8, 384, "r3"), (0, 0, "r01"), (1, 128, "r01")):
+        dma("s", T.TB[r:128:16, 0:2048], T.rows[:, c0:c0 + 128], [k], ["TB"], "tb", 80)
+    dma("s", T.DS[64:128, 0:2048], T.ds[64:128, :], [], ["DS"], "ds", 32)
+    ts(T.fo16[:], T.x16[:], 1.0, None, A.is_equal, None, ["x16"], ["fo16"])
+    ts(col(OFF), col(PM), 15.0, BB, A.not_equal, A.mult, ["PM"], ["OFF"])
+    act(T.K16[:], T.colI[:, 0:128], ["colI"], ["K16"], F.Identity, 2048.0, 2.0)
+    scaled(T.BDm[:], T.BD[:], -4096.0, ["BD"], ["BDm"])
+
+    def xb_build(tab, key, c0, b0, b1, ok, e="a"):
+        src = T.XS[:, 0:2080].indirect(T.offx[:, c0 + b0:c0 + b1])
+        if e == "a":
+            act(tab[:, 16 * b0:16 * b1], src, XSk + [ok], [key], F.Copy)
+        else:
+            cp(tab[:, 16 * b0:16 * b1], src, XSk + [ok], [key])
+
+    def xb_clear(tab, key, off, ok):
+        op("a", lambda: S.activation(tab[:].indirect(off), T.BIG[:], F.Silu), ["BIG", ok], [key])
+
+    ea0 = [0]
+    for b in range(NB, 11):
+        ea0.append(ea0[-1] + 176 - 16 * b)
+
+    def dedupe(kv, ka, kp, pd, w, wk, early, mid, late):
+        scan(T.H[:, 1:193], T.HD2[:], P[kv][:, 0:192], 2 * BB, A.add, A.max, ["HD2", pk(kv)], ["H"])
+        act(T.keyr[:], P[ka][:, 0:192], [pk(ka)], ["keyr"])
+        early()
+        ts(T.keyw[:], T.H[:, 16:193:16], col(OFF), None, A.subtract, None, ["H", "OFF"], ["keyw"])
+        for b in range(NB, 11):
+            act(T.AB[:, ea0[b - NB]:ea0[b - NB + 1]], P[ka][:, 16 * b + 16:192], [pk(ka), "keyw"], ["AB%d" % b], F.Abs, T.keyw[:, b:b + 1], -1.0)
+        if NB < 11:
+            act(T.EA[:, 0:ea0[-1]], T.AB[:, 0:ea0[-1]], ["AB%d" % b for b in range(NB, 11)], ["EA"], F.Relu, 1.0, -1.0)
+        late()
+        tt(T.EQ[:, 0:192], T.H[:, 0:192], P[kp][:, 0:192], A.is_equal, ["H", "H0", pk(kp)], ["EQ0"])
+        for b in range(NB):
+            ts(T.EQ[:, 208 * b + 208:192 * b + 384], T.keyr[:, 16 * b + 16:192], T.keyw[:, b:b + 1], None, A.is_equal, None, ["keyr", "keyw"], ["EQ%d" % (b + 1)])
+            mid(b)
+
+    def dup_mm(pd, w, wk, bs, stop=False):
+        for b in bs:
+            last = stop and b == bs[-1]
+            if b < 0:
+                mm(P[pd][:, 0:192], w, T.EQ[:, 0:192], False, last, [wk, "EQ0"], [pk(pd)])
+            elif b < NB:
+                mm(P[pd][:, 16 * b + 16:192], w, T.EQ[:, 208 * b + 208:192 * b + 384], False, last, [wk, "EQ%d" % (b + 1)], [pk(pd)])
+            else:
+                mm(P[pd][:, 16 * b + 16:192], w, T.EA[:, ea0[b - NB]:ea0[b - NB + 1]], False, last, [wk, "EA"], [pk(pd)])
+
+    w12 = lambda k: T.w12[:, 12 * k:12 * k + 12]
+    peers = [p for p in range(len(T.cores)) if p != rank]
+    peers = peers[rank % 3:] + peers[:rank % 3]
+    sent = [0]
+    XF, XFk = (T.XZ, ["XZ"]) if SPLIT else (T.XA, ["XA%d" % c for c in range(6)])
+    CMPk = ["CMP%d" % c for c in range(6)]
+    EFk = ["EF%d" % c for c in range(4)]
+
+    for t in range(3):
+        odd = t & 1
+        XB, XBk = (T.XBe, ["XBe"]) if odd else (T.XBo, ["XBo", "XBv"])
+        swu, boff, endu, roff = T.swu[:, 12 * t:12 * t + 12], T.boff[:, 12 * t:12 * t + 12], T.endu[:, 12 * t:12 * t + 12], T.roff[:, 8 * t:8 * t + 8]
+        sk, bk, ek, rk, wk, mk = ["%s%d" % (n, t) for n in ("swu", "boff", "endu", "roff", "WIN", "MSG")]
+        if t > 0:
+            wrap(P[0][:, 0:128], zw(ZFO if odd else ZFE), lambda i: T.TB[:, i:2048:16], ["TB", "Zf"], ["P0"])
+            tab, tk = (T.XBe, "XBe") if odd else (T.XBo, "XBo")
+            cp(tab[:].indirect(T.endu[:, 12 * t - 12:12 * t]), XF[:, 0:3072:16], XFk + ["endu%d" % (t - 1)], [tk])
+        act(T.Fw[:], P[0][:, 0:128], ["P0"], ["Fw"])
+        if t == 0:
+            scaled(T.Idn[:], T.Id[:], -1.0, ["Id"], ["Idn"])
+            act(T.sq2[:], T.colI[:, 0:128], ["colI", "PM"], ["sq2"], F.Identity, col(PM), 16.0)
+            for k in range(4):
+                act(T.HOLD[:, 160 * k:160 * k + 160], T.J16[:, 0:160], ["J16"], ["HOLD%d" % k], F.Sign)
+        mm(P[2][:, 0:128], T.BD[:], T.Fw[:], True, True, ["BD", "Fw"], ["P2"])
+        mm(P[6][:, 0:128], T.Id16[:], T.K16[:], True, False, ["Id16", "K16"], ["P6"])
+        mm(P[6][:, 0:128], T.BDm[:], T.Fw[:], False, True, ["BDm", "Fw"], ["P6"])
+        mm(P[1][:, 0:128], T.Id[:], T.cm64[:], True, False, ["Id", "cm64"], ["P1"])
+        mm(P[1][:, 0:128], T.Tri[:], T.Fw[:], False, True, ["Tri", "Fw"], ["P1"])
+        if t == 0:
+            mm(P[3][:, 0:192], T.Id[:], T.HDa[:], True, False, ["Id", "HDa"], ["P3"])
+            mm(P[3][:, 0:192], T.Id[:], T.HDb[:], False, True, ["Id", "HDb"], ["P3"])
+            act(T.HD2[:], P[3][:, 0:192], ["P3"], ["HD2"])
+        act(T.V0[:], P[1][:, 0:128], ["P1"], ["V0"], F.Identity, 0.5 + 32.5 / 16384, -1.0 / 16384)
+        if t == 0:
+            mm(P[7][:, 0:128], T.o16[:], T.Id16[:], True, False, ["o16", "Id16"], ["P7"])
+            mm(P[7][:, 0:128], T.fo16[:], T.IdK[:, 0:128], False, True, ["fo16", "IdK0"], ["P7"])
+        if t == 1:
+            scaled(T.Zh[:, 288:432], zt(Z1), col(WU), ["Z1", "WU"], ["Zh2"])
+            scaled(bdv(1), T.BD[:], col(WAO), ["BD", "WAO"], ["BD1"])
+            wrap(P[7][:, 0:8], zh(2), lambda i: T.RXh[:, i:128:16], ["Zh2", "RXh"], ["P7"])
+            xb_clear(T.XBo, "XBo", T.boff[:, 0:12], "boff0")
+        scan(T.CE[:, 16:144], P[2][:, 0:128], T.c192[:], 0.0, A.add, A.min, ["P2", "c192"], ["CE"])
+        if t == 0:
+            ts(T.offx[:, 0:128], P[7][:, 0:128], 4096.0, 2048.0, A.add, A.min, ["P7"], ["offo"])
+        tt(T.HS[:], T.CE[:, 15:143], P[6][:, 0:128], A.max, ["CE", "CE0", "P6"], ["HS"])
+        ts(T.d0[:], T.colI[:], T.CE[:, 143:144], 1.0 / 16384, A.is_equal, A.max, ["colI", "CE"], ["d0"])
+        scan(T.H3[:], T.HD2[:, 0:128], T.HS[:], 2 * BB, A.add, A.max, ["HD2", "HS"], ["H3"])
+        if t == 0:
+            scaled(bdv(3), T.BD[:], 256.0, ["BD"], ["BD3"])
+            scaled(bdv(0), T.BD[:], col(WAE), ["BD", "WAE"], ["BD0"])
+            scaled(T.BDn[:], T.BD[:], -2048.0, ["BD"], ["BDn"])
+            xb_build(T.XBo, "XBo", 0, 0, 48, "offo")
+            iota(T.PFi[:], [[2, 32]], H0 + 64 * rank, 0, ["PFi"])
+            asel(T.M1t[:], T.BDn[:], [[1, 128]], A.is_gt, 0.0, 0, -1, ["BDn"], ["M1t"])
+            asel(T.M1[:], T.M1t[:], [[1, 128]], A.not_equal, 2048.0, 0, -1, ["M1t"], ["M1"])
+            iota(T.HM[:], [[0, 2080]], 0, 0, ["HM"], False)
+            dma("s", T.HM[7:128:16, 0:2048], T.hm[:], [], ["HM"], "hm", 16)
+            iota(T.BIG[:], [[0, 192]], 8388608, 0, ["BIG"])
+            iota(T.TS[:], [[0, 2048]], 4096, 0, ["TS"])
+        ts(T.coff[:], T.H3[:, 15:128:16], col(OFF), None, A.subtract, None, ["H3", "OFF"], ["coff"])
+        cp(T.WIN[:, 2304 * t:2304 * t + 2304].indirect(T.coff[:]), T.V0[:], ["V0", "coff"], [wk])
+        scan(T.SB[:], T.d0[:], T.WIN[:, 2304 * t:2304 * t + 192], 0.5, A.add, A.max, ["d0", wk], ["SB"])
+        mm(P[3][:, 0:192], bdv(3), T.SB[:], True, True, ["BD3", "SB"], ["P3"])
+        mm(P[4][:, 0:192], bdv(3), T.SB[:], True, True, ["BD3", "SB"], ["P4"])
+        if t == 0:
+            ts(col(OFS), col(OFF), 2048.0, None, A.add, None, ["OFF"], ["OFS"])
+            ts(col(OFS1), col(OFF), 2047.0, None, A.add, None, ["OFF"], ["OFS1"])
+        if t == 1:
+            cp(T.vw[:], P[7][:, 0:8], ["P7"], ["vw"])
+        scan(T.SH[:], T.HD2[:], P[3][:, 0:192], 2 * BB, A.add, A.max, ["HD2", "P3"], ["SH"])
+        ts(T.swg[:], T.SH[:, 15:192:16], col(OFS), 2048.0, A.subtract, A.min, ["SH", "OFS"], ["swg"])
+        act(T.srep[:], P[4][:, 0:192], ["P4"], ["srep"], F.Identity, -2048.0)
+        if t == 0:
+            act(T.mov[:], T.sq2[:], ["sq2", "srep"], ["mov"], F.Sign, T.srep[:, 191:192], -1.0)
+            ts(col(WOCC), Rr(2), Rr(3), None, A.add, None, ["R"], ["WOCC"])
+            xb_build(T.XBo, "XBo", 0, 48, 96, "offo")
+            ts(T.K2[:], T.jw[:], col(PM), col(OFS), A.add, A.add, ["jw", "PM", "OFS"], ["K2"])
+            ts(col(OFFA), col(OFF), -2064.0, None, A.add, None, ["OFF"], ["OFFA"])
+            ms(T.DS[:, 2048:2080], 0, ["DSa"])
+        if t == 1:
+            act(T.xv[:], T.XS[:, 0:2080].indirect(T.vw[:]), XSk + ["vw"], ["xv"], F.Copy)
+        cp(T.acol[:], T.TB[:, 0:GW].indirect(T.swg[:]), ["TB", "swg"], ["acol"])
+        mm(P[5][:, 0:192], bdv(odd), T.acol[:], True, True, ["BD%d" % odd, "acol"], ["P5"])
+        if t == 0:
+            mm(P[7][:, 0:128], T.o16[:], T.Id16[:], True, False, ["o16", "Id16"], ["P7"])
+            mm(P[7][:, 0:128], T.fe16[:], T.IdK[:, 0:128], False, False, ["fe16", "IdK0"], ["P7"])
+            mm(P[7][:, 0:128], T.IdK[:, 128:256], T.mov[:], False, True, ["mov", "IdK1"], ["P7"])
+        tt(T.swf[:], T.SH[:, 15:192:16], T.K2[:], A.min, ["SH", "K2"], ["swf"])
+        if not SPLIT:
+            ts(T.arep[:], P[5][:, 0:192], 2064.0, None, A.add, None, ["P5"], ["arep"])
+        scan(T.H2[:], T.HD2[:], P[5][:, 0:192], 2 * BB, A.add, A.max, ["HD2", "P5"], ["H2"])
+        ts(T.aw[:], T.H2[:, 15:192:16], col(OFFA), None, A.subtract, None, ["H2", "OFFA"], ["aw"])
+        if SPLIT:
+            act(T.XZ[:, 0:3072:16], T.XS[:, 0:2080].indirect(T.aw[:]), XSk + ["aw", "XZ0", "XZ1", "XZ2"], ["XZ"], F.Copy)
+            if t == 0:
+                xb_build(T.XBo, "XBv", 0, 96, 128, "offo")
+        else:
+            for c in range(6):
+                act(T.XA[:, 512 * c:512 * c + 512], T.XS[:, 0:2080].indirect(T.arep[:, 32 * c:32 * c + 32]), XSk + ["arep"], ["XA%d" % c], F.Copy)
+        if t == 0:
+            ts(col(BSEL), col(PM), -2048.0, -2048.0, A.mult, A.add, ["PM"], ["BSEL"])
+            ts(col(MA), Rr(0), Rr(1), Rr(8), A.add, A.add, ["R"], ["MA"])
+            ts(T.PAT[:], T.J16[:, 15:207], col(PM), BB, A.not_equal, A.mult, ["J16", "PM"], ["PAT"])
+            ts(T.offx[:, 128:256], P[7][:, 0:128], 8192.0, 2048.0, A.add, A.min, ["P7"], ["offe"])
+        tt(T.qx[:], T.DS[:].indirect(T.aw[:]), T.srep[:], A.add, ["DS", "DSa", "aw", "srep"], ["qx"])
+        ts(T.q32[:], T.qx[:], 2047, None, A.bitwise_and, None, ["qx"], ["q32"])
+        cp(T.qu[:], T.q32[:], ["q32"], ["qu"])
+        if t == 0 and not SPLIT:
+            xb_build(T.XBo, "XBv", 0, 96, 128, "offo", "v")
+
+        def extra():
+            ts(T.q1[:], T.qu[:], 1.0, None, A.add, None, ["qu"], ["q1"])
+            ts(swu, T.swf[:], col(OFS), None, A.subtract, None, ["swf", "OFS"], [sk])
+
+        def cmpv(a, b, c, xk):
+            tt(T.CMP[:, 16 * a:16 * b], XB[:, 0:2048].indirect(T.qu[:, a:b]), T.XA[:, 16 * a:16 * b], A.is_lt, XBk + ["qu", xk], [CMPk[c]])
+
+        def count(bank, a, b, ks):
+            wrap(P[bank][:, a:b], zw(Z1), lambda i: T.CMP[:, 16 * a + i:16 * b:16], ["Z1"] + ks, [pk(bank)], not SPLIT, True)
+
+        def choose(a, b, bc, bs, bf_, n, before=None):
+            mm(P[bs][:, a:b], T.Id16[:], T.q1[:, a:b], True, False, ["Id16", "q1"], [pk(bs)])
+            mm(P[bf_][:, a:b], bdv(3), T.SB[:, a:b], True, False, ["BD3", "SB"], [pk(bf_)])
+            if before:
+                before()
+            act(T.sg[:, a:b], P[bc][:, a:b], [pk(bc)], ["sg%d" % n], F.Sign, -9.5)
+            mm(P[bs][:, a:b], T.M1[:], T.sg[:, a:b], False, True, ["M1", "sg%d" % n], [pk(bs)])
+            mm(P[bf_][:, a:b], bdv(4), T.sg[:, a:b], False, True, ["BD4", "sg%d" % n], [pk(bf_)])
+            act(T.sel[:, a:b], P[bs][:, a:b], [pk(bs), "BSEL"], ["sel%d" % n], F.Relu, col(BSEL))
+            act(T.fb[:, a:b], P[bf_][:, a:b], [pk(bf_)], ["fb%d" % n], F.Relu, -2047.0 - 65536.0)
+
+        def keys(a, b, n, ks):
+            for k in ks:
+                if k == 3:
+                    mm(P[k][:, a:b], T.Id[:], T.PAT[:, a:b], True, False, ["Id", "PAT"], [pk(k)])
+                mm(P[k][:, a:b], T.BDh[:, 0:128], T.sel[:, a:b], k != 3, False, ["sel%d" % n, "BDh0"], [pk(k)])
+                mm(P[k][:, a:b], T.BDh[:, 128:256], T.fb[:, a:b], False, True, ["fb%d" % n, "BDh1"], [pk(k)])
+
+        def act_consts():
+            if t == 0:
+                scaled(bdv(4), T.BD[:], -4096.0, ["BD"], ["BD4"])
+                scaled(T.BDh[:, 0:128], T.BD[:], 1.0, ["BD"], ["BDh0"])
+                scaled(T.BDh[:, 128:256], T.BD[:], 0.0625, ["BD"], ["BDh1"])
+            act(T.acolA[:], T.acol[:], ["acol", "MA", "R"], ["acolA"], F.Identity, Rr(4 + t), col(MA))
+            if t == 0:
+                xb_build(T.XBe, "XBe", 128, 0, 10, "offe")
+
+        if SPLIT:
+            cut = 144
+
+            def pre(bank, a, b):
+                for i in range(16):
+                    mm(P[bank][:, i:16 * (b - a):16], T.Id[:], T.XZ[:, 16 * a:16 * b:16], i == 0, False, ["Id", "XZ"], [pk(bank)])
+
+            def gat(bank, a, b, c):
+                act(T.XA[:, 16 * a:16 * b], XB[:, 0:2048].indirect(T.qu[:, a:b]), XBk + ["qu"], ["XA%d" % c], F.Copy)
+
+            def dif(bank, a, b, c):
+                mm(P[bank][:, 0:16 * (b - a)], T.Idn[:], T.XA[:, 16 * a:16 * b], False, True, ["Idn", "XA%d" % c], [pk(bank)])
+
+            def sgn(bank, a, b, c):
+                act(T.CMP[:, 16 * a:16 * b], P[bank][:, 0:16 * (b - a)], [pk(bank)], [CMPk[c]], F.Sign, -TINY)
+
+            def spread(a, b, c):
+                scan(T.XA[:, 16 * a:16 * b], T.HOLD[:, 0:16 * (b - a)], T.XZ[:, 16 * a:16 * b], 0.0, A.mult, A.add, ["HOLD3", "XZ"], ["XA%d" % c])
+
+            pre(0, 0, 32)
+            gat(0, 0, 32, 3)
+            spread(32, 72, 0)
+            spread(104, 144, 1)
+            pre(1, 72, 104)
+            gat(1, 72, 104, 4)
+            dif(0, 0, 32, 3)
+            cmpv(32, 72, 0, "XA0")
+            pre(2, 144, 160)
+            dif(1, 72, 104, 4)
+            sgn(0, 0, 32, 3)
+            gat(2, 144, 160, 5)
+            spread(160, 192, 2)
+            mm(P[6][:, 0:144], T.Id[:], T.c65[:, 0:144], True, False, ["Id", "c65160"], ["P6"])
+            mm(P[4][:, 144:192], T.Id[:], T.c65[:, 144:192], True, False, ["Id", "c65160"], ["P4"])
+            for i in range(16):
+                mm(P[6][:, 0:72], zw(Z1)(i), T.CMP[:, i:1152:16], False, False, ["Z1", CMPk[0], CMPk[3]], ["P6"])
+            dif(2, 144, 160, 5)
+            sgn(1, 72, 104, 4)
+            cmpv(104, 144, 1, "XA1")
+            extra()
+            sgn(2, 144, 160, 5)
+            count(6, 72, 144, [CMPk[1], CMPk[4]])
+            act_consts()
+            cmpv(160, 192, 2, "XA2")
+            choose(0, cut, 6, 5, 0, 0)
+            choose(cut, 192, 4, 1, 2, 1, lambda: (count(4, cut, 192, [CMPk[2], CMPk[5]]), keys(0, cut, 0, [7])))
+            keys(cut, 192, 1, [7])
+            keys(0, cut, 0, [3])
+            keys(cut, 192, 1, [3])
+        else:
+            cut = 128
+            for c in range(6):
+                cmpv(32 * c, 32 * c + 32, c, "XA%d" % c)
+                if c == 0:
+                    extra()
+                if c in (1, 3):
+                    count(6, 32 * c - 32, 32 * c + 32, CMPk[c - 1:c + 1])
+                if c == 3:
+                    act_consts()
+                    choose(0, cut, 6, 5, 0, 0)
+            keys(0, cut, 0, [7, 3])
+            choose(cut, 192, 4, 1, 6, 1, lambda: count(4, cut, 192, CMPk[4:6]))
+            keys(cut, 192, 1, [7, 3])
+        cp(T.TB[:].indirect(swu), T.acolA[:], ["acolA", sk], ["TB"])
+        if t == 0:
+            ms(T.H[:, 0:1], 3 * BB, ["H0"])
+            ts(col(OFF1), col(OFF), 1.0, None, A.add, None, ["OFF"], ["OFF1"])
+            ts(col(MV), col(MA), col(WOCC), None, A.add, None, ["MA", "WOCC"], ["MV"])
+            ts(zt(ZU), zt(Z1), col(WU), None, A.mult, None, ["Z1", "WU"], ["ZU"])
+            ts(col(I192), col(PM), 192.0, None, A.mult, None, ["PM"], ["I192"])
+            ts(col(WE0), Rr(4), col(WOCC), None, A.add, None, ["R", "WOCC"], ["WE0"])
+        if t == 1:
+            cp(T.XBo[:].indirect(T.roff[:, 0:8]), T.xv[:], ["xv", "roff0"], ["XBo"])
+        if t == 2:
+            cp(T.hcol[:], T.HM[:].indirect(T.aw[:]), ["HM", "aw"], ["hcol"])
+        sf = ["fb0", "fb1", "BDh0"]
+
+        def early1():
+            ts(T.atw[:], T.H[:, 16:193:16], col(OFF1), 2048.0, A.subtract, A.min, ["H", "OFF1"], ["atw"])
+            cp(T.vcol[:], T.TB[:, 0:GW].indirect(T.atw[:]), ["TB", "atw"], ["vcol"])
+            wrap(P[0][:, 0:12], zw(ZU), lambda i: T.vcol[:, i:192:16], ["ZU", "vcol"], ["P0"])
+            act(T.atr[:], P[7][:, 0:192], ["P7"], ["atr"], F.Identity, -1.0)
+            if t == 0:
+                scaled(bdv(2), T.BD[:], Rr(0), ["BD", "R"], ["BD2"])
+                scaled(T.PF[:], T.PFi[:], Rr(7), ["PFi", "R"], ["PF"])
+                for k in range(12):
+                    c0 = 960 * (k // 4) + 192 * (k % 4)
+                    dma("s", T.MSG[:, c0:c0 + 32], T.PF[:], ["PF"], ["MSG%d" % (k // 4)], "pf", 192)
+            mm(P[1][:, 0:192], bdv(2), T.acol[:], True, False, ["BD2", "acol"], ["P1"])
+            mm(P[1][:, 0:192], T.BDh[:, 0:128], T.fb[:], False, False, sf, ["P1"])
+
+        def late1():
+            act(T.vcf[:], T.vcol[:], ["vcol", "MV"], ["vcf"], F.Identity, 0.0, col(MV))
+            if t == 0:
+                xb_build(T.XBe, "XBe", 128, 24, 44, "offe")
+
+        lk = (0, 64, 128, 144, 192)
+
+        def look(c, e):
+            src = T.TB[:, 0:GW].indirect(T.qu[:, lk[c]:lk[c + 1]])
+            if e == "a":
+                act(T.CMP[:, 16 * lk[c]:16 * lk[c + 1]], src, ["TB", "qu", "WE%d" % t], [EFk[c]], F.Identity, 0.0, col(WE0 + t))
+            else:
+                ts(T.CMP[:, 16 * lk[c]:16 * lk[c + 1]], src, col(WE0 + t), None, A.mult, None, ["TB", "qu", "WE%d" % t], [EFk[c]])
+
+        def mid1(b):
+            if b == NB - 2:
+                cp(T.whow[:], P[0][:, 0:12], ["P0"], ["whow"])
+            dup_mm(1, bdv(3), "BD3", [-1, 0] if b == 0 else [b])
+
+        dedupe(7, 7, 3, 1, None, None, early1, mid1, late1)
+        dup_mm(1, bdv(3), "BD3", list(range(NB, 11)), True)
+        tt(T.qx[:], T.DS[:].indirect(T.whow[:]), T.atr[:], A.add, ["DS", "DSa", "whow", "atr"], ["qx"])
+        ts(T.q32[:], T.qx[:], 2047, None, A.bitwise_and, None, ["qx"], ["q32"])
+        cp(T.qu[:], T.q32[:], ["q32"], ["qu"])
+        for c in range(3):
+            look(c, "a")
+        ts(T.G[:], P[1][:, 0:192], 4.0, col(PM), A.min, A.is_equal, ["P1", "PM"], ["G"])
+        ts(T.q1[:], T.qu[:], 1.0, None, A.add, None, ["qu"], ["q1"])
+        scan(P[4][:, 0:192], T.G[:], T.G[:], col(I192), A.add, A.max, ["G", "I192"], ["P4"])
+        ts(w12(2), T.swf[:], col(OFS1), None, A.subtract, None, ["swf", "OFS1"], ["s1"])
+        tt(T.z[:], P[4][:, 0:192], T.G[:], A.mult, ["P4", "G"], ["z"])
+        mm(P[5][:, 0:192], T.BDh[:, 0:128], T.z[:], True, True, ["BDh0", "z"], ["P5"])
+        if t < 2:
+            cp(T.hcol[:], T.HM[:].indirect(T.aw[:]), ["HM", "aw"], ["hcol"])
+        if t == 0:
+            ts(T.K3[:], T.jw[:], col(PM), float(BD0 + 1 - 2048), A.add, A.add, ["jw", "PM"], ["K3"])
+        tt(w12(1), T.keyw[:], T.K3[:], A.subtract, ["keyw", "K3"], ["w1"])
+        tt(w12(4), T.keyw[:], w12(2), A.subtract, ["keyw", "s1"], ["w4"])
+        scan(T.H2[:], T.HD2[:], P[5][:, 0:192], 2 * BB, A.add, A.max, ["HD2", "P5"], ["H2"])
+        ts(T.posu[:], T.H2[:, 15:192:16], col(OFF1), None, A.subtract, None, ["H2", "OFF1"], ["posu"])
+        ts(w12(0), T.H2[:, 15:192:16], col(OFF), 768.0, A.subtract, A.is_le, ["H2", "OFF"], ["won"])
+        op("v", lambda: V.tensor_tensor(T.MSG[:, 960 * t:960 * t + 960].indirect(T.posu[:]), T.vcf[:], T.hcol[:], A.add), ["vcf", "hcol", "posu"], [mk])
+        wait("c", lastw[mk])
+        for p in peers:
+            dst = T.cores[p]
+            rid, pid = topo.addr(dst, core)
+            g.remote_dma(T.RX[:, 128 * t + 32 * rank:128 * t + 32 * rank + 32], T.MSG[:, 960 * t + 192 * p:960 * t + 192 * p + 32],
+                         T.sem["arr%d" % t], T.sem.sent, pid, rid, topo.mask(core, dst))
+            sent[0] += len(topo.engines(core, dst))
+        if t == 0:
+            asel(T.TS[:], T.TS[:], [[-1, 16], [0, 8], [1, 16]], A.is_ge, 0.0, 0, 0, ["TS"], ["TS"])
+            asel(T.TS[:], T.TS[:], [[-1, 16], [0, 8], [1, 16]], A.not_equal, -4096.0, 0, 0, ["TS"], ["TS"])
+            asel(T.TS[:], T.TS[:], [[0, 16], [-16, 8], [0, 16]], A.is_ge, 0.0, 0, 1, ["TS"], ["TS"])
+            asel(T.TS[:], T.TS[:], [[0, 16], [16, 8], [0, 16]], A.is_ge, 0.0, 15, -1, ["TS"], ["TS"])
+        look(3, "v")
+        mm(P[6][:, 0:192], T.Id16[:], T.q1[:], True, False, ["Id16", "q1"], ["P6"])
+        for a, b, ks in ((0, 64, EFk[0:1]), (64, 128, EFk[1:2]), (128, 192, EFk[2:4])):
+            if t == 0:
+                wrap(P[0][:, a:b], zw(Z1), lambda i: T.CMP[:, 16 * a + i:16 * b:16], ["Z1"] + ks, ["P0"])
+            else:
+                wrap(P[6][:, a:b], lambda i: T.TS[:, 128 * i:128 * i + 128], lambda i: T.CMP[:, 16 * a + i:16 * b:16], ["TS"] + ks, ["P6"], False, b == 192)
+        tt(w12(3), w12(1), w12(0), A.mult, ["w1", "won"], ["w3"])
+        tt(w12(6), w12(4), w12(0), A.mult, ["w4", "won"], ["w6"])
+        tt(w12(5), w12(3), T.K3[:], A.add, ["w3", "K3"], ["w5"])
+        tt(w12(7), w12(6), w12(2), A.add, ["w6", "s1"], ["stay"])
+        ts(boff, w12(5), -1.0, None, A.add, None, ["w5"], [bk])
+        cp(T.TB[:].indirect(boff), T.ZR[:], ["ZR", bk], ["TB"])
+        c0 = 128 * t + 32 * rank
+        act(T.RX[:, c0:c0 + 32], T.MSG[:, 960 * t + 192 * rank:960 * t + 192 * rank + 32], [mk], ["RX%d" % t])
+        if t == 0:
+            scaled(T.BDh[:, 256:384], T.BD[:], Rr(7), ["BD", "R"], ["BDh2"])
+            xb_build(T.XBe, "XBe", 128, 10, 24, "offe")
+        if t == 0:
+            act(T.sg[:], P[0][:, 0:192], ["P0"], ["sg0", "sg1"], F.Identity, 1.0, -2.0)
+            mm(P[6][:, 0:192], T.M1[:], T.sg[:], False, True, ["M1", "sg0", "sg1"], ["P6"])
+            act(T.sel[:], P[6][:, 0:192], ["P6", "BSEL"], ["sel0", "sel1"], F.Relu, col(BSEL))
+        else:
+            act(T.sel[:], P[6][:, 0:192], ["P6", "BS2"], ["sel0", "sel1"], F.Relu, col(BS2))
+        mm(P[4][:, 0:192], T.Id[:], T.PAT[:], True, False, ["Id", "PAT"], ["P4"])
+        for k in (1, 4):
+            mm(P[k][:, 0:192], T.BDh[:, 0:128], T.sel[:], k != 4, True, ["sel0", "sel1", "BDh0"], [pk(k)])
+        if t == 0:
+            ts(col(WO2), col(WOCC), float(GW), None, A.mult, None, ["WOCC"], ["WO2"])
+            ts(col(NOCC), col(WOCC), -1.0, None, A.mult, None, ["WOCC"], ["NOCC"])
+            ts(col(OFFM), col(OFF), -1.0, None, A.add, None, ["OFF"], ["OFFM"])
+
+        def early2():
+            if t == 0:
+                scaled(bdv(5), T.BD[:], col(NOCC), ["BD", "NOCC"], ["BD5"])
+            mm(P[5][:, 0:192], bdv(5), T.acol[:], True, False, ["BD5", "acol"], ["P5"])
+            wait("a", ("arr%d" % t, sum(len(topo.engines(T.cores[p], core)) for p in peers)))
+            act(T.RXh[:], T.RX[:, 128 * t:128 * t + 128], ["RX%d" % t], ["RXh"])
+
+        def late2():
+            if t == 0:
+                scaled(bdv(6), T.BD[:], col(WO2), ["BD", "WO2"], ["BD6"])
+
+        def mid2(b):
+            dup_mm(5, T.BD[:], "BD", [-1, 0] if b == 0 else [b])
+            if b == 2:
+                mm(P[2][:, 0:128], T.BDh[:, 256:384], T.RXh[:], True, True, ["BDh2", "RXh"], ["P2"])
+                mm(P[7][:, 0:128], T.BDh[:, 256:384], T.RXh[:], True, False, ["BDh2", "RXh"], ["P7"])
+
+        dedupe(1, 1, 4, 5, None, None, early2, mid2, late2)
+        ts(T.EQ[:, 2304:2496], T.keyr[:], 0.0, None, A.is_equal, None, ["keyr"], ["EQ12"])
+        dup_mm(5, T.BD[:], "BD", list(range(NB, 11)))
+        mm(P[5][:, 0:192], T.BD[:], T.EQ[:, 2304:2496], False, True, ["BD", "EQ12"], ["P5"])
+        scan(T.H3[:], T.HD2[:, 0:128], P[2][:, 0:128], 2 * BB, A.add, A.max, ["HD2", "P2"], ["H3"])
+        tt(w12(1), T.keyw[:], w12(7), A.subtract, ["keyw", "stay"], ["w1"])
+        ts(T.hwu[:], T.H3[:, 15:128:16], col(OFF), None, A.subtract, None, ["H3", "OFF"], ["hwu"])
+        act(T.hg[:], T.TB[:, 0:GW].indirect(T.hwu[:]), ["TB", "hwu"], ["hg"], F.Copy)
+        mm(P[7][:, 0:128], bdv(6), T.hg[:], False, True, ["BD6", "hg"], ["P7"])
+        if t == 0:
+            ts(col(WAO), Rr(3), -2064.0, col(WU), A.mult, A.add, ["R", "WU"], ["WAO"])
+            scaled(zt(ZFO), zt(Z1), Rr(3), ["Z1", "R"], ["Zf"])
+            xb_build(T.XBe, "XBe", 128, 44, 128, "offe")
+        scan(T.H2[:], T.HD2[:], P[5][:, 0:192], 2 * BB, A.add, A.max, ["HD2", "P5"], ["H2"])
+        ts(w12(3), T.H2[:, 15:192:16], col(OFFM), None, A.is_equal, None, ["H2", "OFFM"], ["w3"])
+        tt(w12(4), w12(3), w12(1), A.mult, ["w3", "w1"], ["w4"])
+        scan(T.H3[:], T.HD2[:, 0:128], P[7][:, 0:128], 2 * BB, A.add, A.max, ["HD2", "P7"], ["H3"])
+        tt(w12(5), w12(4), w12(7), A.add, ["w4", "stay"], ["w5"])
+        ts(roff, T.H3[:, 15:128:16], col(OFF), None, A.subtract, None, ["H3", "OFF"], [rk])
+        ts(endu, w12(5), -1.0, None, A.add, None, ["w5"], [ek])
+        cp(T.TB[:].indirect(roff), T.RX[:, 128 * t:128 * t + 128], ["RX%d" % t, "RXh", rk], ["TB"])
+        cp(T.TB[:].indirect(endu), T.acol[:], ["acol", ek], ["TB"])
+        if t == 0:
+            ts(col(BS2), col(PM), -4096.0, None, A.mult, None, ["PM"], ["BS2"])
+            ts(col(WE1), Rr(5), col(WOCC), None, A.add, None, ["R", "WOCC"], ["WE1"])
+            ts(col(WE2), Rr(6), col(WOCC), None, A.add, None, ["R", "WOCC"], ["WE2"])
+            ts(col(WY), col(WOCC), -2048.0, col(WU), A.mult, A.add, ["WOCC", "WU"], ["WY"])
+        if t == 1:
+            scaled(zt(ZFE), zt(Z1), Rr(2), ["Z1", "R"], ["Zf"])
+            xb_clear(T.XBo, "XBo", T.endu[:, 0:12], "endu0")
+            xb_clear(T.XBo, "XBo", swu, sk)
+            scaled(zt(ZY), zt(Z1), col(WY), ["Z1", "WY"], ["ZY"])
+
+    wrap(P[0][:, 0:128], zw(ZY), lambda i: T.TB[:, 128 * i:128 * i + 128], ["ZY", "TB"], ["P0"])
+    ts(T.yb[:], P[0][:, 0:128], 2048.0, 2048.0, A.add, A.min, ["P0"], ["yb"])
+    dma("s", T.y[:], T.yb[:], ["yb"], ["y"], "out", 16)
+    for k, n in (("v", cnt["v"]), ("a", cnt["a"]), ("p", cnt["p"]), ("c", cnt["c"]), ("sent", sent[0]), ("b16", 128), ("blk", 16), ("xs", 16),
+                 ("ds", 32), ("hm", 16), ("tb", 80), ("pf", 192), ("out", 16)):
+        wait("c", (k, n))

@@ -1,11 +1,13 @@
 from concourse.mybir import AluOpType as A, ActivationFunctionType as F
 
-TW, GW = 5184, 2496
-H0, BD0 = 2240, 4992
+D0, H0, GW = 2064, 2304, 2432
+BD0, TW = 2 * GW, 2 * GW + 192
 BB = 16384.0
-SPLIT = True
-NB = 7
+NB = (11, 8)
 TINY = 2.0 ** -110
+LOOKS = ((0, 32, "a"), (32, 64, "v"), (64, 96, "a"), (96, 128, "a"), (128, 160, "v"), (160, 192, "a"))
+CYC, PEC, WAKE, GAT, SCA = 0.00087, 0.0005, 0.18, 1.5, 3.5
+PASSES = 8
 
 
 def _s(n, d):
@@ -14,32 +16,67 @@ def _s(n, d):
 
 f32, bf, f16, i32, u16 = "float32", "bfloat16", "float16", "int32", "uint16"
 SCRATCH = {
-    "b16": _s(128, i32), "blk": _s(128, i32), "XS": _s(2080, bf), "DS": _s(2080, i32), "HM": _s(2080, i32),
-    "TB": _s(TW, bf), "XBe": _s(TW, f32), "XBo": _s(TW, f32), "WIN": _s(6912, f32), "MSG": _s(2880, f32), "RX": _s(384, f32),
-    "pI": _s(2, i32), "pJ": _s(2, i32), "col": _s(32, f32), "R": _s(16, f32), "colI": _s(192, bf), "J16": _s(208, bf),
-    "one": _s(128, bf), "BDt": _s(128, bf), "BD": _s(128, bf), "Tri": _s(128, bf), "Id": _s(128, bf), "Id16": _s(128, f16), "Idn": _s(128, bf),
-    "M1t": _s(128, bf), "M1": _s(128, bf), "BDn": _s(128, bf), "cm64": _s(128, bf), "c192": _s(128, bf),
-    "Z": _s(144 * 9, bf), "Zh": _s(144 * 3, f16), "BDv": _s(128 * 7, bf), "BDh": _s(384, f16), "H3": _s(128, f32), "TS": _s(2048, bf),
-    "HD1": _s(192, bf), "HD2": _s(192, bf), "HDa": _s(192, bf), "HDb": _s(192, bf), "PAT": _s(192, bf),
-    "jw": _s(12, f32), "K8": _s(8, f32), "K2": _s(12, f32), "K3": _s(12, f32), "PFi": _s(32, f32), "PF": _s(32, f32),
-    "ZR": _s(192, bf), "BIG": _s(192, f32), "sqw": _s(128, f32), "c65": _s(192, bf), "HOLD": _s(640, bf),
-    "x16": _s(128, i32), "fe16": _s(128, bf), "fo16": _s(128, bf), "o16": _s(128, f16), "IdK": _s(256, bf), "sq2": _s(128, f32), "mov": _s(128, bf), "offx": _s(256, u16),
-    "xb": _s(128, i32), "rows": _s(640, bf), "ti": _s(256, i32),
+    "blk": _s(128, i32), "hmb": _s(128, i32), "XS": _s(2080, bf), "DS": _s(2080, i32), "HM": _s(2080, bf),
+    "TB": _s(TW, bf), "XBe": _s(TW, f32), "XBo": _s(TW, f32), "DQ": _s(TW, i32), "Y": _s(TW, f32), "SQ": _s(2256, f32),
+    "WIN": _s(6912, f32), "MSG": _s(2880, bf), "RX": _s(384, bf),
+    "pI": _s(2, i32), "pJ": _s(4, i32), "col": _s(40, f32), "R": _s(16, f32), "colI": _s(192, bf), "J16": _s(208, bf),
+    "one": _s(128, bf), "BD": _s(128, bf), "Tri": _s(128, bf), "Id": _s(128, bf), "Id16": _s(128, f16), "Idn": _s(128, bf),
+    "M1": _s(128, bf), "BDn": _s(128, bf), "cm64": _s(128, bf), "c192": _s(128, bf), "PW": _s(320, f16),
+    "Z": _s(144 * 4, bf), "BDv": _s(128 * 11, bf), "BDh": _s(256, f16), "H4": _s(128, f32), "TS": _s(2048, bf), "W": _s(288, bf),
+    "HD2": _s(192, bf), "PAT": _s(192, bf), "PATn": _s(192, bf), "HZ": _s(192, bf), "GH": _s(576, bf),
+    "jw": _s(36, f32), "sq2": _s(128, f32), "ZR": _s(192, bf), "BIG": _s(192, f32), "c65": _s(192, bf), "HOLD": _s(640, bf),
+    "fe": _s(128, f16), "feT": _s(128, f16), "o16": _s(128, f16), "oT": _s(128, f16), "Uw": _s(128, f16), "IdK": _s(256, bf),
+    "mov": _s(128, bf), "XT": _s(256, bf), "SP": _s(1024, bf), "oo": _s(256, f16), "offx": _s(384, u16), "xb": _s(128, i32), "rows": _s(768, bf), "ti": _s(512, i32),
     "Fw": _s(128, bf), "V0": _s(128, f32), "CE": _s(144, f32), "HS": _s(128, f32), "K16": _s(128, f16), "BDm": _s(128, bf),
-    "w8": _s(24, f32), "coff": _s(8, u16), "d0": _s(192, bf), "SB": _s(192, bf), "SH": _s(192, f32),
-    "swg": _s(12, u16), "swf": _s(12, f32), "swu": _s(36, u16), "srep": _s(192, f32), "acol": _s(192, bf), "acolA": _s(192, bf),
-    "arep": _s(192, u16), "aw": _s(12, u16), "qx": _s(192, i32), "q32": _s(192, i32), "qu": _s(192, u16), "q1": _s(192, f16),
+    "coff": _s(8, u16), "d0": _s(192, bf), "SB": _s(192, bf), "SH": _s(192, f32),
+    "swg": _s(12, u16), "swf": _s(12, f32), "swu": _s(36, u16), "srep": _s(192, f32), "acol": _s(192, bf), "ua": _s(192, f32),
+    "aw": _s(36, u16), "qx": _s(192, i32), "q32": _s(192, i32), "qA": _s(192, u16), "qB": _s(192, u16), "q1": _s(192, f16), "q2": _s(192, f16),
+    "qy": _s(192, i32), "qz": _s(192, i32), "ef": _s(192, f32), "hf": _s(128, f32),
     "XA": _s(3072, bf), "XZ": _s(3072, bf), "CMP": _s(3072, bf), "sg": _s(192, bf), "sel": _s(192, f16), "fb": _s(192, f16),
-    "H": _s(200, f32), "keyr": _s(192, f16), "atr": _s(192, f32), "keyw": _s(12, f32), "atw": _s(12, u16),
-    "vcol": _s(192, bf), "vcf": _s(192, f32), "hcol": _s(192, f32), "whow": _s(12, u16),
+    "H": _s(200, f32), "keyr": _s(192, f16), "keyw": _s(12, f32), "atw": _s(12, u16), "vcol": _s(192, bf), "hcol": _s(192, bf),
     "EQ": _s(192 * 13, bf), "AB": _s(640, bf), "EA": _s(640, bf), "G": _s(192, bf), "z": _s(192, f16), "posu": _s(12, u16),
-    "w12": _s(96, f32), "boff": _s(36, u16),
-    "H2": _s(192, f32), "endu": _s(36, u16), "RXh": _s(128, f16), "hwu": _s(8, u16), "hwh": _s(8, f16), "hg": _s(128, bf),
-    "roff": _s(24, u16), "vw": _s(8, u16), "xv": _s(128, f32), "yb": _s(128, f32),
+    "w12": _s(96, f32), "boff": _s(36, u16), "H2": _s(192, f32), "HA": _s(192, f32), "H5": _s(624, f32), "D3": _s(36, f32), "E3": _s(36, f32),
+    "endu": _s(36, u16), "hwu": _s(8, u16), "hg": _s(128, bf), "roff": _s(24, u16), "vw": _s(8, u16), "xv": _s(128, f32),
 }
 for _k in range(8):
     SCRATCH["P%d" % _k] = ("psum", [128, 512], f32)
-SEMAPHORES = ["v", "a", "p", "c", "b16", "blk", "xs", "ds", "hm", "tb", "pf", "out", "sent", "arr0", "arr1", "arr2"]
+SEMAPHORES = ["v", "a", "p", "c", "blk", "hmb", "xs", "ds0", "ds1", "hm", "tb", "out", "sent", "arr0", "arr1", "arr2"]
+
+
+def put_in_order(ops):
+    n = len(ops)
+    cost = [o["cost"] for o in ops]
+    pre = [[(j, d + ops[j]["lat"]) for j, d in o["pre"].items()] for o in ops]
+    post = [[] for o in ops]
+    for i in range(n):
+        for j, d in pre[i]:
+            post[j].append((i, d))
+
+    def place(order, follows, first):
+        start, taken = [0.0] * n, {}
+        for i in order:
+            t = max([start[j] + cost[j] + d for j, d in follows[i]] + [first[i]])
+            line = taken.setdefault(ops[i]["e"], [])
+            k = 0
+            while k < len(line) and line[k][0] < t + cost[i] - 1e-9:
+                t = max(t, line[k][1])
+                k += 1
+            line.insert(k, (t, t + cost[i]))
+            start[i] = t
+        return start
+
+    way = [0.0] * n
+    for i in range(n - 1, -1, -1):
+        way[i] = cost[i] + max([way[j] + d for j, d in post[i]] + [ops[i]["lat"]])
+    best = None
+    for turn in range(PASSES):
+        start = place(sorted(range(n), key=lambda k: (-way[k], k)), pre, [0.0] * n)
+        end = max(start[i] + cost[i] + ops[i]["lat"] for i in range(n))
+        if best is None or end < best[0]:
+            best = (end, start)
+        back = place(sorted(range(n), key=lambda k: (-start[k] - cost[k], -k)), post, [o["lat"] for o in ops])
+        way = [back[i] + cost[i] for i in range(n)]
+    return best[1]
 
 
 def rank_program(g, core, T, topo):
@@ -47,573 +84,569 @@ def rank_program(g, core, T, topo):
     if rank is None:
         return
     Q = {"v": g.vector, "a": g.scalar, "p": g.tensor, "c": g, "s": g.sync}
-    cnt = {"v": 0, "a": 0, "p": 0, "c": 0}
-    seen, lastw, reads = {}, {}, {}
+    ops, lastw, reads, before = [], {}, {}, {}
     banks = ["P%d" % k for k in range(8)]
 
-    def wait(e, tok):
-        if seen.get((e, tok[0]), 0) < tok[1]:
-            seen[(e, tok[0])] = tok[1]
-            Q[e].wait_ge(T.sem[tok[0]], tok[1])
+    def op(e, fn, rd, wr, cost, lat=0.0, sem=None):
+        i, pre = len(ops), set()
+        for k in sorted(set(rd + wr)):
+            w = lastw.get(k, [])
+            if k in wr and sem and w and ops[w[0]]["sem"] == sem:
+                pre |= before[k]
+                w.append(i)
+                continue
+            mine = set(w) | {r for r in reads.get(k, []) if k in wr or (k in banks and ops[r]["e"] != e)}
+            pre |= mine
+            if k in wr:
+                lastw[k], reads[k], before[k] = [i], [], mine
+            else:
+                reads.setdefault(k, []).append(i)
+        ops.append({"e": e, "fn": fn, "cost": cost, "lat": lat, "sem": sem,
+                    "pre": {j: 0.0 if e == "p" == ops[j]["e"] else WAKE for j in pre}})
 
-    def deps(e, rd, wr, tok, free):
-        for k in rd + wr:
-            w = lastw.get(k)
-            if w and (w[0] != tok[0] or not free):
-                wait(e, w)
-            for r in reads.get(k, []):
-                if (k in wr and (r[0] != tok[0] or not free)) or (k in banks and r[0] != tok[0]):
-                    wait(e, r)
-        for k in wr:
-            lastw[k] = tok
-            reads[k] = []
-        for k in rd:
-            if k not in wr:
-                reads.setdefault(k, []).append(tok)
+    rows_of = {}
 
-    def op(e, fn, rd, wr, inc=True):
-        deps(e, rd, wr, (e, cnt[e] + 1), e == "p")
-        ins = fn()
-        if inc:
-            cnt[e] += 1
-            ins.then_inc(T.sem[e], 1)
-
-    def dma(e, out, in_, rd, wr, sem, total):
-        deps(e, rd, wr, (sem, total), True)
-        Q[e].dma_start(out, in_).then_inc(T.sem[sem], 16)
+    def row(name):
+        i = len(ops) - 1
+        if name in rows_of:
+            ops[i]["pre"].setdefault(rows_of[name], 0.0)
+        rows_of[name] = i
 
     V, S = g.vector, g.scalar
+    ga = lambda n: 60 + GAT * n
+    sc = lambda n: 60 + SCA * n
+    vc = lambda c: max(64, c) * CYC
 
-    def ts(out, in0, s1, s2, o0, o1, rd, wr):
+    def dma(e, out, in_, rd, wr, sem, lat, behind=0):
+        op(e, lambda: Q[e].dma_start(out, in_), rd, wr, 0.05, lat, (sem, 16))
+        for j in range(len(ops) - 1 - behind, len(ops) - 1):
+            ops[-1]["pre"][j] = -ops[j]["lat"]
+
+    def ts(out, in0, s1, s2, o0, o1, rd, wr, c=64):
         if s2 is None:
-            op("v", lambda: V.tensor_scalar(out, in0, s1, None, o0), rd, wr)
+            op("v", lambda: V.tensor_scalar(out, in0, s1, None, o0), rd, wr, vc(c))
         else:
-            op("v", lambda: V.tensor_scalar(out, in0, s1, s2, o0, o1), rd, wr)
+            op("v", lambda: V.tensor_scalar(out, in0, s1, s2, o0, o1), rd, wr, vc(c))
 
-    def tt(out, a, b, o, rd, wr):
-        op("v", lambda: V.tensor_tensor(out, a, b, o), rd, wr)
+    def tt(out, a, b, o, rd, wr, c=64):
+        op("v", lambda: V.tensor_tensor(out, a, b, o), rd, wr, vc(c))
 
-    def cp(out, a, rd, wr):
-        op("v", lambda: V.tensor_copy(out, a), rd, wr)
+    def cp(out, a, rd, wr, c=64):
+        op("v", lambda: V.tensor_copy(out, a), rd, wr, vc(c))
 
-    def scan(out, a, b, ini, o0, o1, rd, wr):
-        op("v", lambda: V.tensor_tensor_scan(out, a, b, ini, o0, o1), rd, wr)
+    def scan(out, a, b, ini, o0, o1, rd, wr, c=192):
+        op("v", lambda: V.tensor_tensor_scan(out, a, b, ini, o0, o1), rd, wr, vc(c))
 
-    def ms(ap, c, wr):
-        op("v", lambda: V.memset(ap, c), [], wr)
+    def ms(ap, x, wr, c=64):
+        op("v", lambda: V.memset(ap, x), [], wr, vc(c))
 
-    def act(out, a, rd, wr, func=F.Identity, bias=0.0, scale=1.0):
-        op("a", lambda: S.activation(out, a, func, bias=bias, scale=scale), rd, wr)
+    def act(out, a, rd, wr, func=F.Identity, bias=0.0, scale=1.0, c=128):
+        op("a", lambda: S.activation(out, a, func, bias=bias, scale=scale), rd, wr, 0.05 + vc(c))
 
-    def scaled(out, src, w, rd, wr):
-        act(out, src, rd, wr, F.Identity, 0.0, w)
+    def scaled(out, src, w, rd, wr, c=128):
+        act(out, src, rd, wr, F.Identity, 0.0, w, c)
 
-    def mm(out, l, r, start, stop, rd, wr, inc=None):
-        op("p", lambda: g.tensor.matmul(out, l, r, start, stop), rd, wr, stop if inc is None else inc)
+    def mms(calls, rd, wr, n):
+        def fn():
+            for a in calls:
+                ins = g.tensor.matmul(*a)
+            return ins
+        op("p", fn, rd, wr, len(calls) * max(64, n) * PEC)
 
-    def wrap(out, z, src, rd, wr, start=True, stop=True):
-        for i in range(16):
-            mm(out, z(i), src(i), start and i == 0, stop and i == 15, rd, wr, i == 15)
+    def mm(out, l, r, start, stop, rd, wr, n=192):
+        mms([(out, l, r, start, stop)], rd, wr, n)
 
-    def iota(out, p, base, cm, wr, flag=True):
+    def wrap(out, z, src, rd, wr, n, start=True, stop=True):
+        mms([(out, z(i), src(i), start and i == 0, stop and i == 15) for i in range(16)], rd, wr, n)
+
+    def iota(out, p, base, cm, wr, n, flag=True):
         if flag:
-            op("c", lambda: g.iota(out, p, base, cm, allow_small_or_imprecise_dtypes=True), [], wr)
+            op("c", lambda: g.iota(out, p, base, cm, allow_small_or_imprecise_dtypes=True), [], wr, 0.13 + 2 * n * CYC)
         else:
-            op("c", lambda: g.iota(out, p, base, cm), [], wr)
+            op("c", lambda: g.iota(out, p, base, cm), [], wr, 0.13 + 2 * n * CYC)
 
-    def asel(out, a, p, o, fill, base, cm, rd, wr):
-        op("c", lambda: g.affine_select(out, a, p, o, fill, base, cm), rd, wr)
+    def asel(out, a, p, o, fill, base, cm, rd, wr, n=128):
+        op("c", lambda: g.affine_select(out, a, p, o, fill, base, cm), rd, wr, 0.17 + 2 * n * CYC)
 
     P = [T["P%d" % k] for k in range(8)]
     pk = lambda k: "P%d" % k
     col = lambda k: T.col[:, k:k + 1]
     Rr = lambda k: T.R[:, k:k + 1]
-    (PM, C15, WU, WAE, WAO, WOCC, WY, WO2, WE0, WE1, WE2, MA, MV, OFF, OFF1, BSEL, I192, TMP, NOCC, OFFM, OFFA, OFS, OFS1, BS2) = range(24)
-    (Z1, ZU, ZOCC, ZFE, ZFO, ZY, ZE0, ZE1, ZE2) = range(9)
+    (PM, C15, WU, WAE, WAO, WOCC, WY, WO2, WE0, WE1, WE2, MV, OFF, OFF1, BSEL, I192, TMP, OFA0, OFA1, OFS, BS2, P16, U0, U1, WH, PB, OFS1) = range(27)
+    (Z1, ZU, ZFE, ZFO) = range(4)
     zt = lambda n: T.Z[:, 144 * n:144 * n + 144]
     zw = lambda n: (lambda i: T.Z[:, 144 * n + 15 - i:144 * n + 143 - i])
-    zh = lambda n: (lambda i: T.Zh[:, 144 * n + 15 - i:144 * n + 143 - i])
+    (BAE, BAO, BIRTH, B256, B4096N, BOCC, BGW, BHOME, BNEG, BY, BU) = range(11)
     bdv = lambda n: T.BDv[:, 128 * n:128 * n + 128]
     XSk = ["XS", "XSa", "XSb"]
+    DSk = ["DS0", "DS1", "DSa"]
+    NQ = 8
+    DQk = ["DQ%d" % c for c in range(NQ)] + ["DQa"]
+    XBk = {0: ["XBe%d" % c for c in range(8)] + ["XBea"], 1: ["XBo%d" % c for c in range(8)] + ["XBoa"]}
+    XBt = {0: T.XBe, 1: T.XBo}
 
-    dma("s", T.blk[:], T.board[:], [], ["blk"], "blk", 16)
-    for k in range(8):
-        dma("s" if k < 4 else "a", T.b16[:, 16 * k:16 * k + 16], T.board[k, :], [], ["b16"], "b16", 128)
-    dma("a", T.XS[:, 0:2048], T.xs[:], [], ["XS"], "xs", 16)
-    dma("s", T.DS[0:64, 0:2048], T.ds[0:64, :], [], ["DS"], "ds", 32)
+    dma("s", T.blk[:], T.board[:], [], ["blk"], "blk", 2.0)
+    dma("s", T.XS[:, 0:2048], T.xs[:], [], ["XS"], "xs", 3.5, 1)
+    dma("s", T.hmb[:], T.hm[:], [], ["hmb"], "hmb", 4.0, 1)
+    dma("s", T.DS[0:64, 0:2048], T.ds[0:64, :], [], ["DS0"], "ds0", 5.5, 1)
 
-    iota(T.pI[:, 0:1], [[0, 1]], 0, 1, ["pI"], False)
-    iota(T.colI[:], [[1, 192]], 0, 0, ["colI"])
+    iota(T.pI[:, 0:1], [[0, 1]], 0, 1, ["pI"], 1, False)
+    iota(T.colI[:], [[1, 192]], 0, 0, ["colI"], 192)
     ms(T.one[:], 1.0, ["one"])
     asel(T.Id[:], T.one[:], [[-1, 128]], A.is_equal, 0.0, 0, 1, ["one"], ["Id"])
-    asel(T.BDt[:], T.one[:], [[-16, 8], [0, 16]], A.is_ge, 0.0, 0, 1, ["one"], ["BDt"])
-    asel(T.BD[:], T.BDt[:], [[16, 8], [0, 16]], A.is_ge, 0.0, 15, -1, ["BDt"], ["BD"])
-    iota(T.J16[:], [[0, 13], [1, 16]], 0, 0, ["J16"])
+    asel(T.BD[:], T.one[:], [[-16, 8], [0, 16]], A.is_ge, 0.0, 0, 1, ["one"], ["BD"])
+    asel(T.BD[:], T.BD[:], [[16, 8], [0, 16]], A.is_ge, 0.0, 15, -1, ["BD"], ["BD"])
+    iota(T.J16[:], [[0, 13], [1, 16]], 0, 0, ["J16"], 208)
     asel(T.Tri[:], T.BD[:], [[1, 128]], A.is_ge, 0.0, 0, -1, ["BD"], ["Tri"])
-    iota(T.jw[:], [[16, 12]], 2048, 0, ["jw"])
-    if SPLIT:
-        for k, (a, b) in enumerate(((32, 72), (104, 144), (160, 192))):
-            iota(T.XZ[:, 16 * a:16 * b], [[0, 16 * (b - a)]], 0, 0, ["XZ%d" % k])
-    ms(T.TB[:, 0:GW], 0.0, ["TB"])
-    scaled(T.cm64[:], T.colI[:, 0:128], -64.0, ["colI"], ["cm64"])
-    scaled(T.WIN[:, 0:192], T.colI[:], 0.0, ["colI"], ["WIN0"])
-    scaled(T.WIN[:, 2304:2496], T.colI[:], 0.0, ["colI"], ["WIN1"])
-    scaled(T.WIN[:, 4608:4800], T.colI[:], 0.0, ["colI"], ["WIN2"])
-    act(T.c192[:], T.colI[:, 0:128], ["colI"], ["c192"], F.Identity, 4096.0, 0.0)
-    scaled(T.ZR[:], T.colI[:], 0.0, ["colI"], ["ZR"])
-    for a, b, c in ((0, 32, 6.5), (32, 72, 0.0), (72, 104, 6.5), (104, 144, 0.0), (144, 160, 6.5), (160, 192, 0.0)):
-        act(T.c65[:, a:b], T.colI[:, a:b], ["colI"], ["c65%d" % a], F.Identity, c, 0.0)
-    act(T.Id16[:], T.Id[:], ["Id"], ["Id16"])
-    scaled(T.IdK[:, 0:128], T.Id[:], -4096.0, ["Id"], ["IdK0"])
-    scaled(T.IdK[:, 128:256], T.Id[:], 4096.0, ["Id"], ["IdK1"])
+    JW, K2, K3 = T.jw[:, 0:12], T.jw[:, 12:24], T.jw[:, 24:36]
+    iota(JW, [[16, 12]], D0, 0, ["jw"], 12)
+    VSH = ((32, 72), (104, 144), (160, 192))
+    for k, (a, b) in enumerate(VSH):
+        ms(T.XZ[:, 16 * a:16 * b], 0.0, ["XZ%d" % k], 8 * (b - a))
+    for c in range(4):
+        iota(T.SQ[:, 564 * c:564 * c + 564], [[1, 564]], 564 * c, 0, ["SQ%d" % c], 564)
+    SQk = ["SQ%d" % c for c in range(4)]
+    ms(T.TB[:, 0:GW], 0.0, ["TB"], GW // 2)
+    ms(T.XS[:, 2048:2064], 1e9, ["XSa"])
+    ms(T.XS[:, 2064:2080], -1e9, ["XSb"])
+    ms(T.DS[:, 2048:2080], 0, ["DSa"])
+    ms(T.DQ[:, 2048:2064], 0, ["DQa"])
+    ms(T.XBe[:, 2048:2064], -1e9, ["XBea"])
+    ms(T.XBo[:, 2048:2064], -1e9, ["XBoa"])
+    ms(T.CE[:, 0:16], 0.0, ["CE0"])
+    ms(T.H[:, 0:1], 3 * BB, ["H0"])
+    ms(T.H5[:, 77:624:48], 0.0, ["H5z"])
+    ms(T.D3[:, 0:36:3], 0.0, ["D3a"])
+    ms(T.D3[:, 2:36:3], 1.0, ["D3b"])
     ts(T.pJ[:, 0:1], T.pI[:, 0:1], 15, None, A.bitwise_and, None, ["pI"], ["pJ0"])
     ts(T.pJ[:, 1:2], T.pI[:, 0:1], 112, None, A.bitwise_and, None, ["pI"], ["pJ1"])
-    ms(T.CE[:, 0:16], 0.0, ["CE0"])
+    ts(T.pJ[:, 2:3], T.pI[:, 0:1], 16, None, A.bitwise_and, None, ["pI"], ["pJ2"])
     cp(col(PM), T.pJ[:, 0:1], ["pJ0"], ["PM"])
     ts(col(C15), T.pJ[:, 1:2], 15.0, None, A.add, None, ["pJ1"], ["C15"])
-    ms(T.XS[:, 2048:2064], 1e9, ["XSa"])
+    ts(col(P16), T.pI[:, 0:1], 16.0, None, A.add, None, ["pI"], ["P16"])
+    for u in range(2):
+        ts(col(U0 + u), T.pJ[:, 2:3], 16.0 * u, None, A.is_equal, None, ["pJ2"], ["U%d" % u])
+        ts(T.PW[:, 160 * u:160 * u + 160], T.colI[:, 0:160], col(P16), col(U0 + u), A.is_equal, A.mult, ["colI", "P16", "U%d" % u], ["PW%d" % u], 80)
     ts(T.R[:], T.colI[:, 0:16], col(PM), None, A.is_equal, None, ["colI", "PM"], ["R"])
-    ts(zt(Z1), T.colI[:, 0:144], col(C15), None, A.is_equal, None, ["colI", "C15"], ["Z1"])
-    ms(T.XS[:, 2064:2080], -1e9, ["XSb"])
+    ts(zt(Z1), T.colI[:, 0:144], col(C15), None, A.is_equal, None, ["colI", "C15"], ["Z1"], 72)
     ts(col(TMP), Rr(0), 256.0, Rr(1), A.mult, A.add, ["R"], ["TMP"])
     ts(col(WU), col(TMP), 2.0, Rr(8), A.mult, A.add, ["TMP", "R"], ["WU"])
     ts(col(WAE), Rr(2), -2064.0, col(WU), A.mult, A.add, ["R", "WU"], ["WAE"])
-    ts(T.x16[:], T.b16[:], 2049, None, A.bitwise_and, None, ["b16"], ["x16"])
-    ts(T.xb[:], T.blk[:], 2049, None, A.bitwise_and, None, ["blk"], ["xb"])
-    ts(T.fe16[:], T.x16[:], 0.0, None, A.is_equal, None, ["x16"], ["fe16"])
-    mm(P[0][:, 0:128], T.fe16[:], T.Id[:], True, True, ["fe16", "Id"], ["P0"])
-    ts(T.rows[:, 256:384], T.xb[:], 0.0, None, A.is_equal, None, ["xb"], ["r2"])
-    ts(T.rows[:, 384:512], T.xb[:], 1.0, None, A.is_equal, None, ["xb"], ["r3"])
-    ts(T.HDa[:], T.J16[:, 0:192], col(PM), -4 * BB, A.is_equal, A.mult, ["J16", "PM"], ["HDa"])
-    ts(T.HDb[:], T.J16[:, 15:207], col(PM), BB, A.is_equal, A.mult, ["J16", "PM"], ["HDb"])
-    ts(T.ti[:, 0:128], T.blk[:], 9, 3, A.logical_shift_right, A.bitwise_and, ["blk"], ["ti0"])
-    ts(T.ti[:, 128:256], T.blk[:], 1, 255, A.logical_shift_right, A.bitwise_and, ["blk"], ["ti1"])
-    cp(T.o16[:], T.b16[:], ["b16"], ["o16"])
-    cp(T.rows[:, 0:256], T.ti[:], ["ti0", "ti1"], ["r01"])
-    for r, c0, k in ((2, 256, "r2"), (3, 384, "r3"), (8, 384, "r3"), (0, 0, "r01"), (1, 128, "r01")):
-        dma("s", T.TB[r:128:16, 0:2048], T.rows[:, c0:c0 + 128], [k], ["TB"], "tb", 80)
-    dma("s", T.DS[64:128, 0:2048], T.ds[64:128, :], [], ["DS"], "ds", 32)
-    ts(T.fo16[:], T.x16[:], 1.0, None, A.is_equal, None, ["x16"], ["fo16"])
+    ts(col(WAO), Rr(3), -2064.0, col(WU), A.mult, A.add, ["R", "WU"], ["WAO"])
+    ts(col(WOCC), Rr(2), Rr(3), None, A.add, None, ["R"], ["WOCC"])
+    ts(col(WY), col(WOCC), -2048.0, col(WU), A.mult, A.add, ["WOCC", "WU"], ["WY"])
+    ts(col(WO2), col(WOCC), float(GW), None, A.mult, None, ["WOCC"], ["WO2"])
+    for t in range(3):
+        ts(col(WE0 + t), Rr(4 + t), col(WOCC), None, A.add, None, ["R", "WOCC"], ["WE%d" % t])
+    ts(col(TMP + 12), Rr(0), Rr(1), Rr(8), A.add, A.add, ["R"], ["MA"])
+    ts(col(MV), col(TMP + 12), col(WOCC), None, A.add, None, ["MA", "WOCC"], ["MV"])
     ts(col(OFF), col(PM), 15.0, BB, A.not_equal, A.mult, ["PM"], ["OFF"])
+    for k, x in ((OFF1, 1.0), (OFA0, -2064.0), (OFS, 2048.0), (OFS1, 2047.0)):
+        ts(col(k), col(OFF), x, None, A.add, None, ["OFF"], ["c%d" % k])
+    ts(col(BSEL), col(PM), -2048.0, -2048.0, A.mult, A.add, ["PM"], ["BSEL"])
+    ts(col(BS2), col(PM), -4096.0, None, A.mult, None, ["PM"], ["BS2"])
+    ts(col(I192), col(PM), 192.0, None, A.mult, None, ["PM"], ["I192"])
+    ts(col(WH), Rr(9), 256.0, Rr(7), A.mult, A.add, ["R"], ["WH"])
+    ts(col(TMP + 13), Rr(9), float(H0 // 256), None, A.mult, None, ["R"], ["PBa"])
+    ts(col(PB), Rr(7), 32.0 * rank, col(TMP + 13), A.mult, A.add, ["R", "PBa"], ["PB"])
+    ts(T.AB[:, 0:192], T.J16[:, 0:192], col(PM), -4 * BB, A.is_equal, A.mult, ["J16", "PM"], ["HDa"], 96)
+    ts(T.EA[:, 0:192], T.J16[:, 15:207], col(PM), BB, A.is_equal, A.mult, ["J16", "PM"], ["HDb"], 96)
+    tt(T.HD2[:], T.AB[:, 0:192], T.EA[:, 0:192], A.add, ["HDa", "HDb"], ["HD2"], 384)
+    ts(T.PAT[:], T.J16[:, 15:207], col(PM), BB, A.not_equal, A.mult, ["J16", "PM"], ["PAT"], 96)
+    ts(T.HZ[:], T.J16[:, 0:192], col(PM), None, A.not_equal, None, ["J16", "PM"], ["HZ"], 96)
+    scaled(T.PATn[:], T.HZ[:], -BB, ["HZ"], ["PATn"], 192)
+    ts(K2, JW, col(PM), col(OFS), A.add, A.add, ["jw", "PM", "c%d" % OFS], ["K2"])
+    ts(K3, JW, col(PM), float(BD0 + 1 - D0), A.add, A.add, ["jw", "PM"], ["K3"])
+    scaled(T.cm64[:], T.colI[:, 0:128], -64.0, ["colI"], ["cm64"])
+    for t in range(3):
+        scaled(T.WIN[:, 2304 * t:2304 * t + 192], T.colI[:], 0.0, ["colI"], ["WIN%d" % t], 192)
+        act(T.GH[:, 192 * t:192 * t + 192], T.colI[:], ["colI", "R"], ["GH%d" % t], F.Identity, Rr(4 + t), 0.0, 192)
+        for p in range(4):
+            c0 = 960 * t + 192 * p
+            act(T.MSG[:, c0:c0 + 32], T.colI[:, 0:32], ["colI", "R", "PB"], ["MSG%d%d" % (t, p)], F.Identity, col(PB), Rr(7), 64)
+    act(T.c192[:], T.colI[:, 0:128], ["colI"], ["c192"], F.Identity, 4096.0, 0.0)
+    scaled(T.ZR[:], T.colI[:], 0.0, ["colI"], ["ZR"], 192)
+    c65k = []
+    for a, b, x in ((0, 32, 6.5), (32, 72, 0.0), (72, 104, 6.5), (104, 144, 0.0), (144, 160, 6.5), (160, 192, 0.0)):
+        ms(T.c65[:, a:b], x, ["c65%d" % a])
+        c65k.append("c65%d" % a)
+    act(T.Id16[:], T.Id[:], ["Id"], ["Id16"])
+    scaled(T.IdK[:, 0:128], T.Id[:], 4096.0, ["Id"], ["IdK0"])
+    scaled(T.IdK[:, 128:256], T.Id[:], -4096.0, ["Id"], ["IdK1"])
+    scaled(T.Idn[:], T.Id[:], -1.0, ["Id"], ["Idn"])
     act(T.K16[:], T.colI[:, 0:128], ["colI"], ["K16"], F.Identity, 2048.0, 2.0)
     scaled(T.BDm[:], T.BD[:], -4096.0, ["BD"], ["BDm"])
+    act(T.sq2[:], T.colI[:, 0:128], ["colI", "PM"], ["sq2"], F.Identity, col(PM), 16.0)
+    for k in range(4):
+        act(T.HOLD[:, 160 * k:160 * k + 160], T.J16[:, 0:160], ["J16"], ["HOLD%d" % k], F.Sign, c=160)
+    HOLDk = ["HOLD%d" % k for k in range(4)]
+    for k, w, wk in ((BAE, col(WAE), "WAE"), (BAO, col(WAO), "WAO"), (BIRTH, Rr(0), "R"), (B256, 256.0, "BD"), (B4096N, -4096.0, "BD"),
+                     (BOCC, col(WOCC), "WOCC"), (BGW, col(WO2), "WO2"), (BHOME, col(WH), "WH"), (BNEG, -1.0, "BD"), (BY, col(WY), "WY")):
+        scaled(bdv(k), T.BD[:], w, ["BD", wk], ["BD%d" % k])
+    scaled(bdv(BU), T.BD[:], col(WU), ["BD", "WU"], ["BD%d" % BU])
+    scaled(T.BDh[:, 0:128], T.BD[:], 1.0, ["BD"], ["BDh0"])
+    scaled(T.BDh[:, 128:256], T.BD[:], 0.0625, ["BD"], ["BDh1"])
+    scaled(T.BDn[:], T.BD[:], -2048.0, ["BD"], ["BDn"])
+    asel(T.BDn[:], T.BDn[:], [[1, 128]], A.is_gt, 0.0, 0, -1, ["BDn"], ["BDn"])
+    asel(T.M1[:], T.BDn[:], [[1, 128]], A.not_equal, 2048.0, 0, -1, ["BDn"], ["M1"])
+    scaled(zt(ZU), zt(Z1), col(WU), ["Z1", "WU"], ["ZU"], 144)
+    scaled(zt(ZFE), zt(Z1), Rr(2), ["Z1", "R"], ["ZF0"], 144)
+    scaled(zt(ZFO), zt(Z1), Rr(3), ["Z1", "R"], ["ZF1"], 144)
+    ms(T.EQ[:, 0:512], 1.0, ["EQ0"], 256)
+    for k in range(2):
+        asel(T.SP[:, 512 * k:512 * k + 512], T.EQ[:, 0:512], [[-1, 32], [0, 16]], A.is_equal, 0.0, -72 * k, 1, ["EQ0"], ["SP%d" % k], 512)
+    iota(T.BIG[:], [[0, 192]], 8388608, 0, ["BIG"], 192)
+    iota(T.HM[:], [[0, 2080]], 0, 0, ["HM"], 2080)
+    ts(T.W[:, 0:144], T.colI[:, 0:144], col(C15), 4096.0, A.is_gt, A.mult, ["colI", "C15"], ["Wa"], 72)
+    scaled(T.W[:, 144:288], zt(Z1), -4096.0, ["Z1"], ["Wb"], 144)
+    tt(T.W[:, 0:144], T.W[:, 0:144], T.W[:, 144:288], A.add, ["Wa", "Wb"], ["Wa"], 288)
+    for k in range(16):
+        asel(T.TS[:, 128 * k:128 * k + 128], T.W[:, 15 - k:143 - k], [[-16, 8], [0, 16]], A.is_ge, 0.0, 0, 1, ["Wa"], ["TS%d" % k])
+        row("TS")
+    TSk = ["TS%d" % k for k in range(16)]
 
-    def xb_build(tab, key, c0, b0, b1, ok, e="a"):
-        src = T.XS[:, 0:2080].indirect(T.offx[:, c0 + b0:c0 + b1])
-        if e == "a":
-            act(tab[:, 16 * b0:16 * b1], src, XSk + [ok], [key], F.Copy)
-        else:
-            cp(tab[:, 16 * b0:16 * b1], src, XSk + [ok], [key])
+    def rewrap(bank, src, sk, c0=0):
+        calls = []
+        for be in range(4):
+            for u in range(2):
+                for h in range(2):
+                    x = 160 * u + 16 - 16 * (h - u)
+                    calls.append((P[bank][:, 2 * be + u:128:8], T.PW[:, x:x + 128], src[:, c0 + 32 * be + 16 * h:c0 + 32 * be + 16 * h + 16], not calls, len(calls) == 15))
+        mms(calls, ["PW0", "PW1", sk], [pk(bank)], 64)
 
-    def xb_clear(tab, key, off, ok):
-        op("a", lambda: S.activation(tab[:].indirect(off), T.BIG[:], F.Silu), ["BIG", ok], [key])
+    ts(T.xb[:], T.blk[:], 2049, None, A.bitwise_and, None, ["blk"], ["xb"], 128)
+    ts(T.fe[:], T.xb[:], 0.0, None, A.is_equal, None, ["xb"], ["fe"], 128)
+    op("v", lambda: V.transpose(T.feT[:], T.fe[:]), ["fe"], ["feT"], vc(64))
+    rewrap(0, T.feT, "feT")
+    cp(T.o16[:], T.blk[:], ["blk"], ["o16"], 128)
+    op("v", lambda: V.transpose(T.oT[:], T.o16[:]), ["o16"], ["oT"], vc(64))
+    ts(T.oo[:, 0:128], T.xb[:], 0.0, 2048.0, A.is_equal, A.mult, ["xb"], ["oo"], 128)
+    tt(T.oo[:, 0:128], T.oo[:, 0:128], T.o16[:], A.max, ["oo", "o16"], ["oo"], 256)
+    op("v", lambda: V.transpose(T.oo[:, 128:256], T.oo[:, 0:128]), ["oo"], ["ooT"], vc(64))
+    rewrap(5, T.oo, "ooT", 128)
+    cp(T.offx[:, 0:128], P[5][:, 0:128], ["P5"], ["offo"], 128)
+    rewrap(7, T.oT, "oT")
+    act(T.Uw[:], P[7][:, 0:128], ["P7"], ["Uw"])
+    cp(T.offx[:, 256:384], P[7][:, 0:128], ["P7"], ["offu"], 128)
+    ts(T.rows[:, 256:384], T.xb[:], 0.0, None, A.is_equal, None, ["xb"], ["r2"], 128)
+    ts(T.rows[:, 384:512], T.xb[:], 1.0, None, A.is_equal, None, ["xb"], ["r3"], 128)
+    ts(T.ti[:, 0:128], T.blk[:], 9, 3, A.logical_shift_right, A.bitwise_and, ["blk"], ["ti0"], 128)
+    ts(T.ti[:, 128:256], T.blk[:], 1, 255, A.logical_shift_right, A.bitwise_and, ["blk"], ["ti1"], 128)
+    cp(T.rows[:, 0:256], T.ti[:, 0:256], ["ti0", "ti1"], ["r01"], 256)
+    for r, c0, k in ((2, 256, "r2"), (3, 384, "r3"), (8, 384, "r3"), (0, 0, "r01"), (1, 128, "r01")):
+        dma("s", T.TB[r:128:16, 0:2048], T.rows[:, c0:c0 + 128], [k], ["TB"], "tb", 2.5)
+    dma("s", T.DS[64:128, 0:2048], T.ds[64:128, :], [], ["DS1"], "ds1", 3.5, 5)
+    ts(T.ti[:, 256:384], T.hmb[:], 255, None, A.bitwise_and, None, ["hmb"], ["ti2"], 128)
+    ts(T.ti[:, 384:512], T.hmb[:], 8, None, A.logical_shift_right, None, ["hmb"], ["ti3"], 128)
+    cp(T.rows[:, 512:768], T.ti[:, 256:512], ["ti2", "ti3"], ["r79"], 256)
+    for r, c0 in ((7, 512), (9, 640)):
+        dma("s", T.HM[r:128:16, 0:2048], T.rows[:, c0:c0 + 128], ["r79"], ["HM"], "hm", 2.5)
 
-    ea0 = [0]
-    for b in range(NB, 11):
-        ea0.append(ea0[-1] + 176 - 16 * b)
+    def xb_build(par, c0, ok):
+        for c in range(8):
+            act(XBt[par][:, 256 * c:256 * c + 256], T.XS[:, 0:2080].indirect(T.offx[:, c0 + 16 * c:c0 + 16 * c + 16]), XSk + [ok], [XBk[par][c]], F.Copy, c=GAT * 256)
+            row("XB")
 
-    def dedupe(kv, ka, kp, pd, w, wk, early, mid, late):
-        scan(T.H[:, 1:193], T.HD2[:], P[kv][:, 0:192], 2 * BB, A.add, A.max, ["HD2", pk(kv)], ["H"])
-        act(T.keyr[:], P[ka][:, 0:192], [pk(ka)], ["keyr"])
+    silu = [1.3]
+
+    def xb_clear(par, off, ok):
+        op("a", lambda: S.activation(XBt[par][:].indirect(off), T.BIG[:], F.Silu), ["BIG", ok], XBk[par], vc(sc(192)) + silu[0])
+        silu[0] = 0.0
+
+    def hold(out, src, n, rd, wr):
+        scan(out, T.HD2[:, 0:n], src, 2 * BB, A.add, A.max, ["HD2"] + rd, wr, n)
+
+    def dedupe(kv, ka, kp, pd, w, wk, early, stop, NB):
+        hold(T.H[:, 1:193], P[kv][:, 0:192], 192, [pk(kv)], ["H"])
         early()
+        act(T.keyr[:], P[ka][:, 0:192], [pk(ka)], ["keyr"], c=192)
         ts(T.keyw[:], T.H[:, 16:193:16], col(OFF), None, A.subtract, None, ["H", "OFF"], ["keyw"])
+        ea0 = [0]
         for b in range(NB, 11):
-            act(T.AB[:, ea0[b - NB]:ea0[b - NB + 1]], P[ka][:, 16 * b + 16:192], [pk(ka), "keyw"], ["AB%d" % b], F.Abs, T.keyw[:, b:b + 1], -1.0)
+            ea0.append(ea0[-1] + 176 - 16 * b)
+            act(T.AB[:, ea0[-2]:ea0[-1]], P[ka][:, 16 * b + 16:192], [pk(ka), "keyw"], ["AB%d" % b], F.Abs, T.keyw[:, b:b + 1], -1.0, 176 - 16 * b)
+            row("AB")
         if NB < 11:
-            act(T.EA[:, 0:ea0[-1]], T.AB[:, 0:ea0[-1]], ["AB%d" % b for b in range(NB, 11)], ["EA"], F.Relu, 1.0, -1.0)
-        late()
-        tt(T.EQ[:, 0:192], T.H[:, 0:192], P[kp][:, 0:192], A.is_equal, ["H", "H0", pk(kp)], ["EQ0"])
+            act(T.EA[:, 0:ea0[-1]], T.AB[:, 0:ea0[-1]], ["AB%d" % b for b in range(NB, 11)], ["EA"], F.Relu, 1.0, -1.0, ea0[-1])
+        tt(T.EQ[:, 0:192], T.H[:, 0:192], P[kp][:, 0:192], A.is_equal, ["H", "H0", pk(kp)], ["EQ0"], 192)
+        mm(P[pd][:, 0:192], w, T.EQ[:, 0:192], False, False, [wk, "EQ0"], [pk(pd)])
         for b in range(NB):
-            ts(T.EQ[:, 208 * b + 208:192 * b + 384], T.keyr[:, 16 * b + 16:192], T.keyw[:, b:b + 1], None, A.is_equal, None, ["keyr", "keyw"], ["EQ%d" % (b + 1)])
-            mid(b)
-
-    def dup_mm(pd, w, wk, bs, stop=False):
-        for b in bs:
-            last = stop and b == bs[-1]
-            if b < 0:
-                mm(P[pd][:, 0:192], w, T.EQ[:, 0:192], False, last, [wk, "EQ0"], [pk(pd)])
-            elif b < NB:
-                mm(P[pd][:, 16 * b + 16:192], w, T.EQ[:, 208 * b + 208:192 * b + 384], False, last, [wk, "EQ%d" % (b + 1)], [pk(pd)])
-            else:
-                mm(P[pd][:, 16 * b + 16:192], w, T.EA[:, ea0[b - NB]:ea0[b - NB + 1]], False, last, [wk, "EA"], [pk(pd)])
+            e = T.EQ[:, 208 * b + 208:192 * b + 384]
+            ts(e, T.keyr[:, 16 * b + 16:192], T.keyw[:, b:b + 1], None, A.is_equal, None, ["keyr", "keyw"], ["EQ%d" % (b + 1)], 88 - 8 * b)
+            row("EQ")
+            mm(P[pd][:, 16 * b + 16:192], w, e, False, stop and b == 10, [wk, "EQ%d" % (b + 1)], [pk(pd)], 176 - 16 * b)
+        if NB < 11:
+            mms([(P[pd][:, 16 * b + 16:192], w, T.EA[:, ea0[b - NB]:ea0[b - NB + 1]], False, stop and b == 10) for b in range(NB, 11)], [wk, "EA"], [pk(pd)], 64)
 
     w12 = lambda k: T.w12[:, 12 * k:12 * k + 12]
     peers = [p for p in range(len(T.cores)) if p != rank]
     peers = peers[rank % 3:] + peers[:rank % 3]
-    sent = [0]
-    XF, XFk = (T.XZ, ["XZ"]) if SPLIT else (T.XA, ["XA%d" % c for c in range(6)])
     CMPk = ["CMP%d" % c for c in range(6)]
-    EFk = ["EF%d" % c for c in range(4)]
 
     for t in range(3):
         odd = t & 1
-        XB, XBk = (T.XBe, ["XBe"]) if odd else (T.XBo, ["XBo", "XBv"])
-        swu, boff, endu, roff = T.swu[:, 12 * t:12 * t + 12], T.boff[:, 12 * t:12 * t + 12], T.endu[:, 12 * t:12 * t + 12], T.roff[:, 8 * t:8 * t + 8]
-        sk, bk, ek, rk, wk, mk = ["%s%d" % (n, t) for n in ("swu", "boff", "endu", "roff", "WIN", "MSG")]
+        XB, XK = XBt[1 - odd], XBk[1 - odd]
+        swu, boff, endu, roff, aw = [x[:, n * t:n * t + n] for x, n in ((T.swu, 12), (T.boff, 12), (T.endu, 12), (T.roff, 8), (T.aw, 12))]
+        sk, bk, ek, rk, wk, ak = ["%s%d" % (n, t) for n in ("swu", "boff", "endu", "roff", "WIN", "aw")]
+        mk = ["MSG%d%d" % (t, p) for p in range(4)]
         if t > 0:
-            wrap(P[0][:, 0:128], zw(ZFO if odd else ZFE), lambda i: T.TB[:, i:2048:16], ["TB", "Zf"], ["P0"])
-            tab, tk = (T.XBe, "XBe") if odd else (T.XBo, "XBo")
-            cp(tab[:].indirect(T.endu[:, 12 * t - 12:12 * t]), XF[:, 0:3072:16], XFk + ["endu%d" % (t - 1)], [tk])
+            wrap(P[0][:, 0:128], zw(ZFO if odd else ZFE), lambda i: T.TB[:, i:2048:16], ["TB", "ZF%d" % odd], ["P0"], 128)
+            pe, pa = T.endu[:, 12 * t - 12:12 * t], T.aw[:, 12 * t - 12:12 * t]
+            cp(XB[:].indirect(pe), T.XZ[:, 0:3072:16], ["XZ", "endu%d" % (t - 1)], XK, sc(192))
+            act(T.ef[:], T.SQ[:, 0:2256].indirect(pe), SQk + ["endu%d" % (t - 1)], ["ef"], F.Copy, c=GAT * 192)
+            tt(T.qy[:], T.DS[:].indirect(pa), T.ef[:], A.add, DSk + ["aw%d" % (t - 1), "ef"], ["qy"], ga(192))
+            ts(T.qz[:], T.qy[:], 2047, None, A.bitwise_and, None, ["qy"], ["qz"], 192)
+            cp(T.DQ[:].indirect(pe), T.qz[:], ["qz", "endu%d" % (t - 1)], DQk, sc(192))
         act(T.Fw[:], P[0][:, 0:128], ["P0"], ["Fw"])
-        if t == 0:
-            scaled(T.Idn[:], T.Id[:], -1.0, ["Id"], ["Idn"])
-            act(T.sq2[:], T.colI[:, 0:128], ["colI", "PM"], ["sq2"], F.Identity, col(PM), 16.0)
-            for k in range(4):
-                act(T.HOLD[:, 160 * k:160 * k + 160], T.J16[:, 0:160], ["J16"], ["HOLD%d" % k], F.Sign)
-        mm(P[2][:, 0:128], T.BD[:], T.Fw[:], True, True, ["BD", "Fw"], ["P2"])
-        mm(P[6][:, 0:128], T.Id16[:], T.K16[:], True, False, ["Id16", "K16"], ["P6"])
-        mm(P[6][:, 0:128], T.BDm[:], T.Fw[:], False, True, ["BDm", "Fw"], ["P6"])
-        mm(P[1][:, 0:128], T.Id[:], T.cm64[:], True, False, ["Id", "cm64"], ["P1"])
-        mm(P[1][:, 0:128], T.Tri[:], T.Fw[:], False, True, ["Tri", "Fw"], ["P1"])
-        if t == 0:
-            mm(P[3][:, 0:192], T.Id[:], T.HDa[:], True, False, ["Id", "HDa"], ["P3"])
-            mm(P[3][:, 0:192], T.Id[:], T.HDb[:], False, True, ["Id", "HDb"], ["P3"])
-            act(T.HD2[:], P[3][:, 0:192], ["P3"], ["HD2"])
+        mm(P[2][:, 0:128], T.BD[:], T.Fw[:], True, True, ["BD", "Fw"], ["P2"], 128)
+        mm(P[6][:, 0:128], T.Id16[:], T.K16[:], True, False, ["Id16", "K16"], ["P6"], 128)
+        mm(P[6][:, 0:128], T.BDm[:], T.Fw[:], False, True, ["BDm", "Fw"], ["P6"], 128)
+        mm(P[1][:, 0:128], T.Id[:], T.cm64[:], True, False, ["Id", "cm64"], ["P1"], 128)
+        mm(P[1][:, 0:128], T.Tri[:], T.Fw[:], False, True, ["Tri", "Fw"], ["P1"], 128)
         act(T.V0[:], P[1][:, 0:128], ["P1"], ["V0"], F.Identity, 0.5 + 32.5 / 16384, -1.0 / 16384)
         if t == 0:
-            mm(P[7][:, 0:128], T.o16[:], T.Id16[:], True, False, ["o16", "Id16"], ["P7"])
-            mm(P[7][:, 0:128], T.fo16[:], T.IdK[:, 0:128], False, True, ["fo16", "IdK0"], ["P7"])
-        if t == 1:
-            scaled(T.Zh[:, 288:432], zt(Z1), col(WU), ["Z1", "WU"], ["Zh2"])
-            scaled(bdv(1), T.BD[:], col(WAO), ["BD", "WAO"], ["BD1"])
-            wrap(P[7][:, 0:8], zh(2), lambda i: T.RXh[:, i:128:16], ["Zh2", "RXh"], ["P7"])
-            xb_clear(T.XBo, "XBo", T.boff[:, 0:12], "boff0")
-        scan(T.CE[:, 16:144], P[2][:, 0:128], T.c192[:], 0.0, A.add, A.min, ["P2", "c192"], ["CE"])
-        if t == 0:
-            ts(T.offx[:, 0:128], P[7][:, 0:128], 4096.0, 2048.0, A.add, A.min, ["P7"], ["offo"])
-        tt(T.HS[:], T.CE[:, 15:143], P[6][:, 0:128], A.max, ["CE", "CE0", "P6"], ["HS"])
-        ts(T.d0[:], T.colI[:], T.CE[:, 143:144], 1.0 / 16384, A.is_equal, A.max, ["colI", "CE"], ["d0"])
-        scan(T.H3[:], T.HD2[:, 0:128], T.HS[:], 2 * BB, A.add, A.max, ["HD2", "HS"], ["H3"])
-        if t == 0:
-            scaled(bdv(3), T.BD[:], 256.0, ["BD"], ["BD3"])
-            scaled(bdv(0), T.BD[:], col(WAE), ["BD", "WAE"], ["BD0"])
-            scaled(T.BDn[:], T.BD[:], -2048.0, ["BD"], ["BDn"])
-            xb_build(T.XBo, "XBo", 0, 0, 48, "offo")
-            iota(T.PFi[:], [[2, 32]], H0 + 64 * rank, 0, ["PFi"])
-            asel(T.M1t[:], T.BDn[:], [[1, 128]], A.is_gt, 0.0, 0, -1, ["BDn"], ["M1t"])
-            asel(T.M1[:], T.M1t[:], [[1, 128]], A.not_equal, 2048.0, 0, -1, ["M1t"], ["M1"])
-            iota(T.HM[:], [[0, 2080]], 0, 0, ["HM"], False)
-            dma("s", T.HM[7:128:16, 0:2048], T.hm[:], [], ["HM"], "hm", 16)
-            iota(T.BIG[:], [[0, 192]], 8388608, 0, ["BIG"])
-            iota(T.TS[:], [[0, 2048]], 4096, 0, ["TS"])
-        ts(T.coff[:], T.H3[:, 15:128:16], col(OFF), None, A.subtract, None, ["H3", "OFF"], ["coff"])
-        cp(T.WIN[:, 2304 * t:2304 * t + 2304].indirect(T.coff[:]), T.V0[:], ["V0", "coff"], [wk])
+            xb_build(1, 0, "offo")
+        scan(T.CE[:, 16:144], P[2][:, 0:128], T.c192[:], 0.0, A.add, A.min, ["P2", "c192"], ["CE"], 128)
+        tt(T.HS[:], T.CE[:, 15:143], P[6][:, 0:128], A.max, ["CE", "CE0", "P6"], ["HS"], 128)
+        ts(T.d0[:], T.colI[:], T.CE[:, 143:144], 1.0 / 16384, A.is_equal, A.max, ["colI", "CE"], ["d0"], 96)
+        hold(T.H4[:], T.HS[:], 128, ["HS"], ["H4"])
+        ts(T.coff[:], T.H4[:, 15:128:16], col(OFF), None, A.subtract, None, ["H4", "OFF"], ["coff"])
+        cp(T.WIN[:, 2304 * t:2304 * t + 2304].indirect(T.coff[:]), T.V0[:], ["V0", "coff"], [wk], sc(128))
         scan(T.SB[:], T.d0[:], T.WIN[:, 2304 * t:2304 * t + 192], 0.5, A.add, A.max, ["d0", wk], ["SB"])
-        mm(P[3][:, 0:192], bdv(3), T.SB[:], True, True, ["BD3", "SB"], ["P3"])
-        mm(P[4][:, 0:192], bdv(3), T.SB[:], True, True, ["BD3", "SB"], ["P4"])
+        mm(P[3][:, 0:192], bdv(B256), T.SB[:], True, True, ["BD%d" % B256, "SB"], ["P3"])
+        hold(T.SH[:], P[3][:, 0:192], 192, ["P3"], ["SH"])
+        ts(T.swg[:], T.SH[:, 15:192:16], col(OFS), 2048.0, A.subtract, A.min, ["SH", "c%d" % OFS], ["swg"])
+        XZk = ["XZ0", "XZ1", "XZ2"]
+        if t > 0:
+            cp(T.qA[:], T.DQ[:, 0:2064].indirect(T.swg[:]), DQk + ["swg"], ["qA"], ga(192))
+            act(T.XZ[:, 0:3072:16], XBt[odd][:, 0:2064].indirect(T.swg[:]), XBk[odd] + ["swg"] + XZk, ["XZ"], F.Copy, c=GAT * 192)
         if t == 0:
-            ts(col(OFS), col(OFF), 2048.0, None, A.add, None, ["OFF"], ["OFS"])
-            ts(col(OFS1), col(OFF), 2047.0, None, A.add, None, ["OFF"], ["OFS1"])
-        if t == 1:
-            cp(T.vw[:], P[7][:, 0:8], ["P7"], ["vw"])
-        scan(T.SH[:], T.HD2[:], P[3][:, 0:192], 2 * BB, A.add, A.max, ["HD2", "P3"], ["SH"])
-        ts(T.swg[:], T.SH[:, 15:192:16], col(OFS), 2048.0, A.subtract, A.min, ["SH", "OFS"], ["swg"])
-        act(T.srep[:], P[4][:, 0:192], ["P4"], ["srep"], F.Identity, -2048.0)
-        if t == 0:
-            act(T.mov[:], T.sq2[:], ["sq2", "srep"], ["mov"], F.Sign, T.srep[:, 191:192], -1.0)
-            ts(col(WOCC), Rr(2), Rr(3), None, A.add, None, ["R"], ["WOCC"])
-            xb_build(T.XBo, "XBo", 0, 48, 96, "offo")
-            ts(T.K2[:], T.jw[:], col(PM), col(OFS), A.add, A.add, ["jw", "PM", "OFS"], ["K2"])
-            ts(col(OFFA), col(OFF), -2064.0, None, A.add, None, ["OFF"], ["OFFA"])
-            ms(T.DS[:, 2048:2080], 0, ["DSa"])
-        if t == 1:
-            act(T.xv[:], T.XS[:, 0:2080].indirect(T.vw[:]), XSk + ["vw"], ["xv"], F.Copy)
-        cp(T.acol[:], T.TB[:, 0:GW].indirect(T.swg[:]), ["TB", "swg"], ["acol"])
-        mm(P[5][:, 0:192], bdv(odd), T.acol[:], True, True, ["BD%d" % odd, "acol"], ["P5"])
-        if t == 0:
-            mm(P[7][:, 0:128], T.o16[:], T.Id16[:], True, False, ["o16", "Id16"], ["P7"])
-            mm(P[7][:, 0:128], T.fe16[:], T.IdK[:, 0:128], False, False, ["fe16", "IdK0"], ["P7"])
-            mm(P[7][:, 0:128], T.IdK[:, 128:256], T.mov[:], False, True, ["mov", "IdK1"], ["P7"])
-        tt(T.swf[:], T.SH[:, 15:192:16], T.K2[:], A.min, ["SH", "K2"], ["swf"])
-        if not SPLIT:
-            ts(T.arep[:], P[5][:, 0:192], 2064.0, None, A.add, None, ["P5"], ["arep"])
-        scan(T.H2[:], T.HD2[:], P[5][:, 0:192], 2 * BB, A.add, A.max, ["HD2", "P5"], ["H2"])
-        ts(T.aw[:], T.H2[:, 15:192:16], col(OFFA), None, A.subtract, None, ["H2", "OFFA"], ["aw"])
-        if SPLIT:
-            act(T.XZ[:, 0:3072:16], T.XS[:, 0:2080].indirect(T.aw[:]), XSk + ["aw", "XZ0", "XZ1", "XZ2"], ["XZ"], F.Copy)
-            if t == 0:
-                xb_build(T.XBo, "XBv", 0, 96, 128, "offo")
+            cp(T.acol[:], T.TB[:, 0:GW].indirect(T.swg[:]), ["TB", "swg"], ["acol"], ga(192))
         else:
-            for c in range(6):
-                act(T.XA[:, 512 * c:512 * c + 512], T.XS[:, 0:2080].indirect(T.arep[:, 32 * c:32 * c + 32]), XSk + ["arep"], ["XA%d" % c], F.Copy)
-        if t == 0:
-            ts(col(BSEL), col(PM), -2048.0, -2048.0, A.mult, A.add, ["PM"], ["BSEL"])
-            ts(col(MA), Rr(0), Rr(1), Rr(8), A.add, A.add, ["R"], ["MA"])
-            ts(T.PAT[:], T.J16[:, 15:207], col(PM), BB, A.not_equal, A.mult, ["J16", "PM"], ["PAT"])
-            ts(T.offx[:, 128:256], P[7][:, 0:128], 8192.0, 2048.0, A.add, A.min, ["P7"], ["offe"])
-        tt(T.qx[:], T.DS[:].indirect(T.aw[:]), T.srep[:], A.add, ["DS", "DSa", "aw", "srep"], ["qx"])
-        ts(T.q32[:], T.qx[:], 2047, None, A.bitwise_and, None, ["qx"], ["q32"])
-        cp(T.qu[:], T.q32[:], ["q32"], ["qu"])
-        if t == 0 and not SPLIT:
-            xb_build(T.XBo, "XBv", 0, 96, 128, "offo", "v")
-
-        def extra():
-            ts(T.q1[:], T.qu[:], 1.0, None, A.add, None, ["qu"], ["q1"])
-            ts(swu, T.swf[:], col(OFS), None, A.subtract, None, ["swf", "OFS"], [sk])
-
-        def cmpv(a, b, c, xk):
-            tt(T.CMP[:, 16 * a:16 * b], XB[:, 0:2048].indirect(T.qu[:, a:b]), T.XA[:, 16 * a:16 * b], A.is_lt, XBk + ["qu", xk], [CMPk[c]])
-
-        def count(bank, a, b, ks):
-            wrap(P[bank][:, a:b], zw(Z1), lambda i: T.CMP[:, 16 * a + i:16 * b:16], ["Z1"] + ks, [pk(bank)], not SPLIT, True)
-
-        def choose(a, b, bc, bs, bf_, n, before=None):
-            mm(P[bs][:, a:b], T.Id16[:], T.q1[:, a:b], True, False, ["Id16", "q1"], [pk(bs)])
-            mm(P[bf_][:, a:b], bdv(3), T.SB[:, a:b], True, False, ["BD3", "SB"], [pk(bf_)])
-            if before:
-                before()
-            act(T.sg[:, a:b], P[bc][:, a:b], [pk(bc)], ["sg%d" % n], F.Sign, -9.5)
-            mm(P[bs][:, a:b], T.M1[:], T.sg[:, a:b], False, True, ["M1", "sg%d" % n], [pk(bs)])
-            mm(P[bf_][:, a:b], bdv(4), T.sg[:, a:b], False, True, ["BD4", "sg%d" % n], [pk(bf_)])
-            act(T.sel[:, a:b], P[bs][:, a:b], [pk(bs), "BSEL"], ["sel%d" % n], F.Relu, col(BSEL))
-            act(T.fb[:, a:b], P[bf_][:, a:b], [pk(bf_)], ["fb%d" % n], F.Relu, -2047.0 - 65536.0)
-
-        def keys(a, b, n, ks):
-            for k in ks:
-                if k == 3:
-                    mm(P[k][:, a:b], T.Id[:], T.PAT[:, a:b], True, False, ["Id", "PAT"], [pk(k)])
-                mm(P[k][:, a:b], T.BDh[:, 0:128], T.sel[:, a:b], k != 3, False, ["sel%d" % n, "BDh0"], [pk(k)])
-                mm(P[k][:, a:b], T.BDh[:, 128:256], T.fb[:, a:b], False, True, ["fb%d" % n, "BDh1"], [pk(k)])
-
-        def act_consts():
-            if t == 0:
-                scaled(bdv(4), T.BD[:], -4096.0, ["BD"], ["BD4"])
-                scaled(T.BDh[:, 0:128], T.BD[:], 1.0, ["BD"], ["BDh0"])
-                scaled(T.BDh[:, 128:256], T.BD[:], 0.0625, ["BD"], ["BDh1"])
-            act(T.acolA[:], T.acol[:], ["acol", "MA", "R"], ["acolA"], F.Identity, Rr(4 + t), col(MA))
-            if t == 0:
-                xb_build(T.XBe, "XBe", 128, 0, 10, "offe")
-
-        if SPLIT:
-            cut = 144
-
-            def pre(bank, a, b):
-                for i in range(16):
-                    mm(P[bank][:, i:16 * (b - a):16], T.Id[:], T.XZ[:, 16 * a:16 * b:16], i == 0, False, ["Id", "XZ"], [pk(bank)])
-
-            def gat(bank, a, b, c):
-                act(T.XA[:, 16 * a:16 * b], XB[:, 0:2048].indirect(T.qu[:, a:b]), XBk + ["qu"], ["XA%d" % c], F.Copy)
-
-            def dif(bank, a, b, c):
-                mm(P[bank][:, 0:16 * (b - a)], T.Idn[:], T.XA[:, 16 * a:16 * b], False, True, ["Idn", "XA%d" % c], [pk(bank)])
-
-            def sgn(bank, a, b, c):
-                act(T.CMP[:, 16 * a:16 * b], P[bank][:, 0:16 * (b - a)], [pk(bank)], [CMPk[c]], F.Sign, -TINY)
-
-            def spread(a, b, c):
-                scan(T.XA[:, 16 * a:16 * b], T.HOLD[:, 0:16 * (b - a)], T.XZ[:, 16 * a:16 * b], 0.0, A.mult, A.add, ["HOLD3", "XZ"], ["XA%d" % c])
-
-            pre(0, 0, 32)
-            gat(0, 0, 32, 3)
-            spread(32, 72, 0)
-            spread(104, 144, 1)
-            pre(1, 72, 104)
-            gat(1, 72, 104, 4)
-            dif(0, 0, 32, 3)
-            cmpv(32, 72, 0, "XA0")
-            pre(2, 144, 160)
-            dif(1, 72, 104, 4)
-            sgn(0, 0, 32, 3)
-            gat(2, 144, 160, 5)
-            spread(160, 192, 2)
-            mm(P[6][:, 0:144], T.Id[:], T.c65[:, 0:144], True, False, ["Id", "c65160"], ["P6"])
-            mm(P[4][:, 144:192], T.Id[:], T.c65[:, 144:192], True, False, ["Id", "c65160"], ["P4"])
-            for i in range(16):
-                mm(P[6][:, 0:72], zw(Z1)(i), T.CMP[:, i:1152:16], False, False, ["Z1", CMPk[0], CMPk[3]], ["P6"])
-            dif(2, 144, 160, 5)
-            sgn(1, 72, 104, 4)
-            cmpv(104, 144, 1, "XA1")
-            extra()
-            sgn(2, 144, 160, 5)
-            count(6, 72, 144, [CMPk[1], CMPk[4]])
-            act_consts()
-            cmpv(160, 192, 2, "XA2")
-            choose(0, cut, 6, 5, 0, 0)
-            choose(cut, 192, 4, 1, 2, 1, lambda: (count(4, cut, 192, [CMPk[2], CMPk[5]]), keys(0, cut, 0, [7])))
-            keys(cut, 192, 1, [7])
-            keys(0, cut, 0, [3])
-            keys(cut, 192, 1, [3])
-        else:
-            cut = 128
-            for c in range(6):
-                cmpv(32 * c, 32 * c + 32, c, "XA%d" % c)
-                if c == 0:
-                    extra()
-                if c in (1, 3):
-                    count(6, 32 * c - 32, 32 * c + 32, CMPk[c - 1:c + 1])
-                if c == 3:
-                    act_consts()
-                    choose(0, cut, 6, 5, 0, 0)
-            keys(0, cut, 0, [7, 3])
-            choose(cut, 192, 4, 1, 6, 1, lambda: count(4, cut, 192, CMPk[4:6]))
-            keys(cut, 192, 1, [7, 3])
-        cp(T.TB[:].indirect(swu), T.acolA[:], ["acolA", sk], ["TB"])
-        if t == 0:
-            ms(T.H[:, 0:1], 3 * BB, ["H0"])
-            ts(col(OFF1), col(OFF), 1.0, None, A.add, None, ["OFF"], ["OFF1"])
-            ts(col(MV), col(MA), col(WOCC), None, A.add, None, ["MA", "WOCC"], ["MV"])
-            ts(zt(ZU), zt(Z1), col(WU), None, A.mult, None, ["Z1", "WU"], ["ZU"])
-            ts(col(I192), col(PM), 192.0, None, A.mult, None, ["PM"], ["I192"])
-            ts(col(WE0), Rr(4), col(WOCC), None, A.add, None, ["R", "WOCC"], ["WE0"])
-        if t == 1:
-            cp(T.XBo[:].indirect(T.roff[:, 0:8]), T.xv[:], ["xv", "roff0"], ["XBo"])
+            act(T.acol[:], T.TB[:, 0:GW].indirect(T.swg[:]), ["TB", "swg"], ["acol"], F.Copy, c=GAT * 192)
+        mm(P[3][:, 0:192], bdv(odd), T.acol[:], True, True, ["BD%d" % odd, "acol"], ["P3"])
+        hold(T.HA[:], P[3][:, 0:192], 192, ["P3"], ["HA"])
+        ts(aw, T.HA[:, 15:192:16], col(OFA0), None, A.subtract, None, ["HA", "c%d" % OFA0], [ak])
         if t == 2:
-            cp(T.hcol[:], T.HM[:].indirect(T.aw[:]), ["HM", "aw"], ["hcol"])
-        sf = ["fb0", "fb1", "BDh0"]
+            act(T.ua[:], P[3][:, 0:192], ["P3"], ["ua"], F.Identity, 2064.0, c=192)
+        tt(T.swf[:], T.SH[:, 15:192:16], K2, A.min, ["SH", "K2"], ["swf"])
+        ts(swu, T.swf[:], col(OFS), None, A.subtract, None, ["swf", "c%d" % OFS], [sk])
+        if t == 0:
+            mm(P[4][:, 0:192], bdv(B256), T.SB[:], True, True, ["BD%d" % B256, "SB"], ["P4"])
+            act(T.srep[:], P[4][:, 0:192], ["P4"], ["srep"], F.Identity, -2048.0, c=192)
+            act(T.XZ[:, 0:3072:16], T.XS[:, 0:2080].indirect(aw), XSk + [ak] + XZk, ["XZ"], F.Copy, c=GAT * 192)
+            tt(T.qx[:], T.DS[:].indirect(aw), T.srep[:], A.add, DSk + [ak, "srep"], ["qx"], ga(192))
+            ts(T.q32[:], T.qx[:], 2047, None, A.bitwise_and, None, ["qx"], ["q32"], 192)
+            cp(T.qA[:], T.q32[:], ["q32"], ["qA"], 192)
+            act(T.mov[:], T.sq2[:], ["sq2", "srep"], ["mov"], F.Sign, T.srep[:, 191:192], -1.0)
+            mm(P[7][:, 0:128], T.Id16[:], T.Uw[:], True, False, ["Uw", "Id16"], ["P7"], 128)
+            mm(P[7][:, 0:128], T.IdK[:, 128:256], T.Fw[:], False, False, ["Fw", "IdK1"], ["P7"], 128)
+            mm(P[7][:, 0:128], T.IdK[:, 0:128], T.mov[:], False, True, ["mov", "IdK0"], ["P7"], 128)
+            ts(T.offx[:, 128:256], P[7][:, 0:128], 8192.0, 2048.0, A.add, A.min, ["P7"], ["offe"], 128)
+            xb_build(0, 128, "offe")
+            w = 2048 // NQ
+            for c in range(NQ):
+                tt(T.DQ[:, w * c:w * c + w], T.DS[:].indirect(T.offx[:, 256 + w * c // 16:256 + (w * c + w) // 16]), T.SQ[:, w * c:w * c + w], A.add,
+                   DSk + SQk + ["offu"], [DQk[c]], ga(w))
+                row("DQ")
+        if t == 1:
+            xb_clear(1, T.endu[:, 0:12], "endu0")
+            xb_clear(1, swu, sk)
+        ts(T.q1[:], T.qA[:], 1.0, None, A.add, None, ["qA"], ["q1"], 96)
+
+        def cmpv(a, b, c):
+            scan(T.XA[:, 16 * a:16 * b], T.HOLD[:, 0:16 * (b - a)], T.XZ[:, 16 * a:16 * b], 0.0, A.mult, A.add, HOLDk + ["XZ"], ["XA%d" % c], 8 * (b - a))
+            tt(T.CMP[:, 16 * a:16 * b], XB[:, 0:2048].indirect(T.qA[:, a:b]), T.XA[:, 16 * a:16 * b], A.is_lt, XK + ["qA", "XA%d" % c], [CMPk[c]], ga(16 * (b - a)))
+            row("cmp")
+
+        mms([(P[5][:, 0:128], T.XZ[:, 0:2048:16], T.Id[:], True, True), (P[5][0:64, 128:256], T.XZ[:, 2048:3072:16], T.Id[:], True, True)], ["Id", "XZ"], ["P5"], 128)
+        act(T.XT[:, 0:128], P[5][:, 0:128], ["P5"], ["XT0"])
+        act(T.XT[0:64, 128:256], P[5][0:64, 128:256], ["P5"], ["XT1"])
+
+        def cmpa(bank, a, b, c):
+            n, h = 16 * (b - a), a // 128
+            e0 = 512 * (a == 72) + 16 * (a % 128 % 72)
+            mm(P[bank][:, 0:n], T.XT[0:128 - 64 * h, 128 * h:128 * h + 128], T.SP[0:128 - 64 * h, e0:e0 + n], True, False, ["SP0", "SP1", "XT%d" % h], [pk(bank)], n)
+            act(T.XA[:, 16 * a:16 * b], XB[:, 0:2048].indirect(T.qA[:, a:b]), XK + ["qA"], ["XA%d" % c], F.Copy, c=GAT * n)
+            row("gat")
+            mm(P[bank][:, 0:n], T.Idn[:], T.XA[:, 16 * a:16 * b], False, True, ["Idn", "XA%d" % c], [pk(bank)], n)
+            act(T.CMP[:, 16 * a:16 * b], P[bank][:, 0:n], [pk(bank)], [CMPk[c]], F.Sign, -TINY, c=n)
+
+        def count(bank, a, b, ks, stop):
+            wrap(P[bank][:, a:b], zw(Z1), lambda i: T.CMP[:, 16 * a + i:16 * b:16], ["Z1"] + ks, [pk(bank)], b - a, False, stop)
+
+        def choose(a, b, bc, bs, bf_, n):
+            mm(P[bs][:, a:b], T.Id16[:], T.q1[:, a:b], True, False, ["Id16", "q1"], [pk(bs)], b - a)
+            mm(P[bf_][:, a:b], bdv(B256), T.SB[:, a:b], True, False, ["BD%d" % B256, "SB"], [pk(bf_)], b - a)
+            act(T.sg[:, a:b], P[bc][:, a:b], [pk(bc)], ["sg%d" % n], F.Sign, -9.5, c=b - a)
+            mm(P[bs][:, a:b], T.M1[:], T.sg[:, a:b], False, True, ["M1", "sg%d" % n], [pk(bs)], b - a)
+            mm(P[bf_][:, a:b], bdv(B4096N), T.sg[:, a:b], False, True, ["BD%d" % B4096N, "sg%d" % n], [pk(bf_)], b - a)
+            if n:
+                ts(T.sel[:, a:b], P[bs][:, a:b], col(BSEL), 0.0, A.add, A.max, [pk(bs), "BSEL"], ["sel%d" % n], b - a)
+            else:
+                act(T.sel[:, a:b], P[bs][:, a:b], [pk(bs), "BSEL"], ["sel%d" % n], F.Relu, col(BSEL), c=b - a)
+            act(T.fb[:, a:b], P[bf_][:, a:b], [pk(bf_)], ["fb%d" % n], F.Relu, -2047.0 - 65536.0, c=b - a)
+
+        def keys(k, a, b, n, first):
+            if k == 3 and first:
+                mm(P[k][:, 0:192], T.Id[:], T.PAT[:], True, False, ["Id", "PAT"], [pk(k)])
+            mms([(P[k][:, a:b], T.BDh[:, 0:128], T.sel[:, a:b], first and k != 3, False), (P[k][:, a:b], T.BDh[:, 128:256], T.fb[:, a:b], False, not first)],
+                ["sel%d" % n, "fb%d" % n, "BDh0", "BDh1"], [pk(k)], b - a)
+
+        cut = 144
+        cmpa(0, 0, 32, 3)
+        cmpa(1, 72, 104, 4)
+        cmpa(2, 144, 160, 5)
+        for c, (a, b) in enumerate(VSH):
+            cmpv(a, b, c)
+        mm(P[6][:, 0:cut], T.Id[:], T.c65[:, 0:cut], True, False, ["Id"] + c65k, ["P6"], cut)
+        mm(P[4][:, cut:192], T.Id[:], T.c65[:, cut:192], True, False, ["Id"] + c65k, ["P4"], 64)
+        count(6, 0, 72, [CMPk[0], CMPk[3]], False)
+        count(6, 72, cut, [CMPk[1], CMPk[4]], True)
+        count(4, cut, 192, [CMPk[2], CMPk[5]], True)
+        choose(0, cut, 6, 5, 0, 0)
+        choose(cut, 192, 4, 1, 2, 1)
+        for k in (7, 0, 3):
+            keys(k, 0, cut, 0, True)
+            keys(k, cut, 192, 1, False)
+        cp(T.TB[:].indirect(swu), T.GH[:, 192 * t:192 * t + 192], ["GH%d" % t, sk], ["TB"], sc(192))
+        act(T.hcol[:], T.HM[:].indirect(aw), ["HM", ak], ["hcol"], F.Copy, c=GAT * 192)
+        mm(P[1][:, 0:192], bdv(BIRTH), T.acol[:], True, False, ["BD%d" % BIRTH, "acol"], ["P1"])
+        mm(P[1][:, 0:192], T.BDh[:, 0:128], T.fb[:], False, False, ["fb0", "fb1", "BDh0"], ["P1"])
 
         def early1():
-            ts(T.atw[:], T.H[:, 16:193:16], col(OFF1), 2048.0, A.subtract, A.min, ["H", "OFF1"], ["atw"])
-            cp(T.vcol[:], T.TB[:, 0:GW].indirect(T.atw[:]), ["TB", "atw"], ["vcol"])
-            wrap(P[0][:, 0:12], zw(ZU), lambda i: T.vcol[:, i:192:16], ["ZU", "vcol"], ["P0"])
-            act(T.atr[:], P[7][:, 0:192], ["P7"], ["atr"], F.Identity, -1.0)
+            ts(T.atw[:], T.H[:, 16:193:16], col(OFF1), 2048.0, A.subtract, A.min, ["H", "c%d" % OFF1], ["atw"])
             if t == 0:
-                scaled(bdv(2), T.BD[:], Rr(0), ["BD", "R"], ["BD2"])
-                scaled(T.PF[:], T.PFi[:], Rr(7), ["PFi", "R"], ["PF"])
-                for k in range(12):
-                    c0 = 960 * (k // 4) + 192 * (k % 4)
-                    dma("s", T.MSG[:, c0:c0 + 32], T.PF[:], ["PF"], ["MSG%d" % (k // 4)], "pf", 192)
-            mm(P[1][:, 0:192], bdv(2), T.acol[:], True, False, ["BD2", "acol"], ["P1"])
-            mm(P[1][:, 0:192], T.BDh[:, 0:128], T.fb[:], False, False, sf, ["P1"])
+                ts(T.qx[:], T.DQ[:, 0:2064].indirect(T.atw[:]), 2047, None, A.bitwise_and, None, DQk + ["atw"], ["qx"], ga(192))
+                cp(T.qB[:], T.qx[:], ["qx"], ["qB"], 192)
+                for c in range(NQ):
+                    ts(T.DQ[:, w * c:w * c + w], T.DQ[:, w * c:w * c + w], 2047, None, A.bitwise_and, None, [DQk[c]], [DQk[c]], w)
+                    row("DQ")
+            else:
+                cp(T.qB[:], T.DQ[:, 0:2064].indirect(T.atw[:]), DQk + ["atw"], ["qB"], ga(192))
+            scaled(T.vcol[:], T.TB[:, 0:GW].indirect(T.atw[:]), col(MV), ["TB", "atw", "MV"], ["vcol"], GAT * 192)
 
-        def late1():
-            act(T.vcf[:], T.vcol[:], ["vcol", "MV"], ["vcf"], F.Identity, 0.0, col(MV))
-            if t == 0:
-                xb_build(T.XBe, "XBe", 128, 24, 44, "offe")
-
-        lk = (0, 64, 128, 144, 192)
-
-        def look(c, e):
-            src = T.TB[:, 0:GW].indirect(T.qu[:, lk[c]:lk[c + 1]])
+        dedupe(7, 0, 3, 1, bdv(B256), "BD%d" % B256, early1, True, NB[0])
+        for c, (a, b, e) in enumerate(LOOKS):
+            src, n = T.TB[:, 0:GW].indirect(T.qB[:, a:b]), 16 * (b - a)
             if e == "a":
-                act(T.CMP[:, 16 * lk[c]:16 * lk[c + 1]], src, ["TB", "qu", "WE%d" % t], [EFk[c]], F.Identity, 0.0, col(WE0 + t))
+                act(T.CMP[:, 16 * a:16 * b], src, ["TB", "qB", "WE%d" % t] + CMPk, ["EF%d" % c], F.Identity, 0.0, col(WE0 + t), GAT * n)
             else:
-                ts(T.CMP[:, 16 * lk[c]:16 * lk[c + 1]], src, col(WE0 + t), None, A.mult, None, ["TB", "qu", "WE%d" % t], [EFk[c]])
-
-        def mid1(b):
-            if b == NB - 2:
-                cp(T.whow[:], P[0][:, 0:12], ["P0"], ["whow"])
-            dup_mm(1, bdv(3), "BD3", [-1, 0] if b == 0 else [b])
-
-        dedupe(7, 7, 3, 1, None, None, early1, mid1, late1)
-        dup_mm(1, bdv(3), "BD3", list(range(NB, 11)), True)
-        tt(T.qx[:], T.DS[:].indirect(T.whow[:]), T.atr[:], A.add, ["DS", "DSa", "whow", "atr"], ["qx"])
-        ts(T.q32[:], T.qx[:], 2047, None, A.bitwise_and, None, ["qx"], ["q32"])
-        cp(T.qu[:], T.q32[:], ["q32"], ["qu"])
-        for c in range(3):
-            look(c, "a")
-        ts(T.G[:], P[1][:, 0:192], 4.0, col(PM), A.min, A.is_equal, ["P1", "PM"], ["G"])
-        ts(T.q1[:], T.qu[:], 1.0, None, A.add, None, ["qu"], ["q1"])
+                ts(T.CMP[:, 16 * a:16 * b], src, col(WE0 + t), None, A.mult, None, ["TB", "qB", "WE%d" % t] + CMPk, ["EF%d" % c], ga(n))
+            row("look" + e)
+        ts(T.q2[:], T.qB[:], 1.0, None, A.add, None, ["qB"], ["q2"], 96)
+        mm(P[6][:, 0:192], T.Id16[:], T.q2[:], True, False, ["Id16", "q2"], ["P6"])
+        for a, b in ((0, 64), (64, 128), (128, 192)):
+            ks = ["EF%d" % c for c, x in enumerate(LOOKS) if x[0] < b and x[1] > a]
+            wrap(P[6][:, a:b], lambda i: T.TS[:, 128 * i:128 * i + 128], lambda i: T.CMP[:, 16 * a + i:16 * b:16], TSk + ks + CMPk, ["P6"], 64, False, b == 192)
+        ts(T.G[:], P[1][:, 0:192], 4.0, col(PM), A.min, A.is_equal, ["P1", "PM"], ["G"], 192)
         scan(P[4][:, 0:192], T.G[:], T.G[:], col(I192), A.add, A.max, ["G", "I192"], ["P4"])
-        ts(w12(2), T.swf[:], col(OFS1), None, A.subtract, None, ["swf", "OFS1"], ["s1"])
-        tt(T.z[:], P[4][:, 0:192], T.G[:], A.mult, ["P4", "G"], ["z"])
+        tt(T.z[:], P[4][:, 0:192], T.G[:], A.mult, ["P4", "G"], ["z"], 192)
         mm(P[5][:, 0:192], T.BDh[:, 0:128], T.z[:], True, True, ["BDh0", "z"], ["P5"])
-        if t < 2:
-            cp(T.hcol[:], T.HM[:].indirect(T.aw[:]), ["HM", "aw"], ["hcol"])
-        if t == 0:
-            ts(T.K3[:], T.jw[:], col(PM), float(BD0 + 1 - 2048), A.add, A.add, ["jw", "PM"], ["K3"])
-        tt(w12(1), T.keyw[:], T.K3[:], A.subtract, ["keyw", "K3"], ["w1"])
-        tt(w12(4), T.keyw[:], w12(2), A.subtract, ["keyw", "s1"], ["w4"])
-        scan(T.H2[:], T.HD2[:], P[5][:, 0:192], 2 * BB, A.add, A.max, ["HD2", "P5"], ["H2"])
-        ts(T.posu[:], T.H2[:, 15:192:16], col(OFF1), None, A.subtract, None, ["H2", "OFF1"], ["posu"])
-        ts(w12(0), T.H2[:, 15:192:16], col(OFF), 768.0, A.subtract, A.is_le, ["H2", "OFF"], ["won"])
-        op("v", lambda: V.tensor_tensor(T.MSG[:, 960 * t:960 * t + 960].indirect(T.posu[:]), T.vcf[:], T.hcol[:], A.add), ["vcf", "hcol", "posu"], [mk])
-        wait("c", lastw[mk])
+        hold(T.H2[:], P[5][:, 0:192], 192, ["P5"], ["H2"])
+        ts(T.posu[:], T.H2[:, 15:192:16], col(OFF1), None, A.subtract, None, ["H2", "c%d" % OFF1], ["posu"])
+        tt(T.MSG[:, 960 * t:960 * t + 960].indirect(T.posu[:]), T.vcol[:], T.hcol[:], A.add, ["vcol", "hcol", "posu"], mk, sc(192))
+        arr = sum(len(topo.engines(T.cores[p], core)) for p in peers)
         for p in peers:
-            dst = T.cores[p]
-            rid, pid = topo.addr(dst, core)
-            g.remote_dma(T.RX[:, 128 * t + 32 * rank:128 * t + 32 * rank + 32], T.MSG[:, 960 * t + 192 * p:960 * t + 192 * p + 32],
-                         T.sem["arr%d" % t], T.sem.sent, pid, rid, topo.mask(core, dst))
-            sent[0] += len(topo.engines(core, dst))
-        if t == 0:
-            asel(T.TS[:], T.TS[:], [[-1, 16], [0, 8], [1, 16]], A.is_ge, 0.0, 0, 0, ["TS"], ["TS"])
-            asel(T.TS[:], T.TS[:], [[-1, 16], [0, 8], [1, 16]], A.not_equal, -4096.0, 0, 0, ["TS"], ["TS"])
-            asel(T.TS[:], T.TS[:], [[0, 16], [-16, 8], [0, 16]], A.is_ge, 0.0, 0, 1, ["TS"], ["TS"])
-            asel(T.TS[:], T.TS[:], [[0, 16], [16, 8], [0, 16]], A.is_ge, 0.0, 15, -1, ["TS"], ["TS"])
-        look(3, "v")
-        mm(P[6][:, 0:192], T.Id16[:], T.q1[:], True, False, ["Id16", "q1"], ["P6"])
-        for a, b, ks in ((0, 64, EFk[0:1]), (64, 128, EFk[1:2]), (128, 192, EFk[2:4])):
-            if t == 0:
-                wrap(P[0][:, a:b], zw(Z1), lambda i: T.CMP[:, 16 * a + i:16 * b:16], ["Z1"] + ks, ["P0"])
-            else:
-                wrap(P[6][:, a:b], lambda i: T.TS[:, 128 * i:128 * i + 128], lambda i: T.CMP[:, 16 * a + i:16 * b:16], ["TS"] + ks, ["P6"], False, b == 192)
-        tt(w12(3), w12(1), w12(0), A.mult, ["w1", "won"], ["w3"])
-        tt(w12(6), w12(4), w12(0), A.mult, ["w4", "won"], ["w6"])
-        tt(w12(5), w12(3), T.K3[:], A.add, ["w3", "K3"], ["w5"])
-        tt(w12(7), w12(6), w12(2), A.add, ["w6", "s1"], ["stay"])
-        ts(boff, w12(5), -1.0, None, A.add, None, ["w5"], [bk])
-        cp(T.TB[:].indirect(boff), T.ZR[:], ["ZR", bk], ["TB"])
+            def send(p=p, t=t):
+                dst = T.cores[p]
+                rid, pid = topo.addr(dst, core)
+                g.remote_dma(T.RX[:, 128 * t + 32 * rank:128 * t + 32 * rank + 32], T.MSG[:, 960 * t + 192 * p:960 * t + 192 * p + 32],
+                             T.sem["arr%d" % t], T.sem.sent, pid, rid, topo.mask(core, dst))
+            op("c", send, mk, ["RXr%d" % t], 0.25 + (1.0 if t == 0 and p == peers[0] else 0.0), 1.4, ("arr%d" % t, arr))
         c0 = 128 * t + 32 * rank
-        act(T.RX[:, c0:c0 + 32], T.MSG[:, 960 * t + 192 * rank:960 * t + 192 * rank + 32], [mk], ["RX%d" % t])
+        act(T.RX[:, c0:c0 + 32], T.MSG[:, 960 * t + 192 * rank:960 * t + 192 * rank + 32], mk, ["RX%d" % t], c=64)
+        RX, RXk = T.RX[:, 128 * t:128 * t + 128], ["RX%d" % t, "RXr%d" % t]
+        ts(w12(0), T.H2[:, 15:192:16], col(OFF), 768.0, A.subtract, A.is_le, ["H2", "OFF"], ["won"])
+        ts(w12(2), T.swf[:], col(OFS), None, A.subtract, None, ["swf", "c%d" % OFS], ["s0"])
+        tt(w12(1), T.keyw[:], K3, A.subtract, ["keyw", "K3"], ["w1"])
+        tt(w12(3), w12(1), w12(0), A.mult, ["w1", "won"], ["w3"])
+        tt(w12(5), w12(3), K3, A.add, ["w3", "K3"], ["w5"])
+        ts(boff, w12(5), -1.0, None, A.add, None, ["w5"], [bk])
+        ts(w12(7), T.keyw[:], -1.0, None, A.add, None, ["keyw"], ["w7"])
+        tt(w12(4), w12(7), w12(2), A.subtract, ["w7", "s0"], ["w4"])
+        tt(w12(6), w12(4), w12(0), A.mult, ["w4", "won"], ["w6"])
+        stay = T.H5[:, 61:624:48]
+        tt(stay, w12(6), w12(2), A.add, ["w6", "s0"], ["stay"])
+        cp(T.TB[:].indirect(boff), T.ZR[:], ["ZR", bk], ["TB"], sc(192))
         if t == 0:
-            scaled(T.BDh[:, 256:384], T.BD[:], Rr(7), ["BD", "R"], ["BDh2"])
-            xb_build(T.XBe, "XBe", 128, 10, 24, "offe")
-        if t == 0:
-            act(T.sg[:], P[0][:, 0:192], ["P0"], ["sg0", "sg1"], F.Identity, 1.0, -2.0)
-            mm(P[6][:, 0:192], T.M1[:], T.sg[:], False, True, ["M1", "sg0", "sg1"], ["P6"])
-            act(T.sel[:], P[6][:, 0:192], ["P6", "BSEL"], ["sel0", "sel1"], F.Relu, col(BSEL))
-        else:
-            act(T.sel[:], P[6][:, 0:192], ["P6", "BS2"], ["sel0", "sel1"], F.Relu, col(BS2))
+            xb_clear(1, boff, bk)
+        if t == 2:
+            for c in range(4):
+                k = (0, 3)[c & 1]
+                mm(P[k][:, 0:512], bdv(BY), T.TB[:, 512 * c:512 * c + 512], True, True, ["BD%d" % BY, "TB"], [pk(k)], 512)
+                act(T.Y[:, 512 * c:512 * c + 512], P[k][:, 0:512], [pk(k)], ["Y%d" % c], F.Identity, 2048.0, c=512)
+                row("Y")
+        act(T.sel[:], P[6][:, 0:192], ["P6", "BS2"], ["sel0", "sel1"], F.Relu, col(BS2), c=192)
         mm(P[4][:, 0:192], T.Id[:], T.PAT[:], True, False, ["Id", "PAT"], ["P4"])
-        for k in (1, 4):
+        for k in (1, 6, 4):
             mm(P[k][:, 0:192], T.BDh[:, 0:128], T.sel[:], k != 4, True, ["sel0", "sel1", "BDh0"], [pk(k)])
-        if t == 0:
-            ts(col(WO2), col(WOCC), float(GW), None, A.mult, None, ["WOCC"], ["WO2"])
-            ts(col(NOCC), col(WOCC), -1.0, None, A.mult, None, ["WOCC"], ["NOCC"])
-            ts(col(OFFM), col(OFF), -1.0, None, A.add, None, ["OFF"], ["OFFM"])
+        mm(P[5][:, 0:192], T.Id[:], T.PATn[:], True, False, ["Id", "PATn"], ["P5"])
+        mm(P[5][:, 0:192], bdv(BOCC), T.acol[:], False, False, ["BD%d" % BOCC, "acol"], ["P5"])
+        dedupe(1, 6, 4, 5, bdv(BNEG), "BD%d" % BNEG, lambda: None, False, NB[1])
+        ts(T.EQ[:, 2304:2496], T.keyr[:], 0.0, None, A.is_equal, None, ["keyr"], ["EQ12"], 96)
+        mm(P[5][:, 0:192], bdv(BNEG), T.EQ[:, 2304:2496], False, True, ["BD%d" % BNEG, "EQ12"], ["P5"])
+        ts(w12(7), T.keyw[:], -1.0, None, A.add, None, ["keyw"], ["w7"])
+        tt(T.D3[:, 1:36:3], w12(7), stay, A.subtract, ["w7", "stay"], ["D3"])
+        mm(P[2][:, 0:128], bdv(BHOME), RX, True, True, ["BD%d" % BHOME] + RXk, ["P2"], 128)
+        mm(P[7][:, 0:128], bdv(BHOME), RX, True, False, ["BD%d" % BHOME] + RXk, ["P7"], 128)
+        hold(T.H4[:], P[2][:, 0:128], 128, ["P2"], ["H4"])
+        ts(T.hwu[:], T.H4[:, 15:128:16], col(OFF), None, A.subtract, None, ["H4", "OFF"], ["hwu"])
+        act(T.hg[:], T.TB[:, 0:GW].indirect(T.hwu[:]), ["TB", "hwu"], ["hg"], F.Copy, c=GAT * 128)
+        mm(P[7][:, 0:128], bdv(BGW), T.hg[:], False, True, ["BD%d" % BGW, "hg"], ["P7"], 128)
+        hold(T.H4[:], P[7][:, 0:128], 128, ["P7"], ["H4"])
+        ts(roff, T.H4[:, 15:128:16], col(OFF), None, A.subtract, None, ["H4", "OFF"], [rk])
+        scan(T.H5[:, 0:576:3], T.HZ[:], P[5][:, 0:192], 0.0, A.mult, A.max, ["HZ", "P5"], ["go"])
+        scan(T.E3[:], T.D3[:], T.H5[:, 45:621:16], 0.0, A.mult, A.add, ["D3", "D3a", "D3b", "go", "stay", "H5z"], ["E3"], 64)
+        cp(endu, T.E3[:, 1:36:3], ["E3"], [ek])
+        if t < 2:
+            cp(T.TB[:].indirect(roff), RX, RXk + [rk], ["TB"], sc(128))
+            cp(T.TB[:].indirect(endu), T.acol[:], ["acol", ek], ["TB"], sc(192))
+            wrap(P[0][:, 0:8], zw(ZU), lambda i: T.RX[:, 128 * t + i:128 * t + 128:16], ["ZU"] + RXk, ["P0"], 64)
+            cp(T.vw[:], P[0][:, 0:8], ["P0"], ["vw"])
+            act(T.hf[:], P[2][:, 0:128], ["P2"], ["hf"])
+            act(T.xv[:], T.XS[:, 0:2080].indirect(T.vw[:]), XSk + ["vw"], ["xv"], F.Copy, c=GAT * 128)
+            cp(XB[:].indirect(roff), T.xv[:], ["xv", rk], XK, sc(128))
+            tt(T.qy[:, 0:128], T.DS[:].indirect(T.vw[:]), T.hf[:], A.add, DSk + ["vw", "hf"], ["qy"], ga(128))
+            ts(T.qz[:, 0:128], T.qy[:, 0:128], 2047, None, A.bitwise_and, None, ["qy"], ["qz"], 128)
+            cp(T.DQ[:].indirect(roff), T.qz[:, 0:128], ["qz", rk], DQk, sc(128))
+        else:
+            Yk = ["Y%d" % c for c in range(4)]
+            mm(P[2][:, 0:128], bdv(BU), RX, True, True, ["BD%d" % BU] + RXk, ["P2"], 128)
+            act(T.hf[:], P[2][:, 0:128], ["P2"], ["hf"])
+            cp(T.Y[:].indirect(roff), T.hf[:], ["hf", rk], Yk, sc(128))
+            cp(T.Y[:].indirect(endu), T.ua[:], ["ua", ek], Yk, sc(192))
+            for h in range(2):
+                dma("sa"[h], T.y[:, 1024 * h:1024 * h + 1024], T.Y[h:128:16, 1024 * h:1024 * h + 1024], Yk, ["y"], "out", 2.0)
 
-        def early2():
-            if t == 0:
-                scaled(bdv(5), T.BD[:], col(NOCC), ["BD", "NOCC"], ["BD5"])
-            mm(P[5][:, 0:192], bdv(5), T.acol[:], True, False, ["BD5", "acol"], ["P5"])
-            wait("a", ("arr%d" % t, sum(len(topo.engines(T.cores[p], core)) for p in peers)))
-            act(T.RXh[:], T.RX[:, 128 * t:128 * t + 128], ["RX%d" % t], ["RXh"])
+    start = put_in_order(ops)
+    total, cnt, tok, seen = {}, {"v": 0, "a": 0, "p": 0, "c": 0}, {}, {}
+    for o in ops:
+        if o["sem"]:
+            s, n = o["sem"]
+            total[s] = n if s.startswith("arr") else total.get(s, 0) + n
 
-        def late2():
-            if t == 0:
-                scaled(bdv(6), T.BD[:], col(WO2), ["BD", "WO2"], ["BD6"])
+    def wait(e, s, n):
+        if seen.get((e, s), 0) < n:
+            seen[(e, s)] = n
+            Q[e].wait_ge(T.sem[s], n)
 
-        def mid2(b):
-            dup_mm(5, T.BD[:], "BD", [-1, 0] if b == 0 else [b])
-            if b == 2:
-                mm(P[2][:, 0:128], T.BDh[:, 256:384], T.RXh[:], True, True, ["BDh2", "RXh"], ["P2"])
-                mm(P[7][:, 0:128], T.BDh[:, 256:384], T.RXh[:], True, False, ["BDh2", "RXh"], ["P7"])
-
-        dedupe(1, 1, 4, 5, None, None, early2, mid2, late2)
-        ts(T.EQ[:, 2304:2496], T.keyr[:], 0.0, None, A.is_equal, None, ["keyr"], ["EQ12"])
-        dup_mm(5, T.BD[:], "BD", list(range(NB, 11)))
-        mm(P[5][:, 0:192], T.BD[:], T.EQ[:, 2304:2496], False, True, ["BD", "EQ12"], ["P5"])
-        scan(T.H3[:], T.HD2[:, 0:128], P[2][:, 0:128], 2 * BB, A.add, A.max, ["HD2", "P2"], ["H3"])
-        tt(w12(1), T.keyw[:], w12(7), A.subtract, ["keyw", "stay"], ["w1"])
-        ts(T.hwu[:], T.H3[:, 15:128:16], col(OFF), None, A.subtract, None, ["H3", "OFF"], ["hwu"])
-        act(T.hg[:], T.TB[:, 0:GW].indirect(T.hwu[:]), ["TB", "hwu"], ["hg"], F.Copy)
-        mm(P[7][:, 0:128], bdv(6), T.hg[:], False, True, ["BD6", "hg"], ["P7"])
-        if t == 0:
-            ts(col(WAO), Rr(3), -2064.0, col(WU), A.mult, A.add, ["R", "WU"], ["WAO"])
-            scaled(zt(ZFO), zt(Z1), Rr(3), ["Z1", "R"], ["Zf"])
-            xb_build(T.XBe, "XBe", 128, 44, 128, "offe")
-        scan(T.H2[:], T.HD2[:], P[5][:, 0:192], 2 * BB, A.add, A.max, ["HD2", "P5"], ["H2"])
-        ts(w12(3), T.H2[:, 15:192:16], col(OFFM), None, A.is_equal, None, ["H2", "OFFM"], ["w3"])
-        tt(w12(4), w12(3), w12(1), A.mult, ["w3", "w1"], ["w4"])
-        scan(T.H3[:], T.HD2[:, 0:128], P[7][:, 0:128], 2 * BB, A.add, A.max, ["HD2", "P7"], ["H3"])
-        tt(w12(5), w12(4), w12(7), A.add, ["w4", "stay"], ["w5"])
-        ts(roff, T.H3[:, 15:128:16], col(OFF), None, A.subtract, None, ["H3", "OFF"], [rk])
-        ts(endu, w12(5), -1.0, None, A.add, None, ["w5"], [ek])
-        cp(T.TB[:].indirect(roff), T.RX[:, 128 * t:128 * t + 128], ["RX%d" % t, "RXh", rk], ["TB"])
-        cp(T.TB[:].indirect(endu), T.acol[:], ["acol", ek], ["TB"])
-        if t == 0:
-            ts(col(BS2), col(PM), -4096.0, None, A.mult, None, ["PM"], ["BS2"])
-            ts(col(WE1), Rr(5), col(WOCC), None, A.add, None, ["R", "WOCC"], ["WE1"])
-            ts(col(WE2), Rr(6), col(WOCC), None, A.add, None, ["R", "WOCC"], ["WE2"])
-            ts(col(WY), col(WOCC), -2048.0, col(WU), A.mult, A.add, ["WOCC", "WU"], ["WY"])
-        if t == 1:
-            scaled(zt(ZFE), zt(Z1), Rr(2), ["Z1", "R"], ["Zf"])
-            xb_clear(T.XBo, "XBo", T.endu[:, 0:12], "endu0")
-            xb_clear(T.XBo, "XBo", swu, sk)
-            scaled(zt(ZY), zt(Z1), col(WY), ["Z1", "WY"], ["ZY"])
-
-    wrap(P[0][:, 0:128], zw(ZY), lambda i: T.TB[:, 128 * i:128 * i + 128], ["ZY", "TB"], ["P0"])
-    ts(T.yb[:], P[0][:, 0:128], 2048.0, 2048.0, A.add, A.min, ["P0"], ["yb"])
-    dma("s", T.y[:], T.yb[:], ["yb"], ["y"], "out", 16)
-    for k, n in (("v", cnt["v"]), ("a", cnt["a"]), ("p", cnt["p"]), ("c", cnt["c"]), ("sent", sent[0]), ("b16", 128), ("blk", 16), ("xs", 16),
-                 ("ds", 32), ("hm", 16), ("tb", 80), ("pf", 192), ("out", 16)):
-        wait("c", (k, n))
+    for i in sorted(range(len(ops)), key=lambda k: (start[k], k)):
+        o = ops[i]
+        e = o["e"]
+        for j in sorted(o["pre"]):
+            if o["pre"][j] > 0:
+                wait(e, *tok[j])
+        ins = o["fn"]()
+        if o["sem"]:
+            s = o["sem"][0]
+            tok[i] = (s, total[s])
+            if not s.startswith("arr"):
+                ins.then_inc(T.sem[s], 16)
+        else:
+            cnt[e] += 1
+            tok[i] = (e, cnt[e])
+            ins.then_inc(T.sem[e], 1)
+    total["sent"] = 3 * sum(len(topo.engines(core, T.cores[p])) for p in peers)
+    for s, n in list(cnt.items()) + list(total.items()):
+        wait("c", s, n)

@@ -1,3 +1,4 @@
+import numpy as np
 from concourse.mybir import AluOpType as A, ActivationFunctionType as F
 
 D0, H0, GW = 2064, 2304, 2432
@@ -5,9 +6,15 @@ BD0, TW = 2 * GW, 2 * GW + 192
 BB = 16384.0
 NB = (11, 8)
 TINY = 2.0 ** -110
-LOOKS = ((0, 32, "a"), (32, 64, "v"), (64, 96, "a"), (96, 128, "a"), (128, 160, "v"), (160, 192, "a"))
-CYC, PEC, WAKE, GAT, SCA = 0.00087, 0.0005, 0.18, 1.5, 3.5
-PASSES = 8
+VSH = ((0, 40), (72, 112), (160, 192))
+ASH = ((40, 72), (112, 144), (144, 160))
+NQ, NM = 8, 16
+LOOKS = ((0, 64, "a"), (64, 128, "a"), (128, 160, "a"), (160, 192, "v"))
+CYC, PEC, GAT, SCA = [np.array(v) for v in ((0.00095, 0.00087, 0.00116), (0.0006, 0.0007, 0.0006), (1.6, 1.2, 2.0), (4.0, 2.5, 5.0))]
+WAKE, WEIGHT = (0.2, 0.18, 0.2), (1.0, 1.1, 0.8)
+PASSES = 4000
+DSLATE, TBL = True, 2.0
+MOD = True
 
 
 def _s(n, d):
@@ -22,11 +29,11 @@ SCRATCH = {
     "pI": _s(2, i32), "pJ": _s(4, i32), "col": _s(40, f32), "R": _s(16, f32), "colI": _s(192, bf), "J16": _s(208, bf),
     "one": _s(128, bf), "BD": _s(128, bf), "Tri": _s(128, bf), "Id": _s(128, bf), "Id16": _s(128, f16), "Idn": _s(128, bf),
     "M1": _s(128, bf), "BDn": _s(128, bf), "cm64": _s(128, bf), "c192": _s(128, bf), "PW": _s(320, f16),
-    "Z": _s(144 * 4, bf), "BDv": _s(128 * 11, bf), "BDh": _s(256, f16), "H4": _s(128, f32), "TS": _s(2048, bf), "W": _s(288, bf),
+    "Z": _s(144 * 4, bf), "BDv": _s(128 * 12, bf), "BDh": _s(256, f16), "H4": _s(128, f32), "TS": _s(2048, bf), "W": _s(288, bf),
     "HD2": _s(192, bf), "PAT": _s(192, bf), "PATn": _s(192, bf), "HZ": _s(192, bf), "GH": _s(576, bf),
     "jw": _s(36, f32), "sq2": _s(128, f32), "ZR": _s(192, bf), "BIG": _s(192, f32), "c65": _s(192, bf), "HOLD": _s(640, bf),
     "fe": _s(128, f16), "feT": _s(128, f16), "o16": _s(128, f16), "oT": _s(128, f16), "Uw": _s(128, f16), "IdK": _s(256, bf),
-    "mov": _s(128, bf), "XT": _s(256, bf), "SP": _s(1024, bf), "oo": _s(256, f16), "offx": _s(384, u16), "xb": _s(128, i32), "rows": _s(768, bf), "ti": _s(512, i32),
+    "mov": _s(128, bf), "XT": _s(128, bf), "SP": _s(1536, bf), "oo": _s(256, f16), "offx": _s(384, u16), "xb": _s(128, i32), "rows": _s(768, bf), "ti": _s(512, i32),
     "Fw": _s(128, bf), "V0": _s(128, f32), "CE": _s(144, f32), "HS": _s(128, f32), "K16": _s(128, f16), "BDm": _s(128, bf),
     "coff": _s(8, u16), "d0": _s(192, bf), "SB": _s(192, bf), "SH": _s(192, f32),
     "swg": _s(12, u16), "swf": _s(12, f32), "swu": _s(36, u16), "srep": _s(192, f32), "acol": _s(192, bf), "ua": _s(192, f32),
@@ -52,31 +59,117 @@ def put_in_order(ops):
         for j, d in pre[i]:
             post[j].append((i, d))
 
-    def place(order, follows, first):
-        start, taken = [0.0] * n, {}
+    def place(order, follows, first, queue):
+        start, taken, went = [0.0] * n, {}, [None] * n
         for i in order:
-            t = max([start[j] + cost[j] + d for j, d in follows[i]] + [first[i]])
-            line = taken.setdefault(ops[i]["e"], [])
-            k = 0
-            while k < len(line) and line[k][0] < t + cost[i] - 1e-9:
-                t = max(t, line[k][1])
-                k += 1
-            line.insert(k, (t, t + cost[i]))
-            start[i] = t
-        return start
+            ready, best = max([start[j] + cost[j] + d for j, d in follows[i]] + [first[i]]), None
+            for e, c in ops[i]["can"].items() if queue is None else [(queue[i], cost[i])]:
+                line, t = taken.setdefault(e, []), ready
+                k = bisect(line, t)
+                while k < len(line) and line[k][0] < t + c - 1e-9:
+                    t = max(t, line[k][1])
+                    k += 1
+                if best is None or t + c < best[0] + best[1]:
+                    best = (t, c, e, k)
+            start[i], cost[i], went[i], k = best
+            taken[went[i]].insert(k, (start[i], start[i] + cost[i]))
+        return start, went
+
+    def bisect(line, t):
+        lo, hi = 0, len(line)
+        while lo < hi:
+            mid = (lo + hi) // 2
+            if line[mid][1] <= t:
+                lo = mid + 1
+            else:
+                hi = mid
+        return lo
 
     way = [0.0] * n
     for i in range(n - 1, -1, -1):
         way[i] = cost[i] + max([way[j] + d for j, d in post[i]] + [ops[i]["lat"]])
     best = None
     for turn in range(PASSES):
-        start = place(sorted(range(n), key=lambda k: (-way[k], k)), pre, [0.0] * n)
+        start, went = place(sorted(range(n), key=lambda k: (-way[k], k)), pre, [0.0] * n, None)
         end = max(start[i] + cost[i] + ops[i]["lat"] for i in range(n))
         if best is None or end < best[0]:
-            best = (end, start)
-        back = place(sorted(range(n), key=lambda k: (-start[k] - cost[k], -k)), post, [o["lat"] for o in ops])
+            best = (end, start, went)
+        back = place(sorted(range(n), key=lambda k: (-start[k] - cost[k], -k)), post, [o["lat"] for o in ops], went)[0]
         way = [back[i] + cost[i] for i in range(n)]
-    return best[1]
+    return best[1], best[2]
+
+
+def put_in_order(ops):
+    n, m = len(ops), len(WAKE)
+    gap = lambda j, d, k: WAKE[k] + ops[j]["lat"] if d > 0 else ops[j]["lat"] if d == 0 else 0.0
+    pre = [[[(j, gap(j, d, k)) for j, d in o["pre"].items()] for o in ops] for k in range(m)]
+    can = [[(e, [float(x) for x in c]) for e, c in o["can"].items()] for o in ops]
+    lat = [o["lat"] for o in ops]
+    least = [min(c[0] for e, c in x) for x in can]
+    post = [[] for o in ops]
+    for i in range(n):
+        for j, d in pre[0][i]:
+            post[j].append((i, d))
+
+    def place(more):
+        way = [0.0] * n
+        for i in range(n - 1, -1, -1):
+            way[i] = least[i] + more[i] + max([way[j] + d for j, d in post[i]] + [lat[i]])
+        start, end, went, taken = [0.0] * n, [0.0] * n, [None] * n, {e: ([], []) for e in "vapcs"}
+        for i in sorted(range(n), key=lambda k: (-way[k], k)):
+            ready, best = max([end[j] + d for j, d in pre[0][i]] + [0.0]), None
+            for x in can[i]:
+                (a, b), t, c = taken[x[0]], ready, x[1][0]
+                lo, hi = 0, len(b)
+                while lo < hi:
+                    mid = (lo + hi) // 2
+                    lo, hi = (mid + 1, hi) if b[mid] <= t else (lo, mid)
+                while lo < len(a) and a[lo] < t + c - 1e-9:
+                    t = max(t, b[lo])
+                    lo += 1
+                if best is None or t + c < best[1]:
+                    best = (t, t + c, x, lo)
+            start[i], end[i], went[i], lo = best
+            taken[went[i][0]][0].insert(lo, start[i])
+            taken[went[i][0]][1].insert(lo, end[i])
+        order = sorted(range(n), key=lambda k: (start[k], k))
+        total, chain = 0.0, []
+        for k in range(m):
+            free, by, last = {e: 0.0 for e in "vapcs"}, [None] * n, {}
+            for i in order:
+                e, c = went[i]
+                t, by[i] = free[e], (last.get(e), True)
+                for j, d in pre[k][i]:
+                    if end[j] + d >= t:
+                        t, by[i] = end[j] + d, (j, False)
+                end[i] = free[e] = t + c[k]
+                last[e] = i
+            i = max(range(n), key=lambda q: end[q] + lat[q])
+            total += (end[i] + lat[i]) * WEIGHT[k]
+            while i is not None:
+                if by[i][1] and by[i][0] is not None:
+                    chain.append((i, by[i][0]))
+                i = by[i][0]
+        return total, order, [x[0] for x in went], chain, way
+
+    more, x = [0.0] * n, 1
+    best = place(more)
+    for turn in range(PASSES):
+        x = (x * 1103515245 + 12345) % 2 ** 31
+        i, j = best[3][(x >> 8) % len(best[3])]
+        step = 0.1 + (x >> 4) % 16 * 0.1
+        new = list(more)
+        if x >> 20 & 1:
+            new[i] += max(best[4][j] - best[4][i], 0.0) + step
+        else:
+            new[j] = max(new[j] - step, -least[j] * 0.9) if x >> 21 & 1 else new[j] + step
+        got = place(new)
+        if got[0] <= best[0]:
+            best, more = got, new
+    return best[1], best[2]
+
+
+ORDER = {}
 
 
 def rank_program(g, core, T, topo):
@@ -101,8 +194,9 @@ def rank_program(g, core, T, topo):
                 lastw[k], reads[k], before[k] = [i], [], mine
             else:
                 reads.setdefault(k, []).append(i)
-        ops.append({"e": e, "fn": fn, "cost": cost, "lat": lat, "sem": sem,
-                    "pre": {j: 0.0 if e == "p" == ops[j]["e"] else WAKE for j in pre}})
+        can = cost if e == "x" else {e: cost + 0 * CYC}
+        ops.append({"e": e if e != "x" else "x%d" % i, "fn": fn if e == "x" else {e: fn}, "can": can, "lat": lat, "sem": sem,
+                    "pre": {j: 0.0 if e == "p" == ops[j]["e"] else 1.0 for j in pre}})
 
     rows_of = {}
 
@@ -115,12 +209,12 @@ def rank_program(g, core, T, topo):
     V, S = g.vector, g.scalar
     ga = lambda n: 60 + GAT * n
     sc = lambda n: 60 + SCA * n
-    vc = lambda c: max(64, c) * CYC
+    vc = lambda c: np.maximum(64, c) * CYC
 
     def dma(e, out, in_, rd, wr, sem, lat, behind=0):
         op(e, lambda: Q[e].dma_start(out, in_), rd, wr, 0.05, lat, (sem, 16))
         for j in range(len(ops) - 1 - behind, len(ops) - 1):
-            ops[-1]["pre"][j] = -ops[j]["lat"]
+            ops[-1]["pre"][j] = -1.0
 
     def ts(out, in0, s1, s2, o0, o1, rd, wr, c=64):
         if s2 is None:
@@ -141,10 +235,20 @@ def rank_program(g, core, T, topo):
         op("v", lambda: V.memset(ap, x), [], wr, vc(c))
 
     def act(out, a, rd, wr, func=F.Identity, bias=0.0, scale=1.0, c=128):
-        op("a", lambda: S.activation(out, a, func, bias=bias, scale=scale), rd, wr, 0.05 + vc(c))
+        if isinstance(bias, float) and isinstance(scale, float) and (bias, scale) == (0.0, 1.0):
+            op("a", lambda: S.activation(out, a, func), rd, wr, 0.05 + vc(c))
+        else:
+            op("a", lambda: S.activation(out, a, func, bias=bias, scale=scale), rd, wr, 0.05 + vc(c))
+
+    def line(out, src, w, x, rd, wr, ca, cv):
+        op("x", {"v": lambda: V.tensor_scalar(out, src, w, x, A.mult, A.add), "a": lambda: S.activation(out, src, F.Identity, bias=x, scale=w)},
+           rd, wr, {"v": vc(cv), "a": 0.05 + vc(ca)})
 
     def scaled(out, src, w, rd, wr, c=128):
-        act(out, src, rd, wr, F.Identity, 0.0, w, c)
+        line(out, src, w, 0.0, rd, wr, c, c // 2)
+
+    def pick(out, src, rd, wr, n, w=1.0):
+        line(out, src, w, 0.0, rd, wr, GAT * n, ga(n))
 
     def mms(calls, rd, wr, n):
         def fn():
@@ -176,19 +280,20 @@ def rank_program(g, core, T, topo):
     (Z1, ZU, ZFE, ZFO) = range(4)
     zt = lambda n: T.Z[:, 144 * n:144 * n + 144]
     zw = lambda n: (lambda i: T.Z[:, 144 * n + 15 - i:144 * n + 143 - i])
-    (BAE, BAO, BIRTH, B256, B4096N, BOCC, BGW, BHOME, BNEG, BY, BU) = range(11)
+    (BAE, BAO, BIRTH, B256, B4096N, BOCC, BGW, BHOME, BNEG, BY, BU, B2) = range(12)
     bdv = lambda n: T.BDv[:, 128 * n:128 * n + 128]
     XSk = ["XS", "XSa", "XSb"]
     DSk = ["DS0", "DS1", "DSa"]
-    NQ = 8
-    DQk = ["DQ%d" % c for c in range(NQ)] + ["DQa"]
+    DQk = ["DQ%d" % c for c in range(16)] + ["DQa"]
     XBk = {0: ["XBe%d" % c for c in range(8)] + ["XBea"], 1: ["XBo%d" % c for c in range(8)] + ["XBoa"]}
     XBt = {0: T.XBe, 1: T.XBo}
 
-    dma("s", T.blk[:], T.board[:], [], ["blk"], "blk", 2.0)
-    dma("s", T.XS[:, 0:2048], T.xs[:], [], ["XS"], "xs", 3.5, 1)
-    dma("s", T.hmb[:], T.hm[:], [], ["hmb"], "hmb", 4.0, 1)
-    dma("s", T.DS[0:64, 0:2048], T.ds[0:64, :], [], ["DS0"], "ds0", 5.5, 1)
+    dma("s", T.blk[:], T.board[:], [], ["blk"], "blk", 1.4)
+    dma("s", T.XS[:, 0:2048], T.xs[:], [], ["XS"], "xs", 3.0, 1)
+    dma("s", T.DS[0:64, 0:2048], T.ds[0:64, :], [], ["DS0"], "ds0", 4.6, 1)
+    if not DSLATE:
+        dma("s", T.DS[64:128, 0:2048], T.ds[64:128, :], [], ["DS1"], "ds1", 6.2, 1)
+    dma("s", T.hmb[:], T.hm[:], [], ["hmb"], "hmb", 6.5, 1)
 
     iota(T.pI[:, 0:1], [[0, 1]], 0, 1, ["pI"], 1, False)
     iota(T.colI[:], [[1, 192]], 0, 0, ["colI"], 192)
@@ -200,13 +305,14 @@ def rank_program(g, core, T, topo):
     asel(T.Tri[:], T.BD[:], [[1, 128]], A.is_ge, 0.0, 0, -1, ["BD"], ["Tri"])
     JW, K2, K3 = T.jw[:, 0:12], T.jw[:, 12:24], T.jw[:, 24:36]
     iota(JW, [[16, 12]], D0, 0, ["jw"], 12)
-    VSH = ((32, 72), (104, 144), (160, 192))
     for k, (a, b) in enumerate(VSH):
-        ms(T.XZ[:, 16 * a:16 * b], 0.0, ["XZ%d" % k], 8 * (b - a))
-    for c in range(4):
-        iota(T.SQ[:, 564 * c:564 * c + 564], [[1, 564]], 564 * c, 0, ["SQ%d" % c], 564)
-    SQk = ["SQ%d" % c for c in range(4)]
-    ms(T.TB[:, 0:GW], 0.0, ["TB"], GW // 2)
+        iota(T.XZ[:, 16 * a:16 * b], [[0, 16 * (b - a)]], 0, 0, ["XZ%d" % k], 16 * (b - a))
+    for c in range(12):
+        act(T.SQ[:, 188 * c:188 * c + 188], T.colI[:, 0:188], ["colI"], ["SQ%d" % c], F.Identity, 188.0 * c, c=188)
+        row("SQ")
+    SQk = ["SQ%d" % c for c in range(12)]
+    for c in range(8):
+        ms(T.TB[:, GW // 8 * c:GW // 8 * (c + 1)], 0.0, ["TB%d" % c], GW // 16)
     ms(T.XS[:, 2048:2064], 1e9, ["XSa"])
     ms(T.XS[:, 2064:2080], -1e9, ["XSb"])
     ms(T.DS[:, 2048:2080], 0, ["DSa"])
@@ -229,26 +335,27 @@ def rank_program(g, core, T, topo):
         ts(T.PW[:, 160 * u:160 * u + 160], T.colI[:, 0:160], col(P16), col(U0 + u), A.is_equal, A.mult, ["colI", "P16", "U%d" % u], ["PW%d" % u], 80)
     ts(T.R[:], T.colI[:, 0:16], col(PM), None, A.is_equal, None, ["colI", "PM"], ["R"])
     ts(zt(Z1), T.colI[:, 0:144], col(C15), None, A.is_equal, None, ["colI", "C15"], ["Z1"], 72)
-    ts(col(TMP), Rr(0), 256.0, Rr(1), A.mult, A.add, ["R"], ["TMP"])
-    ts(col(WU), col(TMP), 2.0, Rr(8), A.mult, A.add, ["TMP", "R"], ["WU"])
-    ts(col(WAE), Rr(2), -2064.0, col(WU), A.mult, A.add, ["R", "WU"], ["WAE"])
-    ts(col(WAO), Rr(3), -2064.0, col(WU), A.mult, A.add, ["R", "WU"], ["WAO"])
-    ts(col(WOCC), Rr(2), Rr(3), None, A.add, None, ["R"], ["WOCC"])
-    ts(col(WY), col(WOCC), -2048.0, col(WU), A.mult, A.add, ["WOCC", "WU"], ["WY"])
-    ts(col(WO2), col(WOCC), float(GW), None, A.mult, None, ["WOCC"], ["WO2"])
+    lc = lambda k, src, w, x, rd, wr: line(col(k), src, w, x, rd, [wr], 64, 64)
+    lc(TMP, Rr(0), 256.0, Rr(1), ["R"], "TMP")
+    lc(WU, col(TMP), 2.0, Rr(8), ["TMP", "R"], "WU")
+    lc(WAE, Rr(2), -2064.0, col(WU), ["R", "WU"], "WAE")
+    lc(WAO, Rr(3), -2064.0, col(WU), ["R", "WU"], "WAO")
+    lc(WOCC, Rr(2), 1.0, Rr(3), ["R"], "WOCC")
+    lc(WY, col(WOCC), -2048.0, col(WU), ["WOCC", "WU"], "WY")
+    lc(WO2, col(WOCC), float(GW), 0.0, ["WOCC"], "WO2")
     for t in range(3):
-        ts(col(WE0 + t), Rr(4 + t), col(WOCC), None, A.add, None, ["R", "WOCC"], ["WE%d" % t])
+        lc(WE0 + t, Rr(4 + t), 1.0, col(WOCC), ["R", "WOCC"], "WE%d" % t)
     ts(col(TMP + 12), Rr(0), Rr(1), Rr(8), A.add, A.add, ["R"], ["MA"])
-    ts(col(MV), col(TMP + 12), col(WOCC), None, A.add, None, ["MA", "WOCC"], ["MV"])
-    ts(col(OFF), col(PM), 15.0, BB, A.not_equal, A.mult, ["PM"], ["OFF"])
-    for k, x in ((OFF1, 1.0), (OFA0, -2064.0), (OFS, 2048.0), (OFS1, 2047.0)):
-        ts(col(k), col(OFF), x, None, A.add, None, ["OFF"], ["c%d" % k])
-    ts(col(BSEL), col(PM), -2048.0, -2048.0, A.mult, A.add, ["PM"], ["BSEL"])
-    ts(col(BS2), col(PM), -4096.0, None, A.mult, None, ["PM"], ["BS2"])
-    ts(col(I192), col(PM), 192.0, None, A.mult, None, ["PM"], ["I192"])
-    ts(col(WH), Rr(9), 256.0, Rr(7), A.mult, A.add, ["R"], ["WH"])
-    ts(col(TMP + 13), Rr(9), float(H0 // 256), None, A.mult, None, ["R"], ["PBa"])
-    ts(col(PB), Rr(7), 32.0 * rank, col(TMP + 13), A.mult, A.add, ["R", "PBa"], ["PB"])
+    lc(MV, col(TMP + 12), 1.0, col(WOCC), ["MA", "WOCC"], "MV")
+    lc(OFF, Rr(15), -BB, BB, ["R"], "OFF")
+    for k, x in ((OFF1, 1.0), (OFA0, -2064.0), (OFS, 2048.0)):
+        lc(k, Rr(15), -BB, BB + x, ["R"], "c%d" % k)
+    lc(BSEL, col(PM), -2048.0, -2048.0, ["PM"], "BSEL")
+    lc(BS2, col(PM), -4096.0, 0.0, ["PM"], "BS2")
+    lc(I192, col(PM), 192.0, 0.0, ["PM"], "I192")
+    lc(WH, Rr(9), 256.0, Rr(7), ["R"], "WH")
+    lc(TMP + 13, Rr(9), float(H0 // 256), 0.0, ["R"], "PBa")
+    lc(PB, Rr(7), 32.0 * rank, col(TMP + 13), ["R", "PBa"], "PB")
     ts(T.AB[:, 0:192], T.J16[:, 0:192], col(PM), -4 * BB, A.is_equal, A.mult, ["J16", "PM"], ["HDa"], 96)
     ts(T.EA[:, 0:192], T.J16[:, 15:207], col(PM), BB, A.is_equal, A.mult, ["J16", "PM"], ["HDb"], 96)
     tt(T.HD2[:], T.AB[:, 0:192], T.EA[:, 0:192], A.add, ["HDa", "HDb"], ["HD2"], 384)
@@ -259,28 +366,29 @@ def rank_program(g, core, T, topo):
     ts(K3, JW, col(PM), float(BD0 + 1 - D0), A.add, A.add, ["jw", "PM"], ["K3"])
     scaled(T.cm64[:], T.colI[:, 0:128], -64.0, ["colI"], ["cm64"])
     for t in range(3):
-        scaled(T.WIN[:, 2304 * t:2304 * t + 192], T.colI[:], 0.0, ["colI"], ["WIN%d" % t], 192)
-        act(T.GH[:, 192 * t:192 * t + 192], T.colI[:], ["colI", "R"], ["GH%d" % t], F.Identity, Rr(4 + t), 0.0, 192)
+        act(T.WIN[:, 2304 * t:2304 * t + 192], T.colI[:], ["colI"], ["WIN%d" % t], F.Silu, 0.0, 0.0, 192 + (1500 if t == 0 else 0))
+        row("WIN")
+        line(T.GH[:, 192 * t:192 * t + 192], T.colI[:], 0.0, Rr(4 + t), ["colI", "R"], ["GH%d" % t], 192, 96)
         for p in range(4):
             c0 = 960 * t + 192 * p
-            act(T.MSG[:, c0:c0 + 32], T.colI[:, 0:32], ["colI", "R", "PB"], ["MSG%d%d" % (t, p)], F.Identity, col(PB), Rr(7), 64)
-    act(T.c192[:], T.colI[:, 0:128], ["colI"], ["c192"], F.Identity, 4096.0, 0.0)
+            line(T.MSG[:, c0:c0 + 32], T.colI[:, 0:32], Rr(7), col(PB), ["colI", "R", "PB"], ["MSG%d%d" % (t, p)], 64, 64)
+    line(T.c192[:], T.colI[:, 0:128], 0.0, 4096.0, ["colI"], ["c192"], 128, 64)
     scaled(T.ZR[:], T.colI[:], 0.0, ["colI"], ["ZR"], 192)
     c65k = []
-    for a, b, x in ((0, 32, 6.5), (32, 72, 0.0), (72, 104, 6.5), (104, 144, 0.0), (144, 160, 6.5), (160, 192, 0.0)):
+    for a, b, x in [v + (0.0,) for v in VSH] + [v + (6.5,) for v in ASH]:
         ms(T.c65[:, a:b], x, ["c65%d" % a])
         c65k.append("c65%d" % a)
-    act(T.Id16[:], T.Id[:], ["Id"], ["Id16"])
+    scaled(T.Id16[:], T.Id[:], 1.0, ["Id"], ["Id16"])
     scaled(T.IdK[:, 0:128], T.Id[:], 4096.0, ["Id"], ["IdK0"])
     scaled(T.IdK[:, 128:256], T.Id[:], -4096.0, ["Id"], ["IdK1"])
     scaled(T.Idn[:], T.Id[:], -1.0, ["Id"], ["Idn"])
-    act(T.K16[:], T.colI[:, 0:128], ["colI"], ["K16"], F.Identity, 2048.0, 2.0)
+    line(T.K16[:], T.colI[:, 0:128], 2.0, 2048.0, ["colI"], ["K16"], 128, 64)
     scaled(T.BDm[:], T.BD[:], -4096.0, ["BD"], ["BDm"])
-    act(T.sq2[:], T.colI[:, 0:128], ["colI", "PM"], ["sq2"], F.Identity, col(PM), 16.0)
+    line(T.sq2[:], T.colI[:, 0:128], 16.0, col(PM), ["colI", "PM"], ["sq2"], 128, 128)
     for k in range(4):
-        act(T.HOLD[:, 160 * k:160 * k + 160], T.J16[:, 0:160], ["J16"], ["HOLD%d" % k], F.Sign, c=160)
+        ts(T.HOLD[:, 160 * k:160 * k + 160], T.J16[:, 0:160], 0.0, None, A.not_equal, None, ["J16"], ["HOLD%d" % k], 80)
     HOLDk = ["HOLD%d" % k for k in range(4)]
-    for k, w, wk in ((BAE, col(WAE), "WAE"), (BAO, col(WAO), "WAO"), (BIRTH, Rr(0), "R"), (B256, 256.0, "BD"), (B4096N, -4096.0, "BD"),
+    for k, w, wk in ((BAE, col(WAE), "WAE"), (BAO, col(WAO), "WAO"), (BIRTH, Rr(0), "R"), (B256, 256.0, "BD"), (B2, 2.0, "BD"), (B4096N, -4096.0, "BD"),
                      (BOCC, col(WOCC), "WOCC"), (BGW, col(WO2), "WO2"), (BHOME, col(WH), "WH"), (BNEG, -1.0, "BD"), (BY, col(WY), "WY")):
         scaled(bdv(k), T.BD[:], w, ["BD", wk], ["BD%d" % k])
     scaled(bdv(BU), T.BD[:], col(WU), ["BD", "WU"], ["BD%d" % BU])
@@ -293,8 +401,8 @@ def rank_program(g, core, T, topo):
     scaled(zt(ZFE), zt(Z1), Rr(2), ["Z1", "R"], ["ZF0"], 144)
     scaled(zt(ZFO), zt(Z1), Rr(3), ["Z1", "R"], ["ZF1"], 144)
     ms(T.EQ[:, 0:512], 1.0, ["EQ0"], 256)
-    for k in range(2):
-        asel(T.SP[:, 512 * k:512 * k + 512], T.EQ[:, 0:512], [[-1, 32], [0, 16]], A.is_equal, 0.0, -72 * k, 1, ["EQ0"], ["SP%d" % k], 512)
+    for k, (a, b) in enumerate(ASH):
+        asel(T.SP[:, 512 * k:512 * k + 16 * (b - a)], T.EQ[:, 0:16 * (b - a)], [[-1, b - a], [0, 16]], A.is_equal, 0.0, ASH[0][0] - a, 1, ["EQ0"], ["SP%d" % k], 16 * (b - a))
     iota(T.BIG[:], [[0, 192]], 8388608, 0, ["BIG"], 192)
     iota(T.HM[:], [[0, 2080]], 0, 0, ["HM"], 2080)
     ts(T.W[:, 0:144], T.colI[:, 0:144], col(C15), 4096.0, A.is_gt, A.mult, ["colI", "C15"], ["Wa"], 72)
@@ -334,8 +442,9 @@ def rank_program(g, core, T, topo):
     ts(T.ti[:, 128:256], T.blk[:], 1, 255, A.logical_shift_right, A.bitwise_and, ["blk"], ["ti1"], 128)
     cp(T.rows[:, 0:256], T.ti[:, 0:256], ["ti0", "ti1"], ["r01"], 256)
     for r, c0, k in ((2, 256, "r2"), (3, 384, "r3"), (8, 384, "r3"), (0, 0, "r01"), (1, 128, "r01")):
-        dma("s", T.TB[r:128:16, 0:2048], T.rows[:, c0:c0 + 128], [k], ["TB"], "tb", 2.5)
-    dma("s", T.DS[64:128, 0:2048], T.ds[64:128, :], [], ["DS1"], "ds1", 3.5, 5)
+        dma("s", T.TB[r:128:16, 0:2048], T.rows[:, c0:c0 + 128], [k] + ["TB%d" % c for c in range(8)], ["TB"], "tb", TBL)
+    if DSLATE:
+        dma("s", T.DS[64:128, 0:2048], T.ds[64:128, :], [], ["DS1"], "ds1", 3.5, 5)
     ts(T.ti[:, 256:384], T.hmb[:], 255, None, A.bitwise_and, None, ["hmb"], ["ti2"], 128)
     ts(T.ti[:, 384:512], T.hmb[:], 8, None, A.logical_shift_right, None, ["hmb"], ["ti3"], 128)
     cp(T.rows[:, 512:768], T.ti[:, 256:512], ["ti2", "ti3"], ["r79"], 256)
@@ -347,11 +456,20 @@ def rank_program(g, core, T, topo):
             act(XBt[par][:, 256 * c:256 * c + 256], T.XS[:, 0:2080].indirect(T.offx[:, c0 + 16 * c:c0 + 16 * c + 16]), XSk + [ok], [XBk[par][c]], F.Copy, c=GAT * 256)
             row("XB")
 
-    silu = [1.3]
-
     def xb_clear(par, off, ok):
-        op("a", lambda: S.activation(XBt[par][:].indirect(off), T.BIG[:], F.Silu), ["BIG", ok], XBk[par], vc(sc(192)) + silu[0])
-        silu[0] = 0.0
+        op("a", lambda: S.activation(XBt[par][:].indirect(off), T.BIG[:], F.Silu), ["BIG", ok], XBk[par], vc(sc(192)))
+
+    def targets(out, off, ok, key):
+        if MOD and key != "qB0":
+            cp(out, T.DQ[:, 0:2064].indirect(off), DQk + [ok], [key[:2]], ga(192))
+        else:
+            ts(T.qx[:], T.DQ[:, 0:2064].indirect(off), 2047, None, A.bitwise_and, None, DQk + [ok], ["qx"], ga(192))
+            cp(out, T.qx[:], ["qx"], [key[:2]], 192)
+
+    def ring(n):
+        if MOD:
+            ts(T.qz[:, 0:n], T.qy[:, 0:n], 2047, None, A.bitwise_and, None, ["qy"], ["qz"], n)
+        return (T.qz[:, 0:n], "qz") if MOD else (T.qy[:, 0:n], "qy")
 
     def hold(out, src, n, rd, wr):
         scan(out, T.HD2[:, 0:n], src, 2 * BB, A.add, A.max, ["HD2"] + rd, wr, n)
@@ -393,37 +511,35 @@ def rank_program(g, core, T, topo):
             wrap(P[0][:, 0:128], zw(ZFO if odd else ZFE), lambda i: T.TB[:, i:2048:16], ["TB", "ZF%d" % odd], ["P0"], 128)
             pe, pa = T.endu[:, 12 * t - 12:12 * t], T.aw[:, 12 * t - 12:12 * t]
             cp(XB[:].indirect(pe), T.XZ[:, 0:3072:16], ["XZ", "endu%d" % (t - 1)], XK, sc(192))
-            act(T.ef[:], T.SQ[:, 0:2256].indirect(pe), SQk + ["endu%d" % (t - 1)], ["ef"], F.Copy, c=GAT * 192)
+            pick(T.ef[:], T.SQ[:, 0:2256].indirect(pe), SQk + ["endu%d" % (t - 1)], ["ef"], 192)
             tt(T.qy[:], T.DS[:].indirect(pa), T.ef[:], A.add, DSk + ["aw%d" % (t - 1), "ef"], ["qy"], ga(192))
-            ts(T.qz[:], T.qy[:], 2047, None, A.bitwise_and, None, ["qy"], ["qz"], 192)
-            cp(T.DQ[:].indirect(pe), T.qz[:], ["qz", "endu%d" % (t - 1)], DQk, sc(192))
+            qn, qk = ring(192)
         act(T.Fw[:], P[0][:, 0:128], ["P0"], ["Fw"])
         mm(P[2][:, 0:128], T.BD[:], T.Fw[:], True, True, ["BD", "Fw"], ["P2"], 128)
         mm(P[6][:, 0:128], T.Id16[:], T.K16[:], True, False, ["Id16", "K16"], ["P6"], 128)
         mm(P[6][:, 0:128], T.BDm[:], T.Fw[:], False, True, ["BDm", "Fw"], ["P6"], 128)
         mm(P[1][:, 0:128], T.Id[:], T.cm64[:], True, False, ["Id", "cm64"], ["P1"], 128)
         mm(P[1][:, 0:128], T.Tri[:], T.Fw[:], False, True, ["Tri", "Fw"], ["P1"], 128)
-        act(T.V0[:], P[1][:, 0:128], ["P1"], ["V0"], F.Identity, 0.5 + 32.5 / 16384, -1.0 / 16384)
+        act(T.V0[:], P[1][:, 0:128], ["P1"], ["V0"], F.Identity, 64 + 32.5 / 128, -1.0 / 128)
         if t == 0:
             xb_build(1, 0, "offo")
         scan(T.CE[:, 16:144], P[2][:, 0:128], T.c192[:], 0.0, A.add, A.min, ["P2", "c192"], ["CE"], 128)
         tt(T.HS[:], T.CE[:, 15:143], P[6][:, 0:128], A.max, ["CE", "CE0", "P6"], ["HS"], 128)
-        ts(T.d0[:], T.colI[:], T.CE[:, 143:144], 1.0 / 16384, A.is_equal, A.max, ["colI", "CE"], ["d0"], 96)
+        ts(T.G[:], T.colI[:], T.CE[:, 143:144], None, A.is_equal, None, ["colI", "CE"], ["G"], 96)
+        line(T.d0[:], T.G[:], 128.0, 1.0 / 128, ["G"], ["d0"], 192, 96)
         hold(T.H4[:], T.HS[:], 128, ["HS"], ["H4"])
         ts(T.coff[:], T.H4[:, 15:128:16], col(OFF), None, A.subtract, None, ["H4", "OFF"], ["coff"])
-        cp(T.WIN[:, 2304 * t:2304 * t + 2304].indirect(T.coff[:]), T.V0[:], ["V0", "coff"], [wk], sc(128))
-        scan(T.SB[:], T.d0[:], T.WIN[:, 2304 * t:2304 * t + 192], 0.5, A.add, A.max, ["d0", wk], ["SB"])
-        mm(P[3][:, 0:192], bdv(B256), T.SB[:], True, True, ["BD%d" % B256, "SB"], ["P3"])
+        act(T.WIN[:, 2304 * t:2304 * t + 2304].indirect(T.coff[:]), T.V0[:], ["V0", "coff"], [wk], F.Silu, c=SCA * 128)
+        scan(T.SB[:], T.d0[:], T.WIN[:, 2304 * t:2304 * t + 192], 64.0, A.add, A.max, ["d0", wk], ["SB"])
+        mm(P[3][:, 0:192], bdv(B2), T.SB[:], True, True, ["BD%d" % B2, "SB"], ["P3"])
         hold(T.SH[:], P[3][:, 0:192], 192, ["P3"], ["SH"])
         ts(T.swg[:], T.SH[:, 15:192:16], col(OFS), 2048.0, A.subtract, A.min, ["SH", "c%d" % OFS], ["swg"])
         XZk = ["XZ0", "XZ1", "XZ2"]
         if t > 0:
-            cp(T.qA[:], T.DQ[:, 0:2064].indirect(T.swg[:]), DQk + ["swg"], ["qA"], ga(192))
+            targets(T.qA[:], T.swg[:], "swg", "qA")
+            cp(T.DQ[:].indirect(pe), qn, [qk, "endu%d" % (t - 1)], DQk, sc(192))
             act(T.XZ[:, 0:3072:16], XBt[odd][:, 0:2064].indirect(T.swg[:]), XBk[odd] + ["swg"] + XZk, ["XZ"], F.Copy, c=GAT * 192)
-        if t == 0:
-            cp(T.acol[:], T.TB[:, 0:GW].indirect(T.swg[:]), ["TB", "swg"], ["acol"], ga(192))
-        else:
-            act(T.acol[:], T.TB[:, 0:GW].indirect(T.swg[:]), ["TB", "swg"], ["acol"], F.Copy, c=GAT * 192)
+        pick(T.acol[:], T.TB[:, 0:GW].indirect(T.swg[:]), ["TB", "swg"], ["acol"], 192)
         mm(P[3][:, 0:192], bdv(odd), T.acol[:], True, True, ["BD%d" % odd, "acol"], ["P3"])
         hold(T.HA[:], P[3][:, 0:192], 192, ["P3"], ["HA"])
         ts(aw, T.HA[:, 15:192:16], col(OFA0), None, A.subtract, None, ["HA", "c%d" % OFA0], [ak])
@@ -432,7 +548,7 @@ def rank_program(g, core, T, topo):
         tt(T.swf[:], T.SH[:, 15:192:16], K2, A.min, ["SH", "K2"], ["swf"])
         ts(swu, T.swf[:], col(OFS), None, A.subtract, None, ["swf", "c%d" % OFS], [sk])
         if t == 0:
-            mm(P[4][:, 0:192], bdv(B256), T.SB[:], True, True, ["BD%d" % B256, "SB"], ["P4"])
+            mm(P[4][:, 0:192], bdv(B2), T.SB[:], True, True, ["BD%d" % B2, "SB"], ["P4"])
             act(T.srep[:], P[4][:, 0:192], ["P4"], ["srep"], F.Identity, -2048.0, c=192)
             act(T.XZ[:, 0:3072:16], T.XS[:, 0:2080].indirect(aw), XSk + [ak] + XZk, ["XZ"], F.Copy, c=GAT * 192)
             tt(T.qx[:], T.DS[:].indirect(aw), T.srep[:], A.add, DSk + [ak, "srep"], ["qx"], ga(192))
@@ -447,26 +563,26 @@ def rank_program(g, core, T, topo):
             w = 2048 // NQ
             for c in range(NQ):
                 tt(T.DQ[:, w * c:w * c + w], T.DS[:].indirect(T.offx[:, 256 + w * c // 16:256 + (w * c + w) // 16]), T.SQ[:, w * c:w * c + w], A.add,
-                   DSk + SQk + ["offu"], [DQk[c]], ga(w))
+                   DSk + SQk + ["offu"], DQk[16 // NQ * c:16 // NQ * (c + 1)], ga(w))
                 row("DQ")
         if t == 1:
             xb_clear(1, T.endu[:, 0:12], "endu0")
             xb_clear(1, swu, sk)
         ts(T.q1[:], T.qA[:], 1.0, None, A.add, None, ["qA"], ["q1"], 96)
 
-        def cmpv(a, b, c):
+        def spread(a, b, c):
             scan(T.XA[:, 16 * a:16 * b], T.HOLD[:, 0:16 * (b - a)], T.XZ[:, 16 * a:16 * b], 0.0, A.mult, A.add, HOLDk + ["XZ"], ["XA%d" % c], 8 * (b - a))
-            tt(T.CMP[:, 16 * a:16 * b], XB[:, 0:2048].indirect(T.qA[:, a:b]), T.XA[:, 16 * a:16 * b], A.is_lt, XK + ["qA", "XA%d" % c], [CMPk[c]], ga(16 * (b - a)))
-            row("cmp")
 
-        mms([(P[5][:, 0:128], T.XZ[:, 0:2048:16], T.Id[:], True, True), (P[5][0:64, 128:256], T.XZ[:, 2048:3072:16], T.Id[:], True, True)], ["Id", "XZ"], ["P5"], 128)
-        act(T.XT[:, 0:128], P[5][:, 0:128], ["P5"], ["XT0"])
-        act(T.XT[0:64, 128:256], P[5][0:64, 128:256], ["P5"], ["XT1"])
+        def cmpv(a, b, c):
+            tt(T.CMP[:, 16 * a:16 * b], XB[:, 0:2048].indirect(T.qA[:, a:b]), T.XA[:, 16 * a:16 * b], A.is_lt, XK + ["qA", "XA%d" % c], [CMPk[c]], ga(16 * (b - a)))
+
+        a0 = ASH[0][0]
+        mm(P[5][:, 0:128], T.XZ[:, 16 * a0:16 * a0 + 2048:16], T.Id[:], True, True, ["Id", "XZ"], ["P5"], 128)
+        act(T.XT[:], P[5][:, 0:128], ["P5"], ["XT"])
 
         def cmpa(bank, a, b, c):
-            n, h = 16 * (b - a), a // 128
-            e0 = 512 * (a == 72) + 16 * (a % 128 % 72)
-            mm(P[bank][:, 0:n], T.XT[0:128 - 64 * h, 128 * h:128 * h + 128], T.SP[0:128 - 64 * h, e0:e0 + n], True, False, ["SP0", "SP1", "XT%d" % h], [pk(bank)], n)
+            n = 16 * (b - a)
+            mm(P[bank][:, 0:n], T.XT[:], T.SP[:, 512 * bank:512 * bank + n], True, False, ["SP%d" % bank, "XT"], [pk(bank)], n)
             act(T.XA[:, 16 * a:16 * b], XB[:, 0:2048].indirect(T.qA[:, a:b]), XK + ["qA"], ["XA%d" % c], F.Copy, c=GAT * n)
             row("gat")
             mm(P[bank][:, 0:n], T.Idn[:], T.XA[:, 16 * a:16 * b], False, True, ["Idn", "XA%d" % c], [pk(bank)], n)
@@ -477,7 +593,7 @@ def rank_program(g, core, T, topo):
 
         def choose(a, b, bc, bs, bf_, n):
             mm(P[bs][:, a:b], T.Id16[:], T.q1[:, a:b], True, False, ["Id16", "q1"], [pk(bs)], b - a)
-            mm(P[bf_][:, a:b], bdv(B256), T.SB[:, a:b], True, False, ["BD%d" % B256, "SB"], [pk(bf_)], b - a)
+            mm(P[bf_][:, a:b], bdv(B2), T.SB[:, a:b], True, False, ["BD%d" % B2, "SB"], [pk(bf_)], b - a)
             act(T.sg[:, a:b], P[bc][:, a:b], [pk(bc)], ["sg%d" % n], F.Sign, -9.5, c=b - a)
             mm(P[bs][:, a:b], T.M1[:], T.sg[:, a:b], False, True, ["M1", "sg%d" % n], [pk(bs)], b - a)
             mm(P[bf_][:, a:b], bdv(B4096N), T.sg[:, a:b], False, True, ["BD%d" % B4096N, "sg%d" % n], [pk(bf_)], b - a)
@@ -493,16 +609,16 @@ def rank_program(g, core, T, topo):
             mms([(P[k][:, a:b], T.BDh[:, 0:128], T.sel[:, a:b], first and k != 3, False), (P[k][:, a:b], T.BDh[:, 128:256], T.fb[:, a:b], False, not first)],
                 ["sel%d" % n, "fb%d" % n, "BDh0", "BDh1"], [pk(k)], b - a)
 
-        cut = 144
-        cmpa(0, 0, 32, 3)
-        cmpa(1, 72, 104, 4)
-        cmpa(2, 144, 160, 5)
-        for c, (a, b) in enumerate(VSH):
-            cmpv(a, b, c)
+        half, cut = ASH[0][1], ASH[1][1]
+        for c, (a, b) in enumerate(ASH):
+            cmpa(c, a, b, 3 + c)
+        for f, c in ((spread, 0), (spread, 1), (cmpv, 0), (spread, 2), (cmpv, 1), (cmpv, 2)):
+            f(VSH[c][0], VSH[c][1], c)
+            row("cmp")
         mm(P[6][:, 0:cut], T.Id[:], T.c65[:, 0:cut], True, False, ["Id"] + c65k, ["P6"], cut)
         mm(P[4][:, cut:192], T.Id[:], T.c65[:, cut:192], True, False, ["Id"] + c65k, ["P4"], 64)
-        count(6, 0, 72, [CMPk[0], CMPk[3]], False)
-        count(6, 72, cut, [CMPk[1], CMPk[4]], True)
+        count(6, 0, half, [CMPk[0], CMPk[3]], False)
+        count(6, half, cut, [CMPk[1], CMPk[4]], True)
         count(4, cut, 192, [CMPk[2], CMPk[5]], True)
         choose(0, cut, 6, 5, 0, 0)
         choose(cut, 192, 4, 1, 2, 1)
@@ -510,21 +626,20 @@ def rank_program(g, core, T, topo):
             keys(k, 0, cut, 0, True)
             keys(k, cut, 192, 1, False)
         cp(T.TB[:].indirect(swu), T.GH[:, 192 * t:192 * t + 192], ["GH%d" % t, sk], ["TB"], sc(192))
-        act(T.hcol[:], T.HM[:].indirect(aw), ["HM", ak], ["hcol"], F.Copy, c=GAT * 192)
+        pick(T.hcol[:], T.HM[:].indirect(aw), ["HM", ak], ["hcol"], 192)
         mm(P[1][:, 0:192], bdv(BIRTH), T.acol[:], True, False, ["BD%d" % BIRTH, "acol"], ["P1"])
         mm(P[1][:, 0:192], T.BDh[:, 0:128], T.fb[:], False, False, ["fb0", "fb1", "BDh0"], ["P1"])
 
         def early1():
             ts(T.atw[:], T.H[:, 16:193:16], col(OFF1), 2048.0, A.subtract, A.min, ["H", "c%d" % OFF1], ["atw"])
-            if t == 0:
-                ts(T.qx[:], T.DQ[:, 0:2064].indirect(T.atw[:]), 2047, None, A.bitwise_and, None, DQk + ["atw"], ["qx"], ga(192))
-                cp(T.qB[:], T.qx[:], ["qx"], ["qB"], 192)
-                for c in range(NQ):
-                    ts(T.DQ[:, w * c:w * c + w], T.DQ[:, w * c:w * c + w], 2047, None, A.bitwise_and, None, [DQk[c]], [DQk[c]], w)
+            targets(T.qB[:], T.atw[:], "atw", "qB%d" % t)
+            if t == 0 and MOD:
+                w = 2048 // NM
+                for c in range(NM):
+                    ks = DQk[16 // NM * c:16 // NM * (c + 1)]
+                    ts(T.DQ[:, w * c:w * c + w], T.DQ[:, w * c:w * c + w], 2047, None, A.bitwise_and, None, ks, ks, w)
                     row("DQ")
-            else:
-                cp(T.qB[:], T.DQ[:, 0:2064].indirect(T.atw[:]), DQk + ["atw"], ["qB"], ga(192))
-            scaled(T.vcol[:], T.TB[:, 0:GW].indirect(T.atw[:]), col(MV), ["TB", "atw", "MV"], ["vcol"], GAT * 192)
+            pick(T.vcol[:], T.TB[:, 0:GW].indirect(T.atw[:]), ["TB", "atw", "MV"], ["vcol"], 192, col(MV))
 
         dedupe(7, 0, 3, 1, bdv(B256), "BD%d" % B256, early1, True, NB[0])
         for c, (a, b, e) in enumerate(LOOKS):
@@ -555,7 +670,7 @@ def rank_program(g, core, T, topo):
                              T.sem["arr%d" % t], T.sem.sent, pid, rid, topo.mask(core, dst))
             op("c", send, mk, ["RXr%d" % t], 0.25 + (1.0 if t == 0 and p == peers[0] else 0.0), 1.4, ("arr%d" % t, arr))
         c0 = 128 * t + 32 * rank
-        act(T.RX[:, c0:c0 + 32], T.MSG[:, 960 * t + 192 * rank:960 * t + 192 * rank + 32], mk, ["RX%d" % t], c=64)
+        scaled(T.RX[:, c0:c0 + 32], T.MSG[:, 960 * t + 192 * rank:960 * t + 192 * rank + 32], 1.0, mk, ["RX%d" % t], 64)
         RX, RXk = T.RX[:, 128 * t:128 * t + 128], ["RX%d" % t, "RXr%d" % t]
         ts(w12(0), T.H2[:, 15:192:16], col(OFF), 768.0, A.subtract, A.is_le, ["H2", "OFF"], ["won"])
         ts(w12(2), T.swf[:], col(OFS), None, A.subtract, None, ["swf", "c%d" % OFS], ["s0"])
@@ -592,7 +707,7 @@ def rank_program(g, core, T, topo):
         mm(P[7][:, 0:128], bdv(BHOME), RX, True, False, ["BD%d" % BHOME] + RXk, ["P7"], 128)
         hold(T.H4[:], P[2][:, 0:128], 128, ["P2"], ["H4"])
         ts(T.hwu[:], T.H4[:, 15:128:16], col(OFF), None, A.subtract, None, ["H4", "OFF"], ["hwu"])
-        act(T.hg[:], T.TB[:, 0:GW].indirect(T.hwu[:]), ["TB", "hwu"], ["hg"], F.Copy, c=GAT * 128)
+        pick(T.hg[:], T.TB[:, 0:GW].indirect(T.hwu[:]), ["TB", "hwu"], ["hg"], 128)
         mm(P[7][:, 0:128], bdv(BGW), T.hg[:], False, True, ["BD%d" % BGW, "hg"], ["P7"], 128)
         hold(T.H4[:], P[7][:, 0:128], 128, ["P7"], ["H4"])
         ts(roff, T.H4[:, 15:128:16], col(OFF), None, A.subtract, None, ["H4", "OFF"], [rk])
@@ -605,11 +720,11 @@ def rank_program(g, core, T, topo):
             wrap(P[0][:, 0:8], zw(ZU), lambda i: T.RX[:, 128 * t + i:128 * t + 128:16], ["ZU"] + RXk, ["P0"], 64)
             cp(T.vw[:], P[0][:, 0:8], ["P0"], ["vw"])
             act(T.hf[:], P[2][:, 0:128], ["P2"], ["hf"])
-            act(T.xv[:], T.XS[:, 0:2080].indirect(T.vw[:]), XSk + ["vw"], ["xv"], F.Copy, c=GAT * 128)
+            pick(T.xv[:], T.XS[:, 0:2080].indirect(T.vw[:]), XSk + ["vw"], ["xv"], 128)
             cp(XB[:].indirect(roff), T.xv[:], ["xv", rk], XK, sc(128))
             tt(T.qy[:, 0:128], T.DS[:].indirect(T.vw[:]), T.hf[:], A.add, DSk + ["vw", "hf"], ["qy"], ga(128))
-            ts(T.qz[:, 0:128], T.qy[:, 0:128], 2047, None, A.bitwise_and, None, ["qy"], ["qz"], 128)
-            cp(T.DQ[:].indirect(roff), T.qz[:, 0:128], ["qz", rk], DQk, sc(128))
+            qn, qk = ring(128)
+            cp(T.DQ[:].indirect(roff), qn, [qk, rk], DQk, sc(128))
         else:
             Yk = ["Y%d" % c for c in range(4)]
             mm(P[2][:, 0:128], bdv(BU), RX, True, True, ["BD%d" % BU] + RXk, ["P2"], 128)
@@ -619,7 +734,9 @@ def rank_program(g, core, T, topo):
             for h in range(2):
                 dma("sa"[h], T.y[:, 1024 * h:1024 * h + 1024], T.Y[h:128:16, 1024 * h:1024 * h + 1024], Yk, ["y"], "out", 2.0)
 
-    start = put_in_order(ops)
+    if len(ops) not in ORDER:
+        ORDER[len(ops)] = put_in_order(ops)
+    order, went = ORDER[len(ops)]
     total, cnt, tok, seen = {}, {"v": 0, "a": 0, "p": 0, "c": 0}, {}, {}
     for o in ops:
         if o["sem"]:
@@ -631,13 +748,13 @@ def rank_program(g, core, T, topo):
             seen[(e, s)] = n
             Q[e].wait_ge(T.sem[s], n)
 
-    for i in sorted(range(len(ops)), key=lambda k: (start[k], k)):
+    for i in order:
         o = ops[i]
-        e = o["e"]
+        e = went[i]
         for j in sorted(o["pre"]):
             if o["pre"][j] > 0:
                 wait(e, *tok[j])
-        ins = o["fn"]()
+        ins = o["fn"][e]()
         if o["sem"]:
             s = o["sem"][0]
             tok[i] = (s, total[s])

import numpy as np
from concourse.mybir import AluOpType as A, ActivationFunctionType as F

D0, H0, GW = 2064, 2304, 2432
BD0, TW = 2 * GW, 2 * GW + 192
BB = 16384.0
NB = (11, 8)
TINY = 2.0 ** -110
VSH = ((0, 40), (72, 112), (160, 192))
ASH = ((40, 72), (112, 144), (144, 160))
NQ, NM = 8, 16
LOOKS = ((0, 64, "a"), (64, 128, "a"), (128, 160, "a"), (160, 192, "v"))
CYC, PEC, GAT, SCA = [np.array(v) for v in ((0.00095, 0.00087, 0.00116), (0.0006, 0.0007, 0.0006), (1.6, 1.2, 2.0), (4.0, 2.5, 5.0))]
WAKE, WEIGHT = (0.2, 0.18, 0.2), (1.0, 1.1, 0.8)
PASSES = 4000
DSLATE, TBL = True, 2.0
MOD = True


def _s(n, d):
    return ("sbuf", [128, n], d)


f32, bf, f16, i32, u16 = "float32", "bfloat16", "float16", "int32", "uint16"
SCRATCH = {
    "blk": _s(128, i32), "hmb": _s(128, i32), "XS": _s(2080, bf), "DS": _s(2080, i32), "HM": _s(2080, bf),
    "TB": _s(TW, bf), "XBe": _s(TW, f32), "XBo": _s(TW, f32), "DQ": _s(TW, i32), "Y": _s(TW, f32), "SQ": _s(2256, f32),
    "WIN": _s(6912, f32), "MSG": _s(2880, bf), "RX": _s(384, bf),
    "pI": _s(2, i32), "pJ": _s(4, i32), "col": _s(40, f32), "R": _s(16, f32), "colI": _s(192, bf), "J16": _s(208, bf),
    "one": _s(128, bf), "BD": _s(128, bf), "Tri": _s(128, bf), "Id": _s(128, bf), "Id16": _s(128, f16), "Idn": _s(128, bf),
    "M1": _s(128, bf), "BDn": _s(128, bf), "cm64": _s(128, bf), "c192": _s(128, bf), "PW": _s(320, f16),
    "Z": _s(144 * 4, bf), "BDv": _s(128 * 12, bf), "BDh": _s(256, f16), "H4": _s(128, f32), "TS": _s(2048, bf), "W": _s(288, bf),
    "HD2": _s(192, bf), "PAT": _s(192, bf), "PATn": _s(192, bf), "HZ": _s(192, bf), "GH": _s(576, bf),
    "jw": _s(36, f32), "sq2": _s(128, f32), "ZR": _s(192, bf), "BIG": _s(192, f32), "c65": _s(192, bf), "HOLD": _s(640, bf),
    "fe": _s(128, f16), "feT": _s(128, f16), "o16": _s(128, f16), "oT": _s(128, f16), "Uw": _s(128, f16), "IdK": _s(256, bf),
    "mov": _s(128, bf), "XT": _s(128, bf), "SP": _s(1536, bf), "oo": _s(256, f16), "offx": _s(384, u16), "xb": _s(128, i32), "rows": _s(768, bf), "ti": _s(512, i32),
    "Fw": _s(128, bf), "V0": _s(128, f32), "CE": _s(144, f32), "HS": _s(128, f32), "K16": _s(128, f16), "BDm": _s(128, bf),
    "coff": _s(8, u16), "d0": _s(192, bf), "SB": _s(192, bf), "SH": _s(192, f32),
    "swg": _s(12, u16), "swf": _s(12, f32), "swu": _s(36, u16), "srep": _s(192, f32), "acol": _s(192, bf), "ua": _s(192, f32),
    "aw": _s(36, u16), "qx": _s(192, i32), "q32": _s(192, i32), "qA": _s(192, u16), "qB": _s(192, u16), "q1": _s(192, f16), "q2": _s(192, f16),
    "qy": _s(192, i32), "qz": _s(192, i32), "ef": _s(192, f32), "hf": _s(128, f32),
    "XA": _s(3072, bf), "XZ": _s(3072, bf), "CMP": _s(3072, bf), "sg": _s(192, bf), "sel": _s(192, f16), "fb": _s(192, f16),
    "H": _s(200, f32), "keyr": _s(192, f16), "keyw": _s(12, f32), "atw": _s(12, u16), "vcol": _s(192, bf), "hcol": _s(192, bf),
    "EQ": _s(192 * 13, bf), "AB": _s(640, bf), "EA": _s(640, bf), "G": _s(192, bf), "z": _s(192, f16), "posu": _s(12, u16),
    "w12": _s(96, f32), "boff": _s(36, u16), "H2": _s(192, f32), "HA": _s(192, f32), "H5": _s(624, f32), "D3": _s(36, f32), "E3": _s(36, f32),
    "endu": _s(36, u16), "hwu": _s(8, u16), "hg": _s(128, bf), "roff": _s(24, u16), "vw": _s(8, u16), "xv": _s(128, f32),
}
for _k in range(8):
    SCRATCH["P%d" % _k] = ("psum", [128, 512], f32)
SEMAPHORES = ["v", "a", "p", "c", "blk", "hmb", "xs", "ds0", "ds1", "hm", "tb", "out", "sent", "arr0", "arr1", "arr2"]


def put_in_order(ops):
    n = len(ops)
    cost = [o["cost"] for o in ops]
    pre = [[(j, d + ops[j]["lat"]) for j, d in o["pre"].items()] for o in ops]
    post = [[] for o in ops]
    for i in range(n):
        for j, d in pre[i]:
            post[j].append((i, d))

    def place(order, follows, first, queue):
        start, taken, went = [0.0] * n, {}, [None] * n
        for i in order:
            ready, best = max([start[j] + cost[j] + d for j, d in follows[i]] + [first[i]]), None
            for e, c in ops[i]["can"].items() if queue is None else [(queue[i], cost[i])]:
                line, t = taken.setdefault(e, []), ready
                k = bisect(line, t)
                while k < len(line) and line[k][0] < t + c - 1e-9:
                    t = max(t, line[k][1])
                    k += 1
                if best is None or t + c < best[0] + best[1]:
                    best = (t, c, e, k)
            start[i], cost[i], went[i], k = best
            taken[went[i]].insert(k, (start[i], start[i] + cost[i]))
        return start, went

    def bisect(line, t):
        lo, hi = 0, len(line)
        while lo < hi:
            mid = (lo + hi) // 2
            if line[mid][1] <= t:
                lo = mid + 1
            else:
                hi = mid
        return lo

    way = [0.0] * n
    for i in range(n - 1, -1, -1):
        way[i] = cost[i] + max([way[j] + d for j, d in post[i]] + [ops[i]["lat"]])
    best = None
    for turn in range(PASSES):
        start, went = place(sorted(range(n), key=lambda k: (-way[k], k)), pre, [0.0] * n, None)
        end = max(start[i] + cost[i] + ops[i]["lat"] for i in range(n))
        if best is None or end < best[0]:
            best = (end, start, went)
        back = place(sorted(range(n), key=lambda k: (-start[k] - cost[k], -k)), post, [o["lat"] for o in ops], went)[0]
        way = [back[i] + cost[i] for i in range(n)]
    return best[1], best[2]


def put_in_order(ops):
    n, m = len(ops), len(WAKE)
    gap = lambda j, d, k: WAKE[k] + ops[j]["lat"] if d > 0 else ops[j]["lat"] if d == 0 else 0.0
    pre = [[[(j, gap(j, d, k)) for j, d in o["pre"].items()] for o in ops] for k in range(m)]
    can = [[(e, [float(x) for x in c]) for e, c in o["can"].items()] for o in ops]
    lat = [o["lat"] for o in ops]
    least = [min(c[0] for e, c in x) for x in can]
    post = [[] for o in ops]
    for i in range(n):
        for j, d in pre[0][i]:
            post[j].append((i, d))

    def place(more):
        way = [0.0] * n
        for i in range(n - 1, -1, -1):
            way[i] = least[i] + more[i] + max([way[j] + d for j, d in post[i]] + [lat[i]])
        start, end, went, taken = [0.0] * n, [0.0] * n, [None] * n, {e: ([], []) for e in "vapcs"}
        for i in sorted(range(n), key=lambda k: (-way[k], k)):
            ready, best = max([end[j] + d for j, d in pre[0][i]] + [0.0]), None
            for x in can[i]:
                (a, b), t, c = taken[x[0]], ready, x[1][0]
                lo, hi = 0, len(b)
                while lo < hi:
                    mid = (lo + hi) // 2
                    lo, hi = (mid + 1, hi) if b[mid] <= t else (lo, mid)
                while lo < len(a) and a[lo] < t + c - 1e-9:
                    t = max(t, b[lo])
                    lo += 1
                if best is None or t + c < best[1]:
                    best = (t, t + c, x, lo)
            start[i], end[i], went[i], lo = best
            taken[went[i][0]][0].insert(lo, start[i])
            taken[went[i][0]][1].insert(lo, end[i])
        order = sorted(range(n), key=lambda k: (start[k], k))
        total, chain = 0.0, []
        for k in range(m):
            free, by, last = {e: 0.0 for e in "vapcs"}, [None] * n, {}
            for i in order:
                e, c = went[i]
                t, by[i] = free[e], (last.get(e), True)
                for j, d in pre[k][i]:
                    if end[j] + d >= t:
                        t, by[i] = end[j] + d, (j, False)
                end[i] = free[e] = t + c[k]
                last[e] = i
            i = max(range(n), key=lambda q: end[q] + lat[q])
            total += (end[i] + lat[i]) * WEIGHT[k]
            while i is not None:
                if by[i][1] and by[i][0] is not None:
                    chain.append((i, by[i][0]))
                i = by[i][0]
        return total, order, [x[0] for x in went], chain, way

    more, x = [0.0] * n, 1
    best = place(more)
    for turn in range(PASSES):
        x = (x * 1103515245 + 12345) % 2 ** 31
        i, j = best[3][(x >> 8) % len(best[3])]
        step = 0.1 + (x >> 4) % 16 * 0.1
        new = list(more)
        if x >> 20 & 1:
            new[i] += max(best[4][j] - best[4][i], 0.0) + step
        else:
            new[j] = max(new[j] - step, -least[j] * 0.9) if x >> 21 & 1 else new[j] + step
        got = place(new)
        if got[0] <= best[0]:
            best, more = got, new
    return best[1], best[2]


ORDER = {}


def rank_program(g, core, T, topo):
    rank = T.rank_of(core)
    if rank is None:
        return
    Q = {"v": g.vector, "a": g.scalar, "p": g.tensor, "c": g, "s": g.sync}
    ops, lastw, reads, before = [], {}, {}, {}
    banks = ["P%d" % k for k in range(8)]

    def op(e, fn, rd, wr, cost, lat=0.0, sem=None):
        i, pre = len(ops), set()
        for k in sorted(set(rd + wr)):
            w = lastw.get(k, [])
            if k in wr and sem and w and ops[w[0]]["sem"] == sem:
                pre |= before[k]
                w.append(i)
                continue
            mine = set(w) | {r for r in reads.get(k, []) if k in wr or (k in banks and ops[r]["e"] != e)}
            pre |= mine
            if k in wr:
                lastw[k], reads[k], before[k] = [i], [], mine
            else:
                reads.setdefault(k, []).append(i)
        can = cost if e == "x" else {e: cost + 0 * CYC}
        ops.append({"e": e if e != "x" else "x%d" % i, "fn": fn if e == "x" else {e: fn}, "can": can, "lat": lat, "sem": sem,
                    "pre": {j: 0.0 if e == "p" == ops[j]["e"] else 1.0 for j in pre}})

    rows_of = {}

    def row(name):
        i = len(ops) - 1
        if name in rows_of:
            ops[i]["pre"].setdefault(rows_of[name], 0.0)
        rows_of[name] = i

    V, S = g.vector, g.scalar
    ga = lambda n: 60 + GAT * n
    sc = lambda n: 60 + SCA * n
    vc = lambda c: np.maximum(64, c) * CYC

    def dma(e, out, in_, rd, wr, sem, lat, behind=0):
        op(e, lambda: Q[e].dma_start(out, in_), rd, wr, 0.05, lat, (sem, 16))
        for j in range(len(ops) - 1 - behind, len(ops) - 1):
            ops[-1]["pre"][j] = -1.0

    def ts(out, in0, s1, s2, o0, o1, rd, wr, c=64):
        if s2 is None:
            op("v", lambda: V.tensor_scalar(out, in0, s1, None, o0), rd, wr, vc(c))
        else:
            op("v", lambda: V.tensor_scalar(out, in0, s1, s2, o0, o1), rd, wr, vc(c))

    def tt(out, a, b, o, rd, wr, c=64):
        op("v", lambda: V.tensor_tensor(out, a, b, o), rd, wr, vc(c))

    def cp(out, a, rd, wr, c=64):
        op("v", lambda: V.tensor_copy(out, a), rd, wr, vc(c))

    def scan(out, a, b, ini, o0, o1, rd, wr, c=192):
        op("v", lambda: V.tensor_tensor_scan(out, a, b, ini, o0, o1), rd, wr, vc(c))

    def ms(ap, x, wr, c=64):
        op("v", lambda: V.memset(ap, x), [], wr, vc(c))

    def act(out, a, rd, wr, func=F.Identity, bias=0.0, scale=1.0, c=128):
        if isinstance(bias, float) and isinstance(scale, float) and (bias, scale) == (0.0, 1.0):
            op("a", lambda: S.activation(out, a, func), rd, wr, 0.05 + vc(c))
        else:
            op("a", lambda: S.activation(out, a, func, bias=bias, scale=scale), rd, wr, 0.05 + vc(c))

    def line(out, src, w, x, rd, wr, ca, cv):
        op("x", {"v": lambda: V.tensor_scalar(out, src, w, x, A.mult, A.add), "a": lambda: S.activation(out, src, F.Identity, bias=x, scale=w)},
           rd, wr, {"v": vc(cv), "a": 0.05 + vc(ca)})

    def scaled(out, src, w, rd, wr, c=128):
        line(out, src, w, 0.0, rd, wr, c, c // 2)

    def pick(out, src, rd, wr, n, w=1.0):
        line(out, src, w, 0.0, rd, wr, GAT * n, ga(n))

    def mms(calls, rd, wr, n):
        def fn():
            for a in calls:
                ins = g.tensor.matmul(*a)
            return ins
        op("p", fn, rd, wr, len(calls) * max(64, n) * PEC)

    def mm(out, l, r, start, stop, rd, wr, n=192):
        mms([(out, l, r, start, stop)], rd, wr, n)

    def wrap(out, z, src, rd, wr, n, start=True, stop=True):
        mms([(out, z(i), src(i), start and i == 0, stop and i == 15) for i in range(16)], rd, wr, n)

    def iota(out, p, base, cm, wr, n, flag=True):
        if flag:
            op("c", lambda: g.iota(out, p, base, cm, allow_small_or_imprecise_dtypes=True), [], wr, 0.13 + 2 * n * CYC)
        else:
            op("c", lambda: g.iota(out, p, base, cm), [], wr, 0.13 + 2 * n * CYC)

    def asel(out, a, p, o, fill, base, cm, rd, wr, n=128):
        op("c", lambda: g.affine_select(out, a, p, o, fill, base, cm), rd, wr, 0.17 + 2 * n * CYC)

    P = [T["P%d" % k] for k in range(8)]
    pk = lambda k: "P%d" % k
    col = lambda k: T.col[:, k:k + 1]
    Rr = lambda k: T.R[:, k:k + 1]
    (PM, C15, WU, WAE, WAO, WOCC, WY, WO2, WE0, WE1, WE2, MV, OFF, OFF1, BSEL, I192, TMP, OFA0, OFA1, OFS, BS2, P16, U0, U1, WH, PB, OFS1) = range(27)
    (Z1, ZU, ZFE, ZFO) = range(4)
    zt = lambda n: T.Z[:, 144 * n:144 * n + 144]
    zw = lambda n: (lambda i: T.Z[:, 144 * n + 15 - i:144 * n + 143 - i])
    (BAE, BAO, BIRTH, B256, B4096N, BOCC, BGW, BHOME, BNEG, BY, BU, B2) = range(12)
    bdv = lambda n: T.BDv[:, 128 * n:128 * n + 128]
    XSk = ["XS", "XSa", "XSb"]
    DSk = ["DS0", "DS1", "DSa"]
    DQk = ["DQ%d" % c for c in range(16)] + ["DQa"]
    XBk = {0: ["XBe%d" % c for c in range(8)] + ["XBea"], 1: ["XBo%d" % c for c in range(8)] + ["XBoa"]}
    XBt = {0: T.XBe, 1: T.XBo}

    dma("s", T.blk[:], T.board[:], [], ["blk"], "blk", 1.4)
    dma("s", T.XS[:, 0:2048], T.xs[:], [], ["XS"], "xs", 3.0, 1)
    dma("s", T.DS[0:64, 0:2048], T.ds[0:64, :], [], ["DS0"], "ds0", 4.6, 1)
    if not DSLATE:
        dma("s", T.DS[64:128, 0:2048], T.ds[64:128, :], [], ["DS1"], "ds1", 6.2, 1)
    dma("s", T.hmb[:], T.hm[:], [], ["hmb"], "hmb", 6.5, 1)

    iota(T.pI[:, 0:1], [[0, 1]], 0, 1, ["pI"], 1, False)
    iota(T.colI[:], [[1, 192]], 0, 0, ["colI"], 192)
    ms(T.one[:], 1.0, ["one"])
    asel(T.Id[:], T.one[:], [[-1, 128]], A.is_equal, 0.0, 0, 1, ["one"], ["Id"])
    asel(T.BD[:], T.one[:], [[-16, 8], [0, 16]], A.is_ge, 0.0, 0, 1, ["one"], ["BD"])
    asel(T.BD[:], T.BD[:], [[16, 8], [0, 16]], A.is_ge, 0.0, 15, -1, ["BD"], ["BD"])
    iota(T.J16[:], [[0, 13], [1, 16]], 0, 0, ["J16"], 208)
    asel(T.Tri[:], T.BD[:], [[1, 128]], A.is_ge, 0.0, 0, -1, ["BD"], ["Tri"])
    JW, K2, K3 = T.jw[:, 0:12], T.jw[:, 12:24], T.jw[:, 24:36]
    iota(JW, [[16, 12]], D0, 0, ["jw"], 12)
    for k, (a, b) in enumerate(VSH):
        iota(T.XZ[:, 16 * a:16 * b], [[0, 16 * (b - a)]], 0, 0, ["XZ%d" % k], 16 * (b - a))
    for c in range(12):
        act(T.SQ[:, 188 * c:188 * c + 188], T.colI[:, 0:188], ["colI"], ["SQ%d" % c], F.Identity, 188.0 * c, c=188)
        row("SQ")
    SQk = ["SQ%d" % c for c in range(12)]
    for c in range(8):
        ms(T.TB[:, GW // 8 * c:GW // 8 * (c + 1)], 0.0, ["TB%d" % c], GW // 16)
    ms(T.XS[:, 2048:2064], 1e9, ["XSa"])
    ms(T.XS[:, 2064:2080], -1e9, ["XSb"])
    ms(T.DS[:, 2048:2080], 0, ["DSa"])
    ms(T.DQ[:, 2048:2064], 0, ["DQa"])
    ms(T.XBe[:, 2048:2064], -1e9, ["XBea"])
    ms(T.XBo[:, 2048:2064], -1e9, ["XBoa"])
    ms(T.CE[:, 0:16], 0.0, ["CE0"])
    ms(T.H[:, 0:1], 3 * BB, ["H0"])
    ms(T.H5[:, 77:624:48], 0.0, ["H5z"])
    ms(T.D3[:, 0:36:3], 0.0, ["D3a"])
    ms(T.D3[:, 2:36:3], 1.0, ["D3b"])
    ts(T.pJ[:, 0:1], T.pI[:, 0:1], 15, None, A.bitwise_and, None, ["pI"], ["pJ0"])
    ts(T.pJ[:, 1:2], T.pI[:, 0:1], 112, None, A.bitwise_and, None, ["pI"], ["pJ1"])
    ts(T.pJ[:, 2:3], T.pI[:, 0:1], 16, None, A.bitwise_and, None, ["pI"], ["pJ2"])
    cp(col(PM), T.pJ[:, 0:1], ["pJ0"], ["PM"])
    ts(col(C15), T.pJ[:, 1:2], 15.0, None, A.add, None, ["pJ1"], ["C15"])
    ts(col(P16), T.pI[:, 0:1], 16.0, None, A.add, None, ["pI"], ["P16"])
    for u in range(2):
        ts(col(U0 + u), T.pJ[:, 2:3], 16.0 * u, None, A.is_equal, None, ["pJ2"], ["U%d" % u])
        ts(T.PW[:, 160 * u:160 * u + 160], T.colI[:, 0:160], col(P16), col(U0 + u), A.is_equal, A.mult, ["colI", "P16", "U%d" % u], ["PW%d" % u], 80)
    ts(T.R[:], T.colI[:, 0:16], col(PM), None, A.is_equal, None, ["colI", "PM"], ["R"])
    ts(zt(Z1), T.colI[:, 0:144], col(C15), None, A.is_equal, None, ["colI", "C15"], ["Z1"], 72)
    lc = lambda k, src, w, x, rd, wr: line(col(k), src, w, x, rd, [wr], 64, 64)
    lc(TMP, Rr(0), 256.0, Rr(1), ["R"], "TMP")
    lc(WU, col(TMP), 2.0, Rr(8), ["TMP", "R"], "WU")
    lc(WAE, Rr(2), -2064.0, col(WU), ["R", "WU"], "WAE")
    lc(WAO, Rr(3), -2064.0, col(WU), ["R", "WU"], "WAO")
    lc(WOCC, Rr(2), 1.0, Rr(3), ["R"], "WOCC")
    lc(WY, col(WOCC), -2048.0, col(WU), ["WOCC", "WU"], "WY")
    lc(WO2, col(WOCC), float(GW), 0.0, ["WOCC"], "WO2")
    for t in range(3):
        lc(WE0 + t, Rr(4 + t), 1.0, col(WOCC), ["R", "WOCC"], "WE%d" % t)
    ts(col(TMP + 12), Rr(0), Rr(1), Rr(8), A.add, A.add, ["R"], ["MA"])
    lc(MV, col(TMP + 12), 1.0, col(WOCC), ["MA", "WOCC"], "MV")
    lc(OFF, Rr(15), -BB, BB, ["R"], "OFF")
    for k, x in ((OFF1, 1.0), (OFA0, -2064.0), (OFS, 2048.0)):
        lc(k, Rr(15), -BB, BB + x, ["R"], "c%d" % k)
    lc(BSEL, col(PM), -2048.0, -2048.0, ["PM"], "BSEL")
    lc(BS2, col(PM), -4096.0, 0.0, ["PM"], "BS2")
    lc(I192, col(PM), 192.0, 0.0, ["PM"], "I192")
    lc(WH, Rr(9), 256.0, Rr(7), ["R"], "WH")
    lc(TMP + 13, Rr(9), float(H0 // 256), 0.0, ["R"], "PBa")
    lc(PB, Rr(7), 32.0 * rank, col(TMP + 13), ["R", "PBa"], "PB")
    ts(T.AB[:, 0:192], T.J16[:, 0:192], col(PM), -4 * BB, A.is_equal, A.mult, ["J16", "PM"], ["HDa"], 96)
    ts(T.EA[:, 0:192], T.J16[:, 15:207], col(PM), BB, A.is_equal, A.mult, ["J16", "PM"], ["HDb"], 96)
    tt(T.HD2[:], T.AB[:, 0:192], T.EA[:, 0:192], A.add, ["HDa", "HDb"], ["HD2"], 384)
    ts(T.PAT[:], T.J16[:, 15:207], col(PM), BB, A.not_equal, A.mult, ["J16", "PM"], ["PAT"], 96)
    ts(T.HZ[:], T.J16[:, 0:192], col(PM), None, A.not_equal, None, ["J16", "PM"], ["HZ"], 96)
    scaled(T.PATn[:], T.HZ[:], -BB, ["HZ"], ["PATn"], 192)
    ts(K2, JW, col(PM), col(OFS), A.add, A.add, ["jw", "PM", "c%d" % OFS], ["K2"])
    ts(K3, JW, col(PM), float(BD0 + 1 - D0), A.add, A.add, ["jw", "PM"], ["K3"])
    scaled(T.cm64[:], T.colI[:, 0:128], -64.0, ["colI"], ["cm64"])
    for t in range(3):
        act(T.WIN[:, 2304 * t:2304 * t + 192], T.colI[:], ["colI"], ["WIN%d" % t], F.Silu, 0.0, 0.0, 192 + (1500 if t == 0 else 0))
        row("WIN")
        line(T.GH[:, 192 * t:192 * t + 192], T.colI[:], 0.0, Rr(4 + t), ["colI", "R"], ["GH%d" % t], 192, 96)
        for p in range(4):
            c0 = 960 * t + 192 * p
            line(T.MSG[:, c0:c0 + 32], T.colI[:, 0:32], Rr(7), col(PB), ["colI", "R", "PB"], ["MSG%d%d" % (t, p)], 64, 64)
    line(T.c192[:], T.colI[:, 0:128], 0.0, 4096.0, ["colI"], ["c192"], 128, 64)
    scaled(T.ZR[:], T.colI[:], 0.0, ["colI"], ["ZR"], 192)
    c65k = []
    for a, b, x in [v + (0.0,) for v in VSH] + [v + (6.5,) for v in ASH]:
        ms(T.c65[:, a:b], x, ["c65%d" % a])
        c65k.append("c65%d" % a)
    scaled(T.Id16[:], T.Id[:], 1.0, ["Id"], ["Id16"])
    scaled(T.IdK[:, 0:128], T.Id[:], 4096.0, ["Id"], ["IdK0"])
    scaled(T.IdK[:, 128:256], T.Id[:], -4096.0, ["Id"], ["IdK1"])
    scaled(T.Idn[:], T.Id[:], -1.0, ["Id"], ["Idn"])
    line(T.K16[:], T.colI[:, 0:128], 2.0, 2048.0, ["colI"], ["K16"], 128, 64)
    scaled(T.BDm[:], T.BD[:], -4096.0, ["BD"], ["BDm"])
    line(T.sq2[:], T.colI[:, 0:128], 16.0, col(PM), ["colI", "PM"], ["sq2"], 128, 128)
    for k in range(4):
        ts(T.HOLD[:, 160 * k:160 * k + 160], T.J16[:, 0:160], 0.0, None, A.not_equal, None, ["J16"], ["HOLD%d" % k], 80)
    HOLDk = ["HOLD%d" % k for k in range(4)]
    for k, w, wk in ((BAE, col(WAE), "WAE"), (BAO, col(WAO), "WAO"), (BIRTH, Rr(0), "R"), (B256, 256.0, "BD"), (B2, 2.0, "BD"), (B4096N, -4096.0, "BD"),
                     (BOCC, col(WOCC), "WOCC"), (BGW, col(WO2), "WO2"), (BHOME, col(WH), "WH"), (BNEG, -1.0, "BD"), (BY, col(WY), "WY")):
        scaled(bdv(k), T.BD[:], w, ["BD", wk], ["BD%d" % k])
    scaled(bdv(BU), T.BD[:], col(WU), ["BD", "WU"], ["BD%d" % BU])
    scaled(T.BDh[:, 0:128], T.BD[:], 1.0, ["BD"], ["BDh0"])
    scaled(T.BDh[:, 128:256], T.BD[:], 0.0625, ["BD"], ["BDh1"])
    scaled(T.BDn[:], T.BD[:], -2048.0, ["BD"], ["BDn"])
    asel(T.BDn[:], T.BDn[:], [[1, 128]], A.is_gt, 0.0, 0, -1, ["BDn"], ["BDn"])
    asel(T.M1[:], T.BDn[:], [[1, 128]], A.not_equal, 2048.0, 0, -1, ["BDn"], ["M1"])
    scaled(zt(ZU), zt(Z1), col(WU), ["Z1", "WU"], ["ZU"], 144)
    scaled(zt(ZFE), zt(Z1), Rr(2), ["Z1", "R"], ["ZF0"], 144)
    scaled(zt(ZFO), zt(Z1), Rr(3), ["Z1", "R"], ["ZF1"], 144)
    ms(T.EQ[:, 0:512], 1.0, ["EQ0"], 256)
    for k, (a, b) in enumerate(ASH):
        asel(T.SP[:, 512 * k:512 * k + 16 * (b - a)], T.EQ[:, 0:16 * (b - a)], [[-1, b - a], [0, 16]], A.is_equal, 0.0, ASH[0][0] - a, 1, ["EQ0"], ["SP%d" % k], 16 * (b - a))
    iota(T.BIG[:], [[0, 192]], 8388608, 0, ["BIG"], 192)
    iota(T.HM[:], [[0, 2080]], 0, 0, ["HM"], 2080)
    ts(T.W[:, 0:144], T.colI[:, 0:144], col(C15), 4096.0, A.is_gt, A.mult, ["colI", "C15"], ["Wa"], 72)
    scaled(T.W[:, 144:288], zt(Z1), -4096.0, ["Z1"], ["Wb"], 144)
    tt(T.W[:, 0:144], T.W[:, 0:144], T.W[:, 144:288], A.add, ["Wa", "Wb"], ["Wa"], 288)
    for k in range(16):
        asel(T.TS[:, 128 * k:128 * k + 128], T.W[:, 15 - k:143 - k], [[-16, 8], [0, 16]], A.is_ge, 0.0, 0, 1, ["Wa"], ["TS%d" % k])
        row("TS")
    TSk = ["TS%d" % k for k in range(16)]

    def rewrap(bank, src, sk, c0=0):
        calls = []
        for be in range(4):
            for u in range(2):
                for h in range(2):
                    x = 160 * u + 16 - 16 * (h - u)
                    calls.append((P[bank][:, 2 * be + u:128:8], T.PW[:, x:x + 128], src[:, c0 + 32 * be + 16 * h:c0 + 32 * be + 16 * h + 16], not calls, len(calls) == 15))
        mms(calls, ["PW0", "PW1", sk], [pk(bank)], 64)

    ts(T.xb[:], T.blk[:], 2049, None, A.bitwise_and, None, ["blk"], ["xb"], 128)
    ts(T.fe[:], T.xb[:], 0.0, None, A.is_equal, None, ["xb"], ["fe"], 128)
    op("v", lambda: V.transpose(T.feT[:], T.fe[:]), ["fe"], ["feT"], vc(64))
    rewrap(0, T.feT, "feT")
    cp(T.o16[:], T.blk[:], ["blk"], ["o16"], 128)
    op("v", lambda: V.transpose(T.oT[:], T.o16[:]), ["o16"], ["oT"], vc(64))
    ts(T.oo[:, 0:128], T.xb[:], 0.0, 2048.0, A.is_equal, A.mult, ["xb"], ["oo"], 128)
    tt(T.oo[:, 0:128], T.oo[:, 0:128], T.o16[:], A.max, ["oo", "o16"], ["oo"], 256)
    op("v", lambda: V.transpose(T.oo[:, 128:256], T.oo[:, 0:128]), ["oo"], ["ooT"], vc(64))
    rewrap(5, T.oo, "ooT", 128)
    cp(T.offx[:, 0:128], P[5][:, 0:128], ["P5"], ["offo"], 128)
    rewrap(7, T.oT, "oT")
    act(T.Uw[:], P[7][:, 0:128], ["P7"], ["Uw"])
    cp(T.offx[:, 256:384], P[7][:, 0:128], ["P7"], ["offu"], 128)
    ts(T.rows[:, 256:384], T.xb[:], 0.0, None, A.is_equal, None, ["xb"], ["r2"], 128)
    ts(T.rows[:, 384:512], T.xb[:], 1.0, None, A.is_equal, None, ["xb"], ["r3"], 128)
    ts(T.ti[:, 0:128], T.blk[:], 9, 3, A.logical_shift_right, A.bitwise_and, ["blk"], ["ti0"], 128)
    ts(T.ti[:, 128:256], T.blk[:], 1, 255, A.logical_shift_right, A.bitwise_and, ["blk"], ["ti1"], 128)
    cp(T.rows[:, 0:256], T.ti[:, 0:256], ["ti0", "ti1"], ["r01"], 256)
    for r, c0, k in ((2, 256, "r2"), (3, 384, "r3"), (8, 384, "r3"), (0, 0, "r01"), (1, 128, "r01")):
        dma("s", T.TB[r:128:16, 0:2048], T.rows[:, c0:c0 + 128], [k] + ["TB%d" % c for c in range(8)], ["TB"], "tb", TBL)
    if DSLATE:
        dma("s", T.DS[64:128, 0:2048], T.ds[64:128, :], [], ["DS1"], "ds1", 3.5, 5)
    ts(T.ti[:, 256:384], T.hmb[:], 255, None, A.bitwise_and, None, ["hmb"], ["ti2"], 128)
    ts(T.ti[:, 384:512], T.hmb[:], 8, None, A.logical_shift_right, None, ["hmb"], ["ti3"], 128)
    cp(T.rows[:, 512:768], T.ti[:, 256:512], ["ti2", "ti3"], ["r79"], 256)
    for r, c0 in ((7, 512), (9, 640)):
        dma("s", T.HM[r:128:16, 0:2048], T.rows[:, c0:c0 + 128], ["r79"], ["HM"], "hm", 2.5)

    def xb_build(par, c0, ok):
        for c in range(8):
            act(XBt[par][:, 256 * c:256 * c + 256], T.XS[:, 0:2080].indirect(T.offx[:, c0 + 16 * c:c0 + 16 * c + 16]), XSk + [ok], [XBk[par][c]], F.Copy, c=GAT * 256)
            row("XB")

    def xb_clear(par, off, ok):
        op("a", lambda: S.activation(XBt[par][:].indirect(off), T.BIG[:], F.Silu), ["BIG", ok], XBk[par], vc(sc(192)))

    def targets(out, off, ok, key):
        if MOD and key != "qB0":
            cp(out, T.DQ[:, 0:2064].indirect(off), DQk + [ok], [key[:2]], ga(192))
        else:
            ts(T.qx[:], T.DQ[:, 0:2064].indirect(off), 2047, None, A.bitwise_and, None, DQk + [ok], ["qx"], ga(192))
            cp(out, T.qx[:], ["qx"], [key[:2]], 192)

    def ring(n):
        if MOD:
            ts(T.qz[:, 0:n], T.qy[:, 0:n], 2047, None, A.bitwise_and, None, ["qy"], ["qz"], n)
        return (T.qz[:, 0:n], "qz") if MOD else (T.qy[:, 0:n], "qy")

    def hold(out, src, n, rd, wr):
        scan(out, T.HD2[:, 0:n], src, 2 * BB, A.add, A.max, ["HD2"] + rd, wr, n)

    def dedupe(kv, ka, kp, pd, w, wk, early, stop, NB):
        hold(T.H[:, 1:193], P[kv][:, 0:192], 192, [pk(kv)], ["H"])
        early()
        act(T.keyr[:], P[ka][:, 0:192], [pk(ka)], ["keyr"], c=192)
        ts(T.keyw[:], T.H[:, 16:193:16], col(OFF), None, A.subtract, None, ["H", "OFF"], ["keyw"])
        ea0 = [0]
        for b in range(NB, 11):
            ea0.append(ea0[-1] + 176 - 16 * b)
            act(T.AB[:, ea0[-2]:ea0[-1]], P[ka][:, 16 * b + 16:192], [pk(ka), "keyw"], ["AB%d" % b], F.Abs, T.keyw[:, b:b + 1], -1.0, 176 - 16 * b)
            row("AB")
        if NB < 11:
            act(T.EA[:, 0:ea0[-1]], T.AB[:, 0:ea0[-1]], ["AB%d" % b for b in range(NB, 11)], ["EA"], F.Relu, 1.0, -1.0, ea0[-1])
        tt(T.EQ[:, 0:192], T.H[:, 0:192], P[kp][:, 0:192], A.is_equal, ["H", "H0", pk(kp)], ["EQ0"], 192)
        mm(P[pd][:, 0:192], w, T.EQ[:, 0:192], False, False, [wk, "EQ0"], [pk(pd)])
        for b in range(NB):
            e = T.EQ[:, 208 * b + 208:192 * b + 384]
            ts(e, T.keyr[:, 16 * b + 16:192], T.keyw[:, b:b + 1], None, A.is_equal, None, ["keyr", "keyw"], ["EQ%d" % (b + 1)], 88 - 8 * b)
            row("EQ")
            mm(P[pd][:, 16 * b + 16:192], w, e, False, stop and b == 10, [wk, "EQ%d" % (b + 1)], [pk(pd)], 176 - 16 * b)
        if NB < 11:
            mms([(P[pd][:, 16 * b + 16:192], w, T.EA[:, ea0[b - NB]:ea0[b - NB + 1]], False, stop and b == 10) for b in range(NB, 11)], [wk, "EA"], [pk(pd)], 64)

    w12 = lambda k: T.w12[:, 12 * k:12 * k + 12]
    peers = [p for p in range(len(T.cores)) if p != rank]
    peers = peers[rank % 3:] + peers[:rank % 3]
    CMPk = ["CMP%d" % c for c in range(6)]

    for t in range(3):
        odd = t & 1
        XB, XK = XBt[1 - odd], XBk[1 - odd]
        swu, boff, endu, roff, aw = [x[:, n * t:n * t + n] for x, n in ((T.swu, 12), (T.boff, 12), (T.endu, 12), (T.roff, 8), (T.aw, 12))]
        sk, bk, ek, rk, wk, ak = ["%s%d" % (n, t) for n in ("swu", "boff", "endu", "roff", "WIN", "aw")]
        mk = ["MSG%d%d" % (t, p) for p in range(4)]
        if t > 0:
            wrap(P[0][:, 0:128], zw(ZFO if odd else ZFE), lambda i: T.TB[:, i:2048:16], ["TB", "ZF%d" % odd], ["P0"], 128)
            pe, pa = T.endu[:, 12 * t - 12:12 * t], T.aw[:, 12 * t - 12:12 * t]
            cp(XB[:].indirect(pe), T.XZ[:, 0:3072:16], ["XZ", "endu%d" % (t - 1)], XK, sc(192))
            pick(T.ef[:], T.SQ[:, 0:2256].indirect(pe), SQk + ["endu%d" % (t - 1)], ["ef"], 192)
            tt(T.qy[:], T.DS[:].indirect(pa), T.ef[:], A.add, DSk + ["aw%d" % (t - 1), "ef"], ["qy"], ga(192))
            qn, qk = ring(192)
        act(T.Fw[:], P[0][:, 0:128], ["P0"], ["Fw"])
        mm(P[2][:, 0:128], T.BD[:], T.Fw[:], True, True, ["BD", "Fw"], ["P2"], 128)
        mm(P[6][:, 0:128], T.Id16[:], T.K16[:], True, False, ["Id16", "K16"], ["P6"], 128)
        mm(P[6][:, 0:128], T.BDm[:], T.Fw[:], False, True, ["BDm", "Fw"], ["P6"], 128)
        mm(P[1][:, 0:128], T.Id[:], T.cm64[:], True, False, ["Id", "cm64"], ["P1"], 128)
        mm(P[1][:, 0:128], T.Tri[:], T.Fw[:], False, True, ["Tri", "Fw"], ["P1"], 128)
        act(T.V0[:], P[1][:, 0:128], ["P1"], ["V0"], F.Identity, 64 + 32.5 / 128, -1.0 / 128)
        if t == 0:
            xb_build(1, 0, "offo")
        scan(T.CE[:, 16:144], P[2][:, 0:128], T.c192[:], 0.0, A.add, A.min, ["P2", "c192"], ["CE"], 128)
        tt(T.HS[:], T.CE[:, 15:143], P[6][:, 0:128], A.max, ["CE", "CE0", "P6"], ["HS"], 128)
        ts(T.G[:], T.colI[:], T.CE[:, 143:144], None, A.is_equal, None, ["colI", "CE"], ["G"], 96)
        line(T.d0[:], T.G[:], 128.0, 1.0 / 128, ["G"], ["d0"], 192, 96)
        hold(T.H4[:], T.HS[:], 128, ["HS"], ["H4"])
        ts(T.coff[:], T.H4[:, 15:128:16], col(OFF), None, A.subtract, None, ["H4", "OFF"], ["coff"])
        act(T.WIN[:, 2304 * t:2304 * t + 2304].indirect(T.coff[:]), T.V0[:], ["V0", "coff"], [wk], F.Silu, c=SCA * 128)
        scan(T.SB[:], T.d0[:], T.WIN[:, 2304 * t:2304 * t + 192], 64.0, A.add, A.max, ["d0", wk], ["SB"])
        mm(P[3][:, 0:192], bdv(B2), T.SB[:], True, True, ["BD%d" % B2, "SB"], ["P3"])
        hold(T.SH[:], P[3][:, 0:192], 192, ["P3"], ["SH"])
        ts(T.swg[:], T.SH[:, 15:192:16], col(OFS), 2048.0, A.subtract, A.min, ["SH", "c%d" % OFS], ["swg"])
        XZk = ["XZ0", "XZ1", "XZ2"]
        if t > 0:
            targets(T.qA[:], T.swg[:], "swg", "qA")
            cp(T.DQ[:].indirect(pe), qn, [qk, "endu%d" % (t - 1)], DQk, sc(192))
            act(T.XZ[:, 0:3072:16], XBt[odd][:, 0:2064].indirect(T.swg[:]), XBk[odd] + ["swg"] + XZk, ["XZ"], F.Copy, c=GAT * 192)
        pick(T.acol[:], T.TB[:, 0:GW].indirect(T.swg[:]), ["TB", "swg"], ["acol"], 192)
        mm(P[3][:, 0:192], bdv(odd), T.acol[:], True, True, ["BD%d" % odd, "acol"], ["P3"])
        hold(T.HA[:], P[3][:, 0:192], 192, ["P3"], ["HA"])
        ts(aw, T.HA[:, 15:192:16], col(OFA0), None, A.subtract, None, ["HA", "c%d" % OFA0], [ak])
        if t == 2:
            act(T.ua[:], P[3][:, 0:192], ["P3"], ["ua"], F.Identity, 2064.0, c=192)
        tt(T.swf[:], T.SH[:, 15:192:16], K2, A.min, ["SH", "K2"], ["swf"])
        ts(swu, T.swf[:], col(OFS), None, A.subtract, None, ["swf", "c%d" % OFS], [sk])
        if t == 0:
            mm(P[4][:, 0:192], bdv(B2), T.SB[:], True, True, ["BD%d" % B2, "SB"], ["P4"])
            act(T.srep[:], P[4][:, 0:192], ["P4"], ["srep"], F.Identity, -2048.0, c=192)
            act(T.XZ[:, 0:3072:16], T.XS[:, 0:2080].indirect(aw), XSk + [ak] + XZk, ["XZ"], F.Copy, c=GAT * 192)
            tt(T.qx[:], T.DS[:].indirect(aw), T.srep[:], A.add, DSk + [ak, "srep"], ["qx"], ga(192))
            ts(T.q32[:], T.qx[:], 2047, None, A.bitwise_and, None, ["qx"], ["q32"], 192)
            cp(T.qA[:], T.q32[:], ["q32"], ["qA"], 192)
            act(T.mov[:], T.sq2[:], ["sq2", "srep"], ["mov"], F.Sign, T.srep[:, 191:192], -1.0)
            mm(P[7][:, 0:128], T.Id16[:], T.Uw[:], True, False, ["Uw", "Id16"], ["P7"], 128)
            mm(P[7][:, 0:128], T.IdK[:, 128:256], T.Fw[:], False, False, ["Fw", "IdK1"], ["P7"], 128)
            mm(P[7][:, 0:128], T.IdK[:, 0:128], T.mov[:], False, True, ["mov", "IdK0"], ["P7"], 128)
            ts(T.offx[:, 128:256], P[7][:, 0:128], 8192.0, 2048.0, A.add, A.min, ["P7"], ["offe"], 128)
            xb_build(0, 128, "offe")
            w = 2048 // NQ
            for c in range(NQ):
                tt(T.DQ[:, w * c:w * c + w], T.DS[:].indirect(T.offx[:, 256 + w * c // 16:256 + (w * c + w) // 16]), T.SQ[:, w * c:w * c + w], A.add,
                   DSk + SQk + ["offu"], DQk[16 // NQ * c:16 // NQ * (c + 1)], ga(w))
                row("DQ")
        if t == 1:
            xb_clear(1, T.endu[:, 0:12], "endu0")
            xb_clear(1, swu, sk)
        ts(T.q1[:], T.qA[:], 1.0, None, A.add, None, ["qA"], ["q1"], 96)

        def spread(a, b, c):
            scan(T.XA[:, 16 * a:16 * b], T.HOLD[:, 0:16 * (b - a)], T.XZ[:, 16 * a:16 * b], 0.0, A.mult, A.add, HOLDk + ["XZ"], ["XA%d" % c], 8 * (b - a))

        def cmpv(a, b, c):
            tt(T.CMP[:, 16 * a:16 * b], XB[:, 0:2048].indirect(T.qA[:, a:b]), T.XA[:, 16 * a:16 * b], A.is_lt, XK + ["qA", "XA%d" % c], [CMPk[c]], ga(16 * (b - a)))

        a0 = ASH[0][0]
        mm(P[5][:, 0:128], T.XZ[:, 16 * a0:16 * a0 + 2048:16], T.Id[:], True, True, ["Id", "XZ"], ["P5"], 128)
        act(T.XT[:], P[5][:, 0:128], ["P5"], ["XT"])

        def cmpa(bank, a, b, c):
            n = 16 * (b - a)
            mm(P[bank][:, 0:n], T.XT[:], T.SP[:, 512 * bank:512 * bank + n], True, False, ["SP%d" % bank, "XT"], [pk(bank)], n)
            act(T.XA[:, 16 * a:16 * b], XB[:, 0:2048].indirect(T.qA[:, a:b]), XK + ["qA"], ["XA%d" % c], F.Copy, c=GAT * n)
            row("gat")
            mm(P[bank][:, 0:n], T.Idn[:], T.XA[:, 16 * a:16 * b], False, True, ["Idn", "XA%d" % c], [pk(bank)], n)
            act(T.CMP[:, 16 * a:16 * b], P[bank][:, 0:n], [pk(bank)], [CMPk[c]], F.Sign, -TINY, c=n)

        def count(bank, a, b, ks, stop):
            wrap(P[bank][:, a:b], zw(Z1), lambda i: T.CMP[:, 16 * a + i:16 * b:16], ["Z1"] + ks, [pk(bank)], b - a, False, stop)

        def choose(a, b, bc, bs, bf_, n):
            mm(P[bs][:, a:b], T.Id16[:], T.q1[:, a:b], True, False, ["Id16", "q1"], [pk(bs)], b - a)
            mm(P[bf_][:, a:b], bdv(B2), T.SB[:, a:b], True, False, ["BD%d" % B2, "SB"], [pk(bf_)], b - a)
            act(T.sg[:, a:b], P[bc][:, a:b], [pk(bc)], ["sg%d" % n], F.Sign, -9.5, c=b - a)
            mm(P[bs][:, a:b], T.M1[:], T.sg[:, a:b], False, True, ["M1", "sg%d" % n], [pk(bs)], b - a)
            mm(P[bf_][:, a:b], bdv(B4096N), T.sg[:, a:b], False, True, ["BD%d" % B4096N, "sg%d" % n], [pk(bf_)], b - a)
            if n:
                ts(T.sel[:, a:b], P[bs][:, a:b], col(BSEL), 0.0, A.add, A.max, [pk(bs), "BSEL"], ["sel%d" % n], b - a)
            else:
                act(T.sel[:, a:b], P[bs][:, a:b], [pk(bs), "BSEL"], ["sel%d" % n], F.Relu, col(BSEL), c=b - a)
            act(T.fb[:, a:b], P[bf_][:, a:b], [pk(bf_)], ["fb%d" % n], F.Relu, -2047.0 - 65536.0, c=b - a)

        def keys(k, a, b, n, first):
            if k == 3 and first:
                mm(P[k][:, 0:192], T.Id[:], T.PAT[:], True, False, ["Id", "PAT"], [pk(k)])
            mms([(P[k][:, a:b], T.BDh[:, 0:128], T.sel[:, a:b], first and k != 3, False), (P[k][:, a:b], T.BDh[:, 128:256], T.fb[:, a:b], False, not first)],
                ["sel%d" % n, "fb%d" % n, "BDh0", "BDh1"], [pk(k)], b - a)

        half, cut = ASH[0][1], ASH[1][1]
        for c, (a, b) in enumerate(ASH):
            cmpa(c, a, b, 3 + c)
        for f, c in ((spread, 0), (spread, 1), (cmpv, 0), (spread, 2), (cmpv, 1), (cmpv, 2)):
            f(VSH[c][0], VSH[c][1], c)
            row("cmp")
        mm(P[6][:, 0:cut], T.Id[:], T.c65[:, 0:cut], True, False, ["Id"] + c65k, ["P6"], cut)
        mm(P[4][:, cut:192], T.Id[:], T.c65[:, cut:192], True, False, ["Id"] + c65k, ["P4"], 64)
        count(6, 0, half, [CMPk[0], CMPk[3]], False)
        count(6, half, cut, [CMPk[1], CMPk[4]], True)
        count(4, cut, 192, [CMPk[2], CMPk[5]], True)
        choose(0, cut, 6, 5, 0, 0)
        choose(cut, 192, 4, 1, 2, 1)
        for k in (7, 0, 3):
            keys(k, 0, cut, 0, True)
            keys(k, cut, 192, 1, False)
        cp(T.TB[:].indirect(swu), T.GH[:, 192 * t:192 * t + 192], ["GH%d" % t, sk], ["TB"], sc(192))
        pick(T.hcol[:], T.HM[:].indirect(aw), ["HM", ak], ["hcol"], 192)
        mm(P[1][:, 0:192], bdv(BIRTH), T.acol[:], True, False, ["BD%d" % BIRTH, "acol"], ["P1"])
        mm(P[1][:, 0:192], T.BDh[:, 0:128], T.fb[:], False, False, ["fb0", "fb1", "BDh0"], ["P1"])

        def early1():
            ts(T.atw[:], T.H[:, 16:193:16], col(OFF1), 2048.0, A.subtract, A.min, ["H", "c%d" % OFF1], ["atw"])
            targets(T.qB[:], T.atw[:], "atw", "qB%d" % t)
            if t == 0 and MOD:
                w = 2048 // NM
                for c in range(NM):
                    ks = DQk[16 // NM * c:16 // NM * (c + 1)]
                    ts(T.DQ[:, w * c:w * c + w], T.DQ[:, w * c:w * c + w], 2047, None, A.bitwise_and, None, ks, ks, w)
                    row("DQ")
            pick(T.vcol[:], T.TB[:, 0:GW].indirect(T.atw[:]), ["TB", "atw", "MV"], ["vcol"], 192, col(MV))

        dedupe(7, 0, 3, 1, bdv(B256), "BD%d" % B256, early1, True, NB[0])
        for c, (a, b, e) in enumerate(LOOKS):
            src, n = T.TB[:, 0:GW].indirect(T.qB[:, a:b]), 16 * (b - a)
            if e == "a":
                act(T.CMP[:, 16 * a:16 * b], src, ["TB", "qB", "WE%d" % t] + CMPk, ["EF%d" % c], F.Identity, 0.0, col(WE0 + t), GAT * n)
            else:
                ts(T.CMP[:, 16 * a:16 * b], src, col(WE0 + t), None, A.mult, None, ["TB", "qB", "WE%d" % t] + CMPk, ["EF%d" % c], ga(n))
            row("look" + e)
        ts(T.q2[:], T.qB[:], 1.0, None, A.add, None, ["qB"], ["q2"], 96)
        mm(P[6][:, 0:192], T.Id16[:], T.q2[:], True, False, ["Id16", "q2"], ["P6"])
        for a, b in ((0, 64), (64, 128), (128, 192)):
            ks = ["EF%d" % c for c, x in enumerate(LOOKS) if x[0] < b and x[1] > a]
            wrap(P[6][:, a:b], lambda i: T.TS[:, 128 * i:128 * i + 128], lambda i: T.CMP[:, 16 * a + i:16 * b:16], TSk + ks + CMPk, ["P6"], 64, False, b == 192)
        ts(T.G[:], P[1][:, 0:192], 4.0, col(PM), A.min, A.is_equal, ["P1", "PM"], ["G"], 192)
        scan(P[4][:, 0:192], T.G[:], T.G[:], col(I192), A.add, A.max, ["G", "I192"], ["P4"])
        tt(T.z[:], P[4][:, 0:192], T.G[:], A.mult, ["P4", "G"], ["z"], 192)
        mm(P[5][:, 0:192], T.BDh[:, 0:128], T.z[:], True, True, ["BDh0", "z"], ["P5"])
        hold(T.H2[:], P[5][:, 0:192], 192, ["P5"], ["H2"])
        ts(T.posu[:], T.H2[:, 15:192:16], col(OFF1), None, A.subtract, None, ["H2", "c%d" % OFF1], ["posu"])
        tt(T.MSG[:, 960 * t:960 * t + 960].indirect(T.posu[:]), T.vcol[:], T.hcol[:], A.add, ["vcol", "hcol", "posu"], mk, sc(192))
        arr = sum(len(topo.engines(T.cores[p], core)) for p in peers)
        for p in peers:
            def send(p=p, t=t):
                dst = T.cores[p]
                rid, pid = topo.addr(dst, core)
                g.remote_dma(T.RX[:, 128 * t + 32 * rank:128 * t + 32 * rank + 32], T.MSG[:, 960 * t + 192 * p:960 * t + 192 * p + 32],
                             T.sem["arr%d" % t], T.sem.sent, pid, rid, topo.mask(core, dst))
            op("c", send, mk, ["RXr%d" % t], 0.25 + (1.0 if t == 0 and p == peers[0] else 0.0), 1.4, ("arr%d" % t, arr))
        c0 = 128 * t + 32 * rank
        scaled(T.RX[:, c0:c0 + 32], T.MSG[:, 960 * t + 192 * rank:960 * t + 192 * rank + 32], 1.0, mk, ["RX%d" % t], 64)
        RX, RXk = T.RX[:, 128 * t:128 * t + 128], ["RX%d" % t, "RXr%d" % t]
        ts(w12(0), T.H2[:, 15:192:16], col(OFF), 768.0, A.subtract, A.is_le, ["H2", "OFF"], ["won"])
        ts(w12(2), T.swf[:], col(OFS), None, A.subtract, None, ["swf", "c%d" % OFS], ["s0"])
        tt(w12(1), T.keyw[:], K3, A.subtract, ["keyw", "K3"], ["w1"])
        tt(w12(3), w12(1), w12(0), A.mult, ["w1", "won"], ["w3"])
        tt(w12(5), w12(3), K3, A.add, ["w3", "K3"], ["w5"])
        ts(boff, w12(5), -1.0, None, A.add, None, ["w5"], [bk])
        ts(w12(7), T.keyw[:], -1.0, None, A.add, None, ["keyw"], ["w7"])
        tt(w12(4), w12(7), w12(2), A.subtract, ["w7", "s0"], ["w4"])
        tt(w12(6), w12(4), w12(0), A.mult, ["w4", "won"], ["w6"])
        stay = T.H5[:, 61:624:48]
        tt(stay, w12(6), w12(2), A.add, ["w6", "s0"], ["stay"])
        cp(T.TB[:].indirect(boff), T.ZR[:], ["ZR", bk], ["TB"], sc(192))
        if t == 0:
            xb_clear(1, boff, bk)
        if t == 2:
            for c in range(4):
                k = (0, 3)[c & 1]
                mm(P[k][:, 0:512], bdv(BY), T.TB[:, 512 * c:512 * c + 512], True, True, ["BD%d" % BY, "TB"], [pk(k)], 512)
                act(T.Y[:, 512 * c:512 * c + 512], P[k][:, 0:512], [pk(k)], ["Y%d" % c], F.Identity, 2048.0, c=512)
                row("Y")
        act(T.sel[:], P[6][:, 0:192], ["P6", "BS2"], ["sel0", "sel1"], F.Relu, col(BS2), c=192)
        mm(P[4][:, 0:192], T.Id[:], T.PAT[:], True, False, ["Id", "PAT"], ["P4"])
        for k in (1, 6, 4):
            mm(P[k][:, 0:192], T.BDh[:, 0:128], T.sel[:], k != 4, True, ["sel0", "sel1", "BDh0"], [pk(k)])
        mm(P[5][:, 0:192], T.Id[:], T.PATn[:], True, False, ["Id", "PATn"], ["P5"])
        mm(P[5][:, 0:192], bdv(BOCC), T.acol[:], False, False, ["BD%d" % BOCC, "acol"], ["P5"])
        dedupe(1, 6, 4, 5, bdv(BNEG), "BD%d" % BNEG, lambda: None, False, NB[1])
        ts(T.EQ[:, 2304:2496], T.keyr[:], 0.0, None, A.is_equal, None, ["keyr"], ["EQ12"], 96)
        mm(P[5][:, 0:192], bdv(BNEG), T.EQ[:, 2304:2496], False, True, ["BD%d" % BNEG, "EQ12"], ["P5"])
        ts(w12(7), T.keyw[:], -1.0, None, A.add, None, ["keyw"], ["w7"])
        tt(T.D3[:, 1:36:3], w12(7), stay, A.subtract, ["w7", "stay"], ["D3"])
        mm(P[2][:, 0:128], bdv(BHOME), RX, True, True, ["BD%d" % BHOME] + RXk, ["P2"], 128)
        mm(P[7][:, 0:128], bdv(BHOME), RX, True, False, ["BD%d" % BHOME] + RXk, ["P7"], 128)
        hold(T.H4[:], P[2][:, 0:128], 128, ["P2"], ["H4"])
        ts(T.hwu[:], T.H4[:, 15:128:16], col(OFF), None, A.subtract, None, ["H4", "OFF"], ["hwu"])
        pick(T.hg[:], T.TB[:, 0:GW].indirect(T.hwu[:]), ["TB", "hwu"], ["hg"], 128)
        mm(P[7][:, 0:128], bdv(BGW), T.hg[:], False, True, ["BD%d" % BGW, "hg"], ["P7"], 128)
        hold(T.H4[:], P[7][:, 0:128], 128, ["P7"], ["H4"])
        ts(roff, T.H4[:, 15:128:16], col(OFF), None, A.subtract, None, ["H4", "OFF"], [rk])
        scan(T.H5[:, 0:576:3], T.HZ[:], P[5][:, 0:192], 0.0, A.mult, A.max, ["HZ", "P5"], ["go"])
        scan(T.E3[:], T.D3[:], T.H5[:, 45:621:16], 0.0, A.mult, A.add, ["D3", "D3a", "D3b", "go", "stay", "H5z"], ["E3"], 64)
        cp(endu, T.E3[:, 1:36:3], ["E3"], [ek])
        if t < 2:
            cp(T.TB[:].indirect(roff), RX, RXk + [rk], ["TB"], sc(128))
            cp(T.TB[:].indirect(endu), T.acol[:], ["acol", ek], ["TB"], sc(192))
            wrap(P[0][:, 0:8], zw(ZU), lambda i: T.RX[:, 128 * t + i:128 * t + 128:16], ["ZU"] + RXk, ["P0"], 64)
            cp(T.vw[:], P[0][:, 0:8], ["P0"], ["vw"])
            act(T.hf[:], P[2][:, 0:128], ["P2"], ["hf"])
            pick(T.xv[:], T.XS[:, 0:2080].indirect(T.vw[:]), XSk + ["vw"], ["xv"], 128)
            cp(XB[:].indirect(roff), T.xv[:], ["xv", rk], XK, sc(128))
            tt(T.qy[:, 0:128], T.DS[:].indirect(T.vw[:]), T.hf[:], A.add, DSk + ["vw", "hf"], ["qy"], ga(128))
            qn, qk = ring(128)
            cp(T.DQ[:].indirect(roff), qn, [qk, rk], DQk, sc(128))
        else:
            Yk = ["Y%d" % c for c in range(4)]
            mm(P[2][:, 0:128], bdv(BU), RX, True, True, ["BD%d" % BU] + RXk, ["P2"], 128)
            act(T.hf[:], P[2][:, 0:128], ["P2"], ["hf"])
            cp(T.Y[:].indirect(roff), T.hf[:], ["hf", rk], Yk, sc(128))
            cp(T.Y[:].indirect(endu), T.ua[:], ["ua", ek], Yk, sc(192))
            for h in range(2):
                dma("sa"[h], T.y[:, 1024 * h:1024 * h + 1024], T.Y[h:128:16, 1024 * h:1024 * h + 1024], Yk, ["y"], "out", 2.0)

    if len(ops) not in ORDER:
        ORDER[len(ops)] = put_in_order(ops)
    order, went = ORDER[len(ops)]
    total, cnt, tok, seen = {}, {"v": 0, "a": 0, "p": 0, "c": 0}, {}, {}
    for o in ops:
        if o["sem"]:
            s, n = o["sem"]
            total[s] = n if s.startswith("arr") else total.get(s, 0) + n

    def wait(e, s, n):
        if seen.get((e, s), 0) < n:
            seen[(e, s)] = n
            Q[e].wait_ge(T.sem[s], n)

    for i in order:
        o = ops[i]
        e = went[i]
        for j in sorted(o["pre"]):
            if o["pre"][j] > 0:
                wait(e, *tok[j])
        ins = o["fn"][e]()
        if o["sem"]:
            s = o["sem"][0]
            tok[i] = (s, total[s])
            if not s.startswith("arr"):
                ins.then_inc(T.sem[s], 16)
        else:
            cnt[e] += 1
            tok[i] = (e, cnt[e])
            ins.then_inc(T.sem[e], 1)
    total["sent"] = 3 * sum(len(topo.engines(core, T.cores[p])) for p in peers)
    for s, n in list(cnt.items()) + list(total.items()):
        wait("c", s, n)
